import numpy as np
import ml_dtypes


def mxq(x, axis, fmt="e4m3"):
    dtype, down = {"e4m3": (ml_dtypes.float8_e4m3fn, 7), "e5m2": (ml_dtypes.float8_e5m2, 14)}[fmt]
    v = np.moveaxis(np.asarray(x, np.float32).astype(ml_dtypes.bfloat16).astype(np.float64), axis, -1)
    blocks = v.reshape(v.shape[:-1] + (-1, 32))
    amax = np.abs(blocks).max(-1, keepdims=True)
    byte = np.maximum(np.where(amax > 0, np.frexp(amax)[1] - 1 + 127, 0) - down, 1)
    scale = np.exp2(byte - 127.0)
    codes = (blocks / scale).astype(np.float32).astype(dtype).astype(np.float64)
    return np.moveaxis((codes * scale).reshape(v.shape), -1, axis)


WIDE = False


def mx_kscale(k):
    if not WIDE:
        return np.ones(k)
    levels = np.array([10, -10, 5, -5, 0])
    if k % 512:
        return np.exp2(np.random.permutation(np.resize(levels, k // 32))).repeat(32)
    a = np.empty((k // 512, 16))
    for p in range(k // 512):
        a[p, :8] = np.random.permutation(np.resize(levels, 8))
        for g in range(8):
            far = levels[np.abs(levels - a[p, g]) >= 10]
            a[p, g + 8] = far[np.random.randint(len(far))]
    return np.exp2(a.ravel()).repeat(32)


def f64(x):
    return np.asarray(x).astype(np.float64)


def striped(idx):
    return np.tile(idx.reshape(-1, 16).T, (8, 1)).astype(np.uint16)


def unstriped(offs):
    return offs[:16].T.reshape(-1).astype(np.int64)


def relu(v):
    return np.maximum(v, 0.0)


K, T, E, C, H, N = 1024, 1024, 8, 256, 512, 128


def by_expert(wq, xq):
    return np.concatenate([wq[e].T @ xq[:, e * C:(e + 1) * C] for e in range(E)], axis=1)


def setup_inputs():
    n = np.random.standard_normal
    s = mx_kscale(K)[:, None]
    u = mx_kscale(H)
    first = np.random.permutation(np.repeat(np.arange(E), T // E))
    second = (first + 1 + np.random.permutation(np.repeat(np.arange(E - 1), -(-T // (E - 1)))[:T])) % E
    while np.bincount(second, minlength=E).max() != T // E:
        load = np.bincount(second, minlength=E); hi, lo = int(load.argmax()), int(load.argmin())
        t = np.flatnonzero((second == hi) & (first != lo))[0]; second[t] = lo
    slot_token = np.empty(E * C, np.int64); pos = np.empty((2, T), np.int64); fill = np.zeros(E, np.int64)
    place = np.stack([np.random.permutation(C) for _ in range(E)])
    for r, deal in enumerate((first, second)):
        for t in np.random.permutation(T):
            e = deal[t]; j = e * C + place[e, fill[e]]; fill[e] += 1; slot_token[j] = t; pos[r, t] = j
    g = np.random.uniform(0.2, 0.8, T)
    w_slot = np.empty(E * C); w_slot[pos[0]] = g; w_slot[pos[1]] = 1.0 - g
    return {
        "xT": (n((K, T)) * s).astype(np.float32),
        "w1": (n((E, K, H)) / np.sqrt(K) / s[None] * u[None, None, :]).astype(np.float32),
        "w2": (n((E, H, N)) / np.sqrt(H) / u[None, :, None]).astype(np.float32),
        "gate": np.tile(w_slot, (K, 1)).astype(np.float32),
        "offs": striped(slot_token),
        "pos1": striped(pos[0]),
        "pos2": striped(pos[1]),
    }


def reference(xT, w1, w2, gate, offs, pos1, pos2):
    idx = unstriped(offs)
    xq = mxq(f64(gate) * f64(xT)[:, idx], 0, "e4m3")
    h = relu(by_expert(mxq(f64(w1), 1, "e4m3"), xq))
    y = by_expert(mxq(f64(w2), 1, "e4m3"), mxq(h, 0, "e4m3"))
    return y[:, unstriped(pos1)] + y[:, unstriped(pos2)]

@@ -1,0 +1,226 @@
+from contextlib import ExitStack
+
+import concourse.mybir as mybir
+
+K, T, E, C, H, N = 1024, 1024, 8, 256, 512, 128
+S = E * C
+FLOPS = 2 * S * (K * H + H * N)
+BYTES = 4 * (K * T + E * K * H + E * H * N + S + N * T) + 2 * 128 * (S + 2 * T) // 16
+
+F32 = mybir.dt.float32
+BF16 = mybir.dt.bfloat16
+U32 = mybir.dt.uint32
+U16 = mybir.dt.uint16
+U8 = mybir.dt.uint8
+FP8X4 = mybir.dt.float8_e4m3fn_x4
+MULT = mybir.AluOpType.mult
+ADD = mybir.AluOpType.add
+MAX = mybir.AluOpType.max
+RELU = mybir.ActivationFunctionType.Relu
+
+P = 128
+PACK = 4
+K_PASS = P * PACK
+PASSES = K // K_PASS
+PAIR = 2 * C
+PAIRS = E // 2
+HALF = 128
+W2_GROUP = 4
+
+
+def tile_moe_pre_mlp_relu_kernel(tc, xT, w1, w2, gate, offs, pos1, pos2, out):
+    nc = tc.nc
+    with ExitStack() as ctx:
+        keep = ctx.enter_context(tc.tile_pool(name="keep", bufs=1))
+        ring = ctx.enter_context(tc.tile_pool(name="ring", bufs=2))
+        psum = ctx.enter_context(tc.psum_pool(name="psum", bufs=2))
+
+        offs_sb = keep.tile([P, S // 16], U16, name="offs_sb")
+        pos1_sb = keep.tile([P, T // 16], U16, name="pos1_sb")
+        pos2_sb = keep.tile([P, T // 16], U16, name="pos2_sb")
+        y_sb = keep.tile([P, S], F32, name="y_sb")
+
+        x_rows = xT.rearrange("(g p t) n -> g t p n", g=PASSES, t=PACK)
+        w1_rows = w1.rearrange("e (g p j) c -> e g p j c", g=PASSES, j=PACK)
+        w2_rows = w2.rearrange("e (p j) n -> p e j n", j=PACK)
+
+        planes, gates, w1_raw, w2_raw = {}, {}, {}, {}
+        gathered, x_bf, x_mx, w1_bf, w1_mx, w2_bf, w2_mx, h_bf, h_mx = {}, {}, {}, {}, {}, {}, {}, {}, {}
+
+        def load_plane(g, t):
+            planes[g, t] = keep.tile([P, T], F32, name="plane_%d_%d" % (g, t))
+            nc.sync.dma_start(planes[g, t][:], x_rows[g, t])
+
+        def load_gate(pair):
+            gates[pair] = keep.tile([P, PAIR], F32, name="gate_%d" % pair)
+            nc.sync.dma_start(gates[pair][:], gate[0:P, pair * PAIR:(pair + 1) * PAIR])
+
+        def load_w1(e, g):
+            w1_raw[e, g] = ring.tile([P, PACK, H], F32, name="w1_raw", bufs=5)
+            nc.sync.dma_start(w1_raw[e, g][:], w1_rows[e, g])
+
+        def load_w2(group):
+            w2_raw[group] = keep.tile([P, W2_GROUP, PACK, N], F32, name="w2_raw_%d" % group)
+            nc.sync.dma_start(w2_raw[group][:], w2_rows[:, group * W2_GROUP:(group + 1) * W2_GROUP])
+
+        def copy(on_vector, dst, src):
+            if on_vector:
+                nc.vector.tensor_copy(dst, src)
+            else:
+                nc.scalar.copy(dst, src)
+
+        def quantize(src, width, name, bufs):
+            codes = ring.tile([P, width], U32, name=name + "_codes", bufs=bufs, align_bytes=64)
+            scales = ring.tile([P, width], U8, name=name + "_scales", bufs=bufs, align_bytes=64)
+            nc.vector.quantize_mx(out=codes[:].bitcast(FP8X4), scales=scales[:], in_=src)
+            return codes, scales
+
+        def gather(pair, g, t):
+            if t == 0:
+                gathered[pair, g] = ring.tile([P, PACK, PAIR], F32, name="gathered", bufs=4)
+            cols = PAIR // 16
+            nc.vector.tensor_tensor(gathered[pair, g][:, t, :],
+                                    planes[g, t][:].indirect(offs_sb[:, pair * cols:(pair + 1) * cols]),
+                                    gates[pair][:], MULT)
+
+        def round_x(pair, g):
+            x_bf[pair, g] = ring.tile([P, PAIR * PACK], BF16, name="x_bf", bufs=2, align_bytes=64)
+            nc.scalar.copy(x_bf[pair, g][:].rearrange("p (c i t) -> p c t i", i=4, t=PACK),
+                           gathered[pair, g][:].rearrange("p t (c i) -> p c t i", i=4))
+
+        def quantize_x(pair, g):
+            x_mx[pair, g] = quantize(x_bf[pair, g][:], PAIR, "x", PAIRS * PASSES)
+
+        def round_w1(e, g, on_vector):
+            w1_bf[e, g] = ring.tile([P, H * PACK], BF16, name="w_bf", bufs=3, align_bytes=64)
+            copy(on_vector, w1_bf[e, g][:].rearrange("p (t m j) -> p m j t", t=PACK, j=PACK),
+                 w1_raw[e, g][:].rearrange("p j (m t) -> p m j t", t=PACK))
+
+        def quantize_w1(e, g):
+            w1_mx[e, g] = quantize(w1_bf[e, g][:], H, "w1", 12)
+
+        def round_w2(group):
+            w2_bf[group] = ring.tile([P, W2_GROUP * N * PACK], BF16, name="w_bf", bufs=3, align_bytes=64)
+            nc.vector.tensor_copy(w2_bf[group][:].rearrange("p (e c i j) -> p e c j i", e=W2_GROUP, i=4, j=PACK),
+                                  w2_raw[group][:].rearrange("p e j (c i) -> p e c j i", i=4))
+
+        def quantize_w2(group):
+            w2_mx[group] = quantize(w2_bf[group][:], W2_GROUP * N, "w2", E // W2_GROUP)
+
+        def first_layer(e, split):
+            h_bf[e] = ring.tile([P, C * PACK], BF16, name="h_bf", bufs=2, align_bytes=64)
+            for half in range(C // HALF):
+                bank = psum.tile([P, PACK, HALF], F32, name="a_bank", bufs=4)
+                s0 = (e % 2) * C + half * HALF
+                for t in range(PACK):
+                    for g in range(PASSES):
+                        w_codes, w_scales = w1_mx[e, g]
+                        x_codes, x_scales = x_mx[e // 2, g]
+                        nc.tensor.matmul_mx(out=bank[:, t, :],
+                                            lhsT=w_codes[:, t * P:(t + 1) * P].bitcast(FP8X4),
+                                            lhsT_scale=w_scales[:, t * P:(t + 1) * P],
+                                            rhs=x_codes[:, s0:s0 + HALF].bitcast(FP8X4),
+                                            rhs_scale=x_scales[:, s0:s0 + HALF],
+                                            start=(g == 0), stop=(g == PASSES - 1))
+                dst = h_bf[e][:, half * HALF * PACK:(half + 1) * HALF * PACK].rearrange("p (s t) -> p s t", t=PACK)
+                src = bank[:].rearrange("p t s -> p s t")
+                if split and half == 1:
+                    nc.vector.tensor_scalar(dst, src, 0.0, None, MAX)
+                else:
+                    nc.scalar.activation(dst, src, RELU)
+
+        def quantize_h(e):
+            h_mx[e] = quantize(h_bf[e][:], C, "h", 2)
+
+        def second_layer(e):
+            bank = psum.tile([P, C], F32, name="y_bank", bufs=2)
+            w_codes, w_scales = w2_mx[e // W2_GROUP]
+            n0 = (e % W2_GROUP) * N
+            h_codes, h_scales = h_mx[e]
+            nc.tensor.matmul_mx(out=bank[:], lhsT=w_codes[:, n0:n0 + N].bitcast(FP8X4),
+                                lhsT_scale=w_scales[:, n0:n0 + N],
+                                rhs=h_codes[:].bitcast(FP8X4), rhs_scale=h_scales[:], start=True, stop=True)
+            nc.scalar.copy(y_sb[:, e * C:(e + 1) * C], bank[:])
+
+        def w1_unit(e, g, on_vector):
+            round_w1(e, g, on_vector)
+            quantize_w1(e, g)
+
+        def x_unit(pair, g):
+            round_x(pair, g)
+            quantize_x(pair, g)
+
+        def expert(e, split=False):
+            first_layer(e, split)
+            quantize_h(e)
+            second_layer(e)
+
+        for step in range(PASSES * PACK):
+            g, t = divmod(step, PACK)
+            load_plane(g, t)
+            if step == 0:
+                nc.sync.dma_start(offs_sb[:], offs)
+                load_gate(0)
+                load_gate(1)
+            load_w1(step // PASSES, step % PASSES)
+            gather(0, g, t)
+            gather(1, g, t)
+            w1_unit(step // PASSES, step % PASSES, False)
+            if t == PACK - 1:
+                x_unit(0, g)
+                x_unit(1, g)
+        load_w2(0)
+        load_gate(2)
+        load_gate(3)
+        load_w1(4, 0)
+        load_w1(4, 1)
+        load_w1(5, 0)
+        load_w1(5, 1)
+        load_w2(1)
+        nc.sync.dma_start(pos1_sb[:], pos1)
+        nc.sync.dma_start(pos2_sb[:], pos2)
+        for e in (6, 7):
+            for g in range(PASSES):
+                load_w1(e, g)
+
+        round_w2(0)
+        quantize_w2(0)
+        for t in range(PACK):
+            gather(2, 0, t)
+        expert(0)
+        expert(1)
+        w1_unit(4, 0, False)
+        x_unit(2, 0)
+        for t in range(PACK):
+            gather(2, 1, t)
+        expert(2)
+        expert(3)
+        w1_unit(4, 1, False)
+        x_unit(2, 1)
+        for t in range(PACK):
+            gather(3, 0, t)
+        round_w2(1)
+        quantize_w2(1)
+        w1_unit(5, 0, False)
+        w1_unit(5, 1, False)
+        x_unit(3, 0)
+        for t in range(PACK):
+            gather(3, 1, t)
+        expert(4)
+        expert(5)
+        x_unit(3, 1)
+        w1_unit(6, 0, True)
+        w1_unit(6, 1, True)
+        w1_unit(7, 0, True)
+        expert(6)
+        w1_unit(7, 1, True)
+        expert(7, split=True)
+
+        chunk = T // 2
+        for c in range(T // chunk):
+            cols = slice(c * chunk // 16, (c + 1) * chunk // 16)
+            first = ring.tile([P, chunk], F32, name="first", bufs=2)
+            both = ring.tile([P, chunk], F32, name="both", bufs=2)
+            nc.vector.tensor_copy(first[:], y_sb[:].indirect(pos1_sb[:, cols]))
+            nc.vector.tensor_tensor(both[:], y_sb[:].indirect(pos2_sb[:, cols]), first[:], ADD)
+            nc.sync.dma_start(out[:, c * chunk:(c + 1) * chunk], both[:])

@@ -42,9 +42,10 @@ def tile_moe_pre_mlp_relu_kernel(tc, xT, w1, w2, gate, offs, pos1, pos2, out):
 
         x_rows = xT.rearrange("(g p t) n -> g t p n", g=PASSES, t=PACK)
         w1_rows = w1.rearrange("e (g p j) c -> e g p j c", g=PASSES, j=PACK)
-        w2_rows = w2.rearrange("e (p j) n -> p e j n", j=PACK)
+        w2_rows = w2.rearrange("e (u t r) n -> r t u e n", t=PACK, r=2)
+        w2_raw = keep.tile([P, E, PACK, N], F32, name="w2_raw")
 
-        planes, gates, w1_raw, w2_raw = {}, {}, {}, {}
+        planes, gates, w1_raw = {}, {}, {}
         gathered, x_bf, x_mx, w1_bf, w1_mx, w2_bf, w2_mx, h_bf, h_mx = {}, {}, {}, {}, {}, {}, {}, {}, {}
 
         def load_plane(g, t):
@@ -56,12 +57,13 @@ def tile_moe_pre_mlp_relu_kernel(tc, xT, w1, w2, gate, offs, pos1, pos2, out):
             nc.sync.dma_start(gates[pair][:], gate[0:P, pair * PAIR:(pair + 1) * PAIR])
 
         def load_w1(e, g):
-            w1_raw[e, g] = ring.tile([P, PACK, H], F32, name="w1_raw", bufs=5)
+            w1_raw[e, g] = ring.tile([P, PACK, H], F32, name="w1_raw", bufs=7)
             nc.sync.dma_start(w1_raw[e, g][:], w1_rows[e, g])
 
-        def load_w2(group):
-            w2_raw[group] = keep.tile([P, W2_GROUP, PACK, N], F32, name="w2_raw_%d" % group)
-            nc.sync.dma_start(w2_raw[group][:], w2_rows[:, group * W2_GROUP:(group + 1) * W2_GROUP])
+        def load_w2():
+            for r in range(2):
+                for t in range(PACK):
+                    nc.sync.dma_start(w2_raw[r:P:2, :, t, :], w2_rows[r, t])
 
         def copy(on_vector, dst, src):
             if on_vector:
@@ -77,32 +79,32 @@ def tile_moe_pre_mlp_relu_kernel(tc, xT, w1, w2, gate, offs, pos1, pos2, out):
 
         def gather(pair, g, t):
             if t == 0:
-                gathered[pair, g] = ring.tile([P, PACK, PAIR], F32, name="gathered", bufs=4)
+                gathered[pair, g] = ring.tile([P, PACK, PAIR], F32, name="gathered", tag="gathered", bufs=4)
             cols = PAIR // 16
             nc.vector.tensor_tensor(gathered[pair, g][:, t, :],
                                     planes[g, t][:].indirect(offs_sb[:, pair * cols:(pair + 1) * cols]),
                                     gates[pair][:], MULT)
 
         def round_x(pair, g):
-            x_bf[pair, g] = ring.tile([P, PAIR * PACK], BF16, name="x_bf", bufs=2, align_bytes=64)
-            nc.scalar.copy(x_bf[pair, g][:].rearrange("p (c i t) -> p c t i", i=4, t=PACK),
-                           gathered[pair, g][:].rearrange("p t (c i) -> p c t i", i=4))
+            x_bf[pair, g] = ring.tile([P, PAIR * PACK], BF16, name="x_bf", bufs=3, align_bytes=64)
+            nc.scalar.copy(x_bf[pair, g][:].rearrange("p (c i t) -> p c t i", i=2, t=PACK),
+                           gathered[pair, g][:].rearrange("p t (c i) -> p c t i", i=2))
 
         def quantize_x(pair, g):
-            x_mx[pair, g] = quantize(x_bf[pair, g][:], PAIR, "x", PAIRS * PASSES)
+            x_mx[pair, g] = quantize(x_bf[pair, g][:], PAIR, "x", 6)
 
         def round_w1(e, g, on_vector):
-            w1_bf[e, g] = ring.tile([P, H * PACK], BF16, name="w_bf", bufs=3, align_bytes=64)
-            copy(on_vector, w1_bf[e, g][:].rearrange("p (t m j) -> p m j t", t=PACK, j=PACK),
-                 w1_raw[e, g][:].rearrange("p j (m t) -> p m j t", t=PACK))
+            w1_bf[e, g] = ring.tile([P, H * PACK], BF16, name="w_bf", bufs=4, align_bytes=64)
+            copy(on_vector, w1_bf[e, g][:].rearrange("p (t u r j) -> p u t j r", t=PACK, r=2, j=PACK),
+                 w1_raw[e, g][:].rearrange("p j (u t r) -> p u t j r", t=PACK, r=2))
 
         def quantize_w1(e, g):
-            w1_mx[e, g] = quantize(w1_bf[e, g][:], H, "w1", 12)
+            w1_mx[e, g] = quantize(w1_bf[e, g][:], H, "w1", 10)
 
         def round_w2(group):
-            w2_bf[group] = ring.tile([P, W2_GROUP * N * PACK], BF16, name="w_bf", bufs=3, align_bytes=64)
-            nc.vector.tensor_copy(w2_bf[group][:].rearrange("p (e c i j) -> p e c j i", e=W2_GROUP, i=4, j=PACK),
-                                  w2_raw[group][:].rearrange("p e j (c i) -> p e c j i", i=4))
+            w2_bf[group] = ring.tile([P, W2_GROUP * N * PACK], BF16, name="w_bf", bufs=4, align_bytes=64)
+            nc.vector.tensor_copy(w2_bf[group][:].rearrange("p (e c i j) -> p e c j i", e=W2_GROUP, i=2, j=PACK),
+                                  w2_raw[:, group * W2_GROUP:(group + 1) * W2_GROUP].rearrange("p e j (c i) -> p e c j i", i=2))
 
         def quantize_w2(group):
             w2_mx[group] = quantize(w2_bf[group][:], W2_GROUP * N, "w2", E // W2_GROUP)
@@ -169,14 +171,13 @@ def tile_moe_pre_mlp_relu_kernel(tc, xT, w1, w2, gate, offs, pos1, pos2, out):
             if t == PACK - 1:
                 x_unit(0, g)
                 x_unit(1, g)
-        load_w2(0)
         load_gate(2)
+        load_w2()
         load_gate(3)
         load_w1(4, 0)
         load_w1(4, 1)
         load_w1(5, 0)
         load_w1(5, 1)
-        load_w2(1)
         nc.sync.dma_start(pos1_sb[:], pos1)
         nc.sync.dma_start(pos2_sb[:], pos2)
         for e in (6, 7):
@@ -219,8 +220,8 @@ def tile_moe_pre_mlp_relu_kernel(tc, xT, w1, w2, gate, offs, pos1, pos2, out):
         chunk = T // 2
         for c in range(T // chunk):
             cols = slice(c * chunk // 16, (c + 1) * chunk // 16)
-            first = ring.tile([P, chunk], F32, name="first", bufs=2)
-            both = ring.tile([P, chunk], F32, name="both", bufs=2)
+            first = ring.tile([P, chunk], F32, name="first", tag="gathered", bufs=4)
+            both = ring.tile([P, chunk], F32, name="both", tag="gathered", bufs=4)
             nc.vector.tensor_copy(first[:], y_sb[:].indirect(pos1_sb[:, cols]))
             nc.vector.tensor_tensor(both[:], y_sb[:].indirect(pos2_sb[:, cols]), first[:], ADD)
             nc.sync.dma_start(out[:, c * chunk:(c + 1) * chunk], both[:])

@@ -3,9 +3,7 @@ from contextlib import ExitStack
 import concourse.mybir as mybir
 
 K, T, E, C, H, N = 1024, 1024, 8, 256, 512, 128
-S = E * C
-FLOPS = 2 * S * (K * H + H * N)
-BYTES = 4 * (K * T + E * K * H + E * H * N + S + N * T) + 2 * 128 * (S + 2 * T) // 16
+SLOTS = E * C
 
 F32 = mybir.dt.float32
 BF16 = mybir.dt.bfloat16
@@ -20,12 +18,30 @@ RELU = mybir.ActivationFunctionType.Relu
 
 P = 128
 PACK = 4
-K_PASS = P * PACK
-PASSES = K // K_PASS
+PASSES = K // (P * PACK)
+PLANES = PASSES * PACK
 PAIR = 2 * C
-PAIRS = E // 2
-HALF = 128
+HALF = C // 2
 W2_GROUP = 4
+RUN = 2
+ENTRIES = 16
+LAST_STORE = 256
+MX_ALIGN = 64
+
+FLOPS = 2 * SLOTS * (K * H + H * N)
+BYTES = 4 * (K * T + E * K * H + E * H * N + SLOTS + N * T) + 2 * P * (SLOTS + 2 * T) // ENTRIES
+
+RAW_BUFS = 7
+GATHER_BUFS = 3
+X_ROUNDED_BUFS = 3
+W_SCALAR_BUFS = 4
+W_VECTOR_BUFS = 2
+H_ROUNDED_BUFS = 3
+X_CODE_BUFS = 6
+W1_CODE_BUFS = 10
+H_CODE_BUFS = 4
+A_BANKS = 6
+Y_BANKS = 2
 
 
 def tile_moe_pre_mlp_relu_kernel(tc, xT, w1, w2, gate, offs, pos1, pos2, out):
@@ -35,18 +51,19 @@ def tile_moe_pre_mlp_relu_kernel(tc, xT, w1, w2, gate, offs, pos1, pos2, out):
         ring = ctx.enter_context(tc.tile_pool(name="ring", bufs=2))
         psum = ctx.enter_context(tc.psum_pool(name="psum", bufs=2))
 
-        offs_sb = keep.tile([P, S // 16], U16, name="offs_sb")
-        pos1_sb = keep.tile([P, T // 16], U16, name="pos1_sb")
-        pos2_sb = keep.tile([P, T // 16], U16, name="pos2_sb")
-        y_sb = keep.tile([P, S], F32, name="y_sb")
+        offs_sb = keep.tile([P, SLOTS // ENTRIES], U16, name="offs_sb")
+        pos1_sb = keep.tile([P, T // ENTRIES], U16, name="pos1_sb")
+        pos2_sb = keep.tile([P, T // ENTRIES], U16, name="pos2_sb")
+        y_sb = keep.tile([P, SLOTS], F32, name="y_sb")
+        w2_raw = keep.tile([P, E, PACK, N], F32, name="w2_raw")
 
         x_rows = xT.rearrange("(g p t) n -> g t p n", g=PASSES, t=PACK)
         w1_rows = w1.rearrange("e (g p j) c -> e g p j c", g=PASSES, j=PACK)
         w2_rows = w2.rearrange("e (u t r) n -> r t u e n", t=PACK, r=2)
-        w2_raw = keep.tile([P, E, PACK, N], F32, name="w2_raw")
 
-        planes, gates, w1_raw = {}, {}, {}
-        gathered, x_bf, x_mx, w1_bf, w1_mx, w2_bf, w2_mx, h_bf, h_mx = {}, {}, {}, {}, {}, {}, {}, {}, {}
+        planes, gates, w1_raw, gathered = {}, {}, {}, {}
+        x_bf, w1_bf, w2_bf, h_bf = {}, {}, {}, {}
+        x_mx, w1_mx, w2_mx, h_mx, y_banks = {}, {}, {}, {}, {}
 
         def load_plane(g, t):
             planes[g, t] = keep.tile([P, T], F32, name="plane_%d_%d" % (g, t))
@@ -57,7 +74,7 @@ def tile_moe_pre_mlp_relu_kernel(tc, xT, w1, w2, gate, offs, pos1, pos2, out):
             nc.sync.dma_start(gates[pair][:], gate[0:P, pair * PAIR:(pair + 1) * PAIR])
 
         def load_w1(e, g):
-            w1_raw[e, g] = ring.tile([P, PACK, H], F32, name="w1_raw", bufs=7)
+            w1_raw[e, g] = ring.tile([P, PACK, H], F32, name="w1_raw", tag="raw", bufs=RAW_BUFS)
             nc.sync.dma_start(w1_raw[e, g][:], w1_rows[e, g])
 
         def load_w2():
@@ -65,56 +82,67 @@ def tile_moe_pre_mlp_relu_kernel(tc, xT, w1, w2, gate, offs, pos1, pos2, out):
                 for t in range(PACK):
                     nc.sync.dma_start(w2_raw[r:P:2, :, t, :], w2_rows[r, t])
 
-        def copy(on_vector, dst, src):
-            if on_vector:
-                nc.vector.tensor_copy(dst, src)
-            else:
-                nc.scalar.copy(dst, src)
-
-        def quantize(src, width, name, bufs):
-            codes = ring.tile([P, width], U32, name=name + "_codes", bufs=bufs, align_bytes=64)
-            scales = ring.tile([P, width], U8, name=name + "_scales", bufs=bufs, align_bytes=64)
-            nc.vector.quantize_mx(out=codes[:].bitcast(FP8X4), scales=scales[:], in_=src)
+        def quantize(src, width, name, bufs, pieces=1):
+            codes = ring.tile([P, width], U32, name=name + "_codes", bufs=bufs, align_bytes=MX_ALIGN)
+            scales = ring.tile([P, width], U8, name=name + "_scales", bufs=bufs, align_bytes=MX_ALIGN)
+            step = width // pieces
+            for c in range(0, width, step):
+                nc.vector.quantize_mx(out=codes[:, c:c + step].bitcast(FP8X4), scales=scales[:, c:c + step],
+                                      in_=src[:, c * PACK:(c + step) * PACK])
             return codes, scales
 
         def gather(pair, g, t):
             if t == 0:
-                gathered[pair, g] = ring.tile([P, PACK, PAIR], F32, name="gathered", tag="gathered", bufs=4)
-            cols = PAIR // 16
+                gathered[pair, g] = ring.tile([P, PACK, PAIR], F32, name="gathered", bufs=GATHER_BUFS)
+            columns = PAIR // ENTRIES
             nc.vector.tensor_tensor(gathered[pair, g][:, t, :],
-                                    planes[g, t][:].indirect(offs_sb[:, pair * cols:(pair + 1) * cols]),
+                                    planes[g, t][:].indirect(offs_sb[:, pair * columns:(pair + 1) * columns]),
                                     gates[pair][:], MULT)
 
-        def round_x(pair, g):
-            x_bf[pair, g] = ring.tile([P, PAIR * PACK], BF16, name="x_bf", bufs=3, align_bytes=64)
-            nc.scalar.copy(x_bf[pair, g][:].rearrange("p (c i t) -> p c t i", i=2, t=PACK),
-                           gathered[pair, g][:].rearrange("p t (c i) -> p c t i", i=2))
+        def gather_pass(pair, g):
+            for t in range(PACK):
+                gather(pair, g, t)
 
-        def quantize_x(pair, g):
-            x_mx[pair, g] = quantize(x_bf[pair, g][:], PAIR, "x", 6)
+        def prepare_x(pair, g):
+            x_bf[pair, g] = ring.tile([P, PAIR * PACK], BF16, name="x_bf", bufs=X_ROUNDED_BUFS, align_bytes=MX_ALIGN)
+            nc.scalar.copy(x_bf[pair, g][:].rearrange("p (c i t) -> p c t i", i=RUN, t=PACK),
+                           gathered[pair, g][:].rearrange("p t (c i) -> p c t i", i=RUN))
+            x_mx[pair, g] = quantize(x_bf[pair, g][:], PAIR, "x", X_CODE_BUFS)
 
         def round_w1(e, g, on_vector):
-            w1_bf[e, g] = ring.tile([P, H * PACK], BF16, name="w_bf", bufs=4, align_bytes=64)
-            copy(on_vector, w1_bf[e, g][:].rearrange("p (t u r j) -> p u t j r", t=PACK, r=2, j=PACK),
+            if on_vector:
+                tile = ring.tile([P, H * PACK], BF16, name="w_bf_vector", bufs=W_VECTOR_BUFS, align_bytes=MX_ALIGN)
+                copy = nc.vector.tensor_copy
+            else:
+                tile = ring.tile([P, H * PACK], BF16, name="w_bf_scalar", bufs=W_SCALAR_BUFS, align_bytes=MX_ALIGN)
+                copy = nc.scalar.copy
+            w1_bf[e, g] = tile
+            copy(tile[:].rearrange("p (t u r j) -> p u t j r", t=PACK, r=2, j=PACK),
                  w1_raw[e, g][:].rearrange("p j (u t r) -> p u t j r", t=PACK, r=2))
 
-        def quantize_w1(e, g):
-            w1_mx[e, g] = quantize(w1_bf[e, g][:], H, "w1", 10)
+        def quantize_w1(e, g, pieces=1):
+            w1_mx[e, g] = quantize(w1_bf[e, g][:], H, "w1", W1_CODE_BUFS, pieces)
+
+        def prepare_w1(e, g, on_vector=False):
+            round_w1(e, g, on_vector)
+            quantize_w1(e, g)
 
         def round_w2(group):
-            w2_bf[group] = ring.tile([P, W2_GROUP * N * PACK], BF16, name="w_bf", bufs=4, align_bytes=64)
-            nc.vector.tensor_copy(w2_bf[group][:].rearrange("p (e c i j) -> p e c j i", e=W2_GROUP, i=2, j=PACK),
-                                  w2_raw[:, group * W2_GROUP:(group + 1) * W2_GROUP].rearrange("p e j (c i) -> p e c j i", i=2))
+            w2_bf[group] = ring.tile([P, W2_GROUP * N * PACK], BF16, name="w_bf_scalar", bufs=W_SCALAR_BUFS,
+                                     align_bytes=MX_ALIGN)
+            experts = slice(group * W2_GROUP, (group + 1) * W2_GROUP)
+            nc.scalar.copy(w2_bf[group][:].rearrange("p (e c i t) -> p e c t i", e=W2_GROUP, i=RUN, t=PACK),
+                           w2_raw[:, experts].rearrange("p e t (c i) -> p e c t i", i=RUN))
 
         def quantize_w2(group):
             w2_mx[group] = quantize(w2_bf[group][:], W2_GROUP * N, "w2", E // W2_GROUP)
 
-        def first_layer(e, split):
-            h_bf[e] = ring.tile([P, C * PACK], BF16, name="h_bf", bufs=2, align_bytes=64)
-            for half in range(C // HALF):
-                bank = psum.tile([P, PACK, HALF], F32, name="a_bank", bufs=4)
-                s0 = (e % 2) * C + half * HALF
-                for t in range(PACK):
+        def first_layer(e, share=False):
+            h_bf[e] = ring.tile([P, C * PACK], BF16, name="h_bf", bufs=H_ROUNDED_BUFS, align_bytes=MX_ALIGN)
+            banks = [psum.tile([P, PACK, HALF], F32, name="a_bank", bufs=A_BANKS) for half in range(C // HALF)]
+            for t in range(PACK):
+                for half, bank in enumerate(banks):
+                    s0 = (e % 2) * C + half * HALF
                     for g in range(PASSES):
                         w_codes, w_scales = w1_mx[e, g]
                         x_codes, x_scales = x_mx[e // 2, g]
@@ -124,104 +152,123 @@ def tile_moe_pre_mlp_relu_kernel(tc, xT, w1, w2, gate, offs, pos1, pos2, out):
                                             rhs=x_codes[:, s0:s0 + HALF].bitcast(FP8X4),
                                             rhs_scale=x_scales[:, s0:s0 + HALF],
                                             start=(g == 0), stop=(g == PASSES - 1))
+            for half, bank in enumerate(banks):
                 dst = h_bf[e][:, half * HALF * PACK:(half + 1) * HALF * PACK].rearrange("p (s t) -> p s t", t=PACK)
                 src = bank[:].rearrange("p t s -> p s t")
-                if split and half == 1:
+                if share and half == 1:
                     nc.vector.tensor_scalar(dst, src, 0.0, None, MAX)
                 else:
                     nc.scalar.activation(dst, src, RELU)
 
         def quantize_h(e):
-            h_mx[e] = quantize(h_bf[e][:], C, "h", 2)
+            h_mx[e] = quantize(h_bf[e][:], C, "h", H_CODE_BUFS)
 
-        def second_layer(e):
-            bank = psum.tile([P, C], F32, name="y_bank", bufs=2)
-            w_codes, w_scales = w2_mx[e // W2_GROUP]
-            n0 = (e % W2_GROUP) * N
-            h_codes, h_scales = h_mx[e]
-            nc.tensor.matmul_mx(out=bank[:], lhsT=w_codes[:, n0:n0 + N].bitcast(FP8X4),
-                                lhsT_scale=w_scales[:, n0:n0 + N],
-                                rhs=h_codes[:].bitcast(FP8X4), rhs_scale=h_scales[:], start=True, stop=True)
-            nc.scalar.copy(y_sb[:, e * C:(e + 1) * C], bank[:])
-
-        def w1_unit(e, g, on_vector):
-            round_w1(e, g, on_vector)
-            quantize_w1(e, g)
-
-        def x_unit(pair, g):
-            round_x(pair, g)
-            quantize_x(pair, g)
-
-        def expert(e, split=False):
-            first_layer(e, split)
+        def hidden(e):
+            first_layer(e)
             quantize_h(e)
-            second_layer(e)
 
-        for step in range(PASSES * PACK):
-            g, t = divmod(step, PACK)
-            load_plane(g, t)
-            if step == 0:
-                nc.sync.dma_start(offs_sb[:], offs)
-                load_gate(0)
-                load_gate(1)
-            load_w1(step // PASSES, step % PASSES)
-            gather(0, g, t)
-            gather(1, g, t)
-            w1_unit(step // PASSES, step % PASSES, False)
-            if t == PACK - 1:
-                x_unit(0, g)
-                x_unit(1, g)
+        def second_layer(experts):
+            bank = psum.tile([P, len(experts) * C], F32, name="y_bank", bufs=Y_BANKS)
+            y_banks[experts] = bank
+            for place, e in enumerate(experts):
+                w_codes, w_scales = w2_mx[e // W2_GROUP]
+                h_codes, h_scales = h_mx[e]
+                n0 = (e % W2_GROUP) * N
+                nc.tensor.matmul_mx(out=bank[:, place * C:(place + 1) * C],
+                                    lhsT=w_codes[:, n0:n0 + N].bitcast(FP8X4), lhsT_scale=w_scales[:, n0:n0 + N],
+                                    rhs=h_codes[:].bitcast(FP8X4), rhs_scale=h_scales[:], start=True, stop=True)
+
+        def copy_y(experts):
+            nc.scalar.copy(y_sb[:, experts[0] * C:(experts[-1] + 1) * C], y_banks[experts][:])
+
+        load_plane(0, 0)
+        nc.sync.dma_start(offs_sb[:], offs)
+        load_gate(0)
+        load_plane(0, 1)
+        load_gate(1)
+        for g in range(PASSES):
+            load_w1(0, g)
+            load_plane(0, 2 + g)
+        for t in range(PACK):
+            load_plane(1, t)
+            load_w1(1 + t // PASSES, t % PASSES)
         load_gate(2)
-        load_w2()
-        load_gate(3)
-        load_w1(4, 0)
-        load_w1(4, 1)
-        load_w1(5, 0)
-        load_w1(5, 1)
-        nc.sync.dma_start(pos1_sb[:], pos1)
-        nc.sync.dma_start(pos2_sb[:], pos2)
-        for e in (6, 7):
+        for e in range(3, E):
             for g in range(PASSES):
                 load_w1(e, g)
+            if e == 4:
+                load_gate(3)
+                load_w2()
+            if e == 5:
+                nc.sync.dma_start(pos1_sb[:], pos1)
+                nc.sync.dma_start(pos2_sb[:], pos2)
 
+        for plane in range(PLANES):
+            g, t = divmod(plane, PACK)
+            gather(0, g, t)
+            gather(1, g, t)
+            if plane < 3 * PASSES:
+                prepare_w1(*divmod(plane, PASSES))
+            if plane == PACK - 1:
+                prepare_x(0, 0)
+                prepare_x(1, 0)
+
+        prepare_x(0, 1)
+        gather_pass(2, 0)
+        prepare_w1(3, 0)
+        prepare_w1(3, 1)
+
+        prepare_x(1, 1)
+        gather_pass(2, 1)
+        prepare_w1(4, 0)
+        hidden(0)
+        hidden(1)
+
+        prepare_x(2, 0)
+        gather_pass(3, 0)
+        prepare_w1(4, 1)
+        hidden(2)
+        hidden(3)
+
+        prepare_x(2, 1)
+        gather_pass(3, 1)
+
+        prepare_w1(5, 0)
+        prepare_x(3, 0)
+        prepare_x(3, 1)
         round_w2(0)
         quantize_w2(0)
-        for t in range(PACK):
-            gather(2, 0, t)
-        expert(0)
-        expert(1)
-        w1_unit(4, 0, False)
-        x_unit(2, 0)
-        for t in range(PACK):
-            gather(2, 1, t)
-        expert(2)
-        expert(3)
-        w1_unit(4, 1, False)
-        x_unit(2, 1)
-        for t in range(PACK):
-            gather(3, 0, t)
+        prepare_w1(5, 1)
+        hidden(4)
+        second_layer((0, 1))
+        second_layer((2, 3))
         round_w2(1)
-        quantize_w2(1)
-        w1_unit(5, 0, False)
-        w1_unit(5, 1, False)
-        x_unit(3, 0)
-        for t in range(PACK):
-            gather(3, 1, t)
-        expert(4)
-        expert(5)
-        x_unit(3, 1)
-        w1_unit(6, 0, True)
-        w1_unit(6, 1, True)
-        w1_unit(7, 0, True)
-        expert(6)
-        w1_unit(7, 1, True)
-        expert(7, split=True)
+        first_layer(5)
+        prepare_w1(6, 0, on_vector=True)
+        prepare_w1(6, 1, on_vector=True)
+        first_layer(6)
+        copy_y((0, 1))
+        copy_y((2, 3))
 
-        chunk = T // 2
-        for c in range(T // chunk):
-            cols = slice(c * chunk // 16, (c + 1) * chunk // 16)
-            first = ring.tile([P, chunk], F32, name="first", tag="gathered", bufs=4)
-            both = ring.tile([P, chunk], F32, name="both", tag="gathered", bufs=4)
-            nc.vector.tensor_copy(first[:], y_sb[:].indirect(pos1_sb[:, cols]))
-            nc.vector.tensor_tensor(both[:], y_sb[:].indirect(pos2_sb[:, cols]), first[:], ADD)
-            nc.sync.dma_start(out[:, c * chunk:(c + 1) * chunk], both[:])
+        prepare_w1(7, 0, on_vector=True)
+        round_w1(7, 1, on_vector=True)
+        quantize_w1(7, 1, pieces=PACK)
+        quantize_w2(1)
+        quantize_h(5)
+        quantize_h(6)
+        second_layer((4, 5))
+        first_layer(7, share=True)
+        copy_y((4, 5))
+        second_layer((6,))
+        copy_y((6,))
+        quantize_h(7)
+        second_layer((7,))
+        copy_y((7,))
+
+        first = ring.tile([P, T], F32, name="first", tag="raw", bufs=RAW_BUFS)
+        nc.vector.tensor_copy(first[:], y_sb[:].indirect(pos1_sb[:]))
+        for t0, t1 in ((0, T - LAST_STORE), (T - LAST_STORE, T)):
+            both = ring.tile([P, t1 - t0], F32, name="both", tag="raw", bufs=RAW_BUFS)
+            nc.vector.tensor_tensor(both[:], y_sb[:].indirect(pos2_sb[:, t0 // ENTRIES:t1 // ENTRIES]),
+                                    first[:, t0:t1], ADD)
+            nc.sync.dma_start(out[:, t0:t1], both[:])

@@ -19,27 +19,22 @@ RELU = mybir.ActivationFunctionType.Relu
 P = 128
 PACK = 4
 PASSES = K // (P * PACK)
-PLANES = PASSES * PACK
 PAIR = 2 * C
-HALF = C // 2
-W2_GROUP = 4
+HALVES = 2
+HALF = SLOTS // HALVES
+BANK = C // 2
 RUN = 2
 ENTRIES = 16
+SPARE = 16
 LAST_STORE = 256
 MX_ALIGN = 64
 
 FLOPS = 2 * SLOTS * (K * H + H * N)
 BYTES = 4 * (K * T + E * K * H + E * H * N + SLOTS + N * T) + 2 * P * (SLOTS + 2 * T) // ENTRIES
 
-RAW_BUFS = 7
-GATHER_BUFS = 3
-X_ROUNDED_BUFS = 3
-W_SCALAR_BUFS = 4
-W_VECTOR_BUFS = 2
-H_ROUNDED_BUFS = 3
-X_CODE_BUFS = 6
-W1_CODE_BUFS = 10
-H_CODE_BUFS = 4
+W_ROUNDED_BUFS = 5
+X_CODE_BUFS = 3
+W1_CODE_BUFS = 4
 A_BANKS = 6
 Y_BANKS = 2
 
@@ -54,27 +49,33 @@ def tile_moe_pre_mlp_relu_kernel(tc, xT, w1, w2, gate, offs, pos1, pos2, out):
         offs_sb = keep.tile([P, SLOTS // ENTRIES], U16, name="offs_sb")
         pos1_sb = keep.tile([P, T // ENTRIES], U16, name="pos1_sb")
         pos2_sb = keep.tile([P, T // ENTRIES], U16, name="pos2_sb")
-        y_sb = keep.tile([P, SLOTS], F32, name="y_sb")
+        gate_sb = keep.tile([P, SLOTS], F32, name="gate_sb")
         w2_raw = keep.tile([P, E, PACK, N], F32, name="w2_raw")
 
         x_rows = xT.rearrange("(g p t) n -> g t p n", g=PASSES, t=PACK)
         w1_rows = w1.rearrange("e (g p j) c -> e g p j c", g=PASSES, j=PACK)
         w2_rows = w2.rearrange("e (u t r) n -> r t u e n", t=PACK, r=2)
 
-        planes, gates, w1_raw, gathered = {}, {}, {}, {}
+        planes, w1_raw, gathered = {}, {}, {}
         x_bf, w1_bf, w2_bf, h_bf = {}, {}, {}, {}
-        x_mx, w1_mx, w2_mx, h_mx, y_banks = {}, {}, {}, {}, {}
+        x_mx, w1_mx, w2_mx, h_mx, a_banks, y_banks, y_sb = {}, {}, {}, {}, {}, {}, {}
+
+        place = {}
+
+        def staged(key, shape, dtype, after=None):
+            place[key] = place.pop(after) if after else "stage_%s" % (key,)
+            return ring.tile(shape, dtype, name="staged", tag=place[key], bufs=1, align_bytes=MX_ALIGN)
 
         def load_plane(g, t):
-            planes[g, t] = keep.tile([P, T], F32, name="plane_%d_%d" % (g, t))
-            nc.sync.dma_start(planes[g, t][:], x_rows[g, t])
+            planes[g, t] = staged("p%d%d" % (g, t), [P, T + SPARE], F32)
+            nc.gpsimd.memset(planes[g, t][:, T:], 0.0)
+            nc.sync.dma_start(planes[g, t][:, :T], x_rows[g, t])
 
-        def load_gate(pair):
-            gates[pair] = keep.tile([P, PAIR], F32, name="gate_%d" % pair)
-            nc.sync.dma_start(gates[pair][:], gate[0:P, pair * PAIR:(pair + 1) * PAIR])
+        def load_gate(s0, s1):
+            nc.sync.dma_start(gate_sb[:, s0:s1], gate[0:P, s0:s1])
 
-        def load_w1(e, g):
-            w1_raw[e, g] = ring.tile([P, PACK, H], F32, name="w1_raw", tag="raw", bufs=RAW_BUFS)
+        def load_w1(e, g, after=None):
+            w1_raw[e, g] = staged("w%d%d" % (e, g), [P, PACK, H], F32, after)
             nc.sync.dma_start(w1_raw[e, g][:], w1_rows[e, g])
 
         def load_w2():
@@ -82,193 +83,224 @@ def tile_moe_pre_mlp_relu_kernel(tc, xT, w1, w2, gate, offs, pos1, pos2, out):
                 for t in range(PACK):
                     nc.sync.dma_start(w2_raw[r:P:2, :, t, :], w2_rows[r, t])
 
-        def quantize(src, width, name, bufs, pieces=1):
+        def mx_tiles(width, name, bufs):
             codes = ring.tile([P, width], U32, name=name + "_codes", bufs=bufs, align_bytes=MX_ALIGN)
             scales = ring.tile([P, width], U8, name=name + "_scales", bufs=bufs, align_bytes=MX_ALIGN)
-            step = width // pieces
-            for c in range(0, width, step):
-                nc.vector.quantize_mx(out=codes[:, c:c + step].bitcast(FP8X4), scales=scales[:, c:c + step],
-                                      in_=src[:, c * PACK:(c + step) * PACK])
             return codes, scales
 
-        def gather(pair, g, t):
-            if t == 0:
-                gathered[pair, g] = ring.tile([P, PACK, PAIR], F32, name="gathered", bufs=GATHER_BUFS)
-            columns = PAIR // ENTRIES
-            nc.vector.tensor_tensor(gathered[pair, g][:, t, :],
-                                    planes[g, t][:].indirect(offs_sb[:, pair * columns:(pair + 1) * columns]),
-                                    gates[pair][:], MULT)
+        def quantize(mx, c0, c1, src):
+            codes, scales = mx
+            nc.vector.quantize_mx(out=codes[:, c0:c1].bitcast(FP8X4), scales=scales[:, c0:c1], in_=src)
 
-        def gather_pass(pair, g):
-            for t in range(PACK):
-                gather(pair, g, t)
+        def gather(half, g, t, s0=0, s1=HALF):
+            if (half, g) not in gathered:
+                gathered[half, g] = staged("g%d%d" % (half, g), [P, PACK, HALF], F32, "g0%d" % g if half else None)
+            a, b = half * HALF + s0, half * HALF + s1
+            nc.vector.tensor_tensor(gathered[half, g][:, t, s0:s1],
+                                    planes[g, t][:].indirect(offs_sb[:, a // ENTRIES:b // ENTRIES]),
+                                    gate_sb[:, a:b], MULT)
 
-        def prepare_x(pair, g):
-            x_bf[pair, g] = ring.tile([P, PAIR * PACK], BF16, name="x_bf", bufs=X_ROUNDED_BUFS, align_bytes=MX_ALIGN)
-            nc.scalar.copy(x_bf[pair, g][:].rearrange("p (c i t) -> p c t i", i=RUN, t=PACK),
-                           gathered[pair, g][:].rearrange("p t (c i) -> p c t i", i=RUN))
-            x_mx[pair, g] = quantize(x_bf[pair, g][:], PAIR, "x", X_CODE_BUFS)
+        def round_x(half, g, copy, after=None, s0=0, s1=HALF):
+            x_bf[half, g, s0] = staged("x%d%d_%d" % (half, g, s0), [P, (s1 - s0) * PACK], BF16, after)
+            copy(x_bf[half, g, s0][:].rearrange("p (c i t) -> p c t i", i=RUN, t=PACK),
+                 gathered[half, g][:, :, s0:s1].rearrange("p t (c i) -> p c t i", i=RUN))
 
-        def round_w1(e, g, on_vector):
-            if on_vector:
-                tile = ring.tile([P, H * PACK], BF16, name="w_bf_vector", bufs=W_VECTOR_BUFS, align_bytes=MX_ALIGN)
-                copy = nc.vector.tensor_copy
-            else:
-                tile = ring.tile([P, H * PACK], BF16, name="w_bf_scalar", bufs=W_SCALAR_BUFS, align_bytes=MX_ALIGN)
-                copy = nc.scalar.copy
-            w1_bf[e, g] = tile
-            copy(tile[:].rearrange("p (t u r j) -> p u t j r", t=PACK, r=2, j=PACK),
+        def quantize_x(half, g, s0=0, s1=HALF):
+            if (half, g) not in x_mx:
+                x_mx[half, g] = mx_tiles(HALF, "x", X_CODE_BUFS)
+            quantize(x_mx[half, g], s0, s1, x_bf[half, g, s0][:])
+
+        def round_w1(e, g, copy):
+            if e not in w1_bf:
+                w1_bf[e] = ring.tile([P, PASSES * H * PACK], BF16, name="w_bf", bufs=W_ROUNDED_BUFS,
+                                     align_bytes=MX_ALIGN)
+            copy(w1_bf[e][:, g * H * PACK:(g + 1) * H * PACK].rearrange("p (t u r j) -> p u t j r", t=PACK, r=2, j=PACK),
                  w1_raw[e, g][:].rearrange("p j (u t r) -> p u t j r", t=PACK, r=2))
 
-        def quantize_w1(e, g, pieces=1):
-            w1_mx[e, g] = quantize(w1_bf[e, g][:], H, "w1", W1_CODE_BUFS, pieces)
+        def quantize_w1(e, c0=0, c1=PASSES * H):
+            if e not in w1_mx:
+                w1_mx[e] = mx_tiles(PASSES * H, "w1", W1_CODE_BUFS)
+            quantize(w1_mx[e], c0, c1, w1_bf[e][:, c0 * PACK:c1 * PACK])
 
-        def prepare_w1(e, g, on_vector=False):
-            round_w1(e, g, on_vector)
-            quantize_w1(e, g)
+        def scalar_w1(e):
+            for g in range(PASSES):
+                round_w1(e, g, nc.scalar.copy)
 
-        def round_w2(group):
-            w2_bf[group] = ring.tile([P, W2_GROUP * N * PACK], BF16, name="w_bf_scalar", bufs=W_SCALAR_BUFS,
-                                     align_bytes=MX_ALIGN)
-            experts = slice(group * W2_GROUP, (group + 1) * W2_GROUP)
-            nc.scalar.copy(w2_bf[group][:].rearrange("p (e c i t) -> p e c t i", e=W2_GROUP, i=RUN, t=PACK),
-                           w2_raw[:, experts].rearrange("p e t (c i) -> p e c t i", i=RUN))
+        def round_w2(e0, e1):
+            if 0 not in w2_bf:
+                w2_bf[0] = ring.tile([P, E * N * PACK], BF16, name="w_bf", bufs=W_ROUNDED_BUFS, align_bytes=MX_ALIGN)
+            nc.scalar.copy(w2_bf[0][:, e0 * N * PACK:e1 * N * PACK].rearrange("p (e c i t) -> p e c t i", e=e1 - e0,
+                                                                              i=RUN, t=PACK),
+                           w2_raw[:, e0:e1].rearrange("p e t (c i) -> p e c t i", i=RUN))
 
-        def quantize_w2(group):
-            w2_mx[group] = quantize(w2_bf[group][:], W2_GROUP * N, "w2", E // W2_GROUP)
+        def quantize_w2():
+            w2_mx[0] = mx_tiles(E * N, "w2", 1)
+            quantize(w2_mx[0], 0, E * N, w2_bf[0][:])
 
-        def first_layer(e, share=False):
-            h_bf[e] = ring.tile([P, C * PACK], BF16, name="h_bf", bufs=H_ROUNDED_BUFS, align_bytes=MX_ALIGN)
-            banks = [psum.tile([P, PACK, HALF], F32, name="a_bank", bufs=A_BANKS) for half in range(C // HALF)]
-            for t in range(PACK):
-                for half, bank in enumerate(banks):
-                    s0 = (e % 2) * C + half * HALF
-                    for g in range(PASSES):
-                        w_codes, w_scales = w1_mx[e, g]
-                        x_codes, x_scales = x_mx[e // 2, g]
+        def first_layer(e, passes=range(PASSES)):
+            if e not in a_banks:
+                a_banks[e] = [psum.tile([P, PACK, BANK], F32, name="a_bank", bufs=A_BANKS) for b in range(C // BANK)]
+            w_codes, w_scales = w1_mx[e]
+            for b, bank in enumerate(a_banks[e]):
+                s0 = (e * C) % HALF + b * BANK
+                for g in passes:
+                    x_codes, x_scales = x_mx[e * C // HALF, g]
+                    for t in range(PACK):
+                        c0 = g * H + t * P
                         nc.tensor.matmul_mx(out=bank[:, t, :],
-                                            lhsT=w_codes[:, t * P:(t + 1) * P].bitcast(FP8X4),
-                                            lhsT_scale=w_scales[:, t * P:(t + 1) * P],
-                                            rhs=x_codes[:, s0:s0 + HALF].bitcast(FP8X4),
-                                            rhs_scale=x_scales[:, s0:s0 + HALF],
-                                            start=(g == 0), stop=(g == PASSES - 1))
-            for half, bank in enumerate(banks):
-                dst = h_bf[e][:, half * HALF * PACK:(half + 1) * HALF * PACK].rearrange("p (s t) -> p s t", t=PACK)
+                                            lhsT=w_codes[:, c0:c0 + P].bitcast(FP8X4),
+                                            lhsT_scale=w_scales[:, c0:c0 + P],
+                                            rhs=x_codes[:, s0:s0 + BANK].bitcast(FP8X4),
+                                            rhs_scale=x_scales[:, s0:s0 + BANK],
+                                            start=(g == 0 and t == 0), stop=(g == PASSES - 1 and t == PACK - 1))
+
+        def relu(e, after=None, share=False):
+            half = e * C // HALF
+            if half not in h_bf:
+                h_bf[half] = staged("h%d" % half, [P, HALF * PACK], BF16, after)
+            for b, bank in enumerate(a_banks[e]):
+                c0 = ((e * C) % HALF + b * BANK) * PACK
+                dst = h_bf[half][:, c0:c0 + BANK * PACK].rearrange("p (s t) -> p s t", t=PACK)
                 src = bank[:].rearrange("p t s -> p s t")
-                if share and half == 1:
+                if share and b == 1:
                     nc.vector.tensor_scalar(dst, src, 0.0, None, MAX)
                 else:
                     nc.scalar.activation(dst, src, RELU)
 
-        def quantize_h(e):
-            h_mx[e] = quantize(h_bf[e][:], C, "h", H_CODE_BUFS)
-
-        def hidden(e):
+        def hidden(e, after=None):
             first_layer(e)
-            quantize_h(e)
+            relu(e, after)
+
+        def quantize_h(e0, e1):
+            half = e0 * C // HALF
+            if half not in h_mx:
+                h_mx[half] = mx_tiles(HALF, "h", HALVES)
+            s0, s1 = e0 * C - half * HALF, e1 * C - half * HALF
+            quantize(h_mx[half], s0, s1, h_bf[half][:, s0 * PACK:s1 * PACK])
 
         def second_layer(experts):
             bank = psum.tile([P, len(experts) * C], F32, name="y_bank", bufs=Y_BANKS)
             y_banks[experts] = bank
+            w_codes, w_scales = w2_mx[0]
             for place, e in enumerate(experts):
-                w_codes, w_scales = w2_mx[e // W2_GROUP]
-                h_codes, h_scales = h_mx[e]
-                n0 = (e % W2_GROUP) * N
+                h_codes, h_scales = h_mx[e * C // HALF]
+                s0 = (e * C) % HALF
                 nc.tensor.matmul_mx(out=bank[:, place * C:(place + 1) * C],
-                                    lhsT=w_codes[:, n0:n0 + N].bitcast(FP8X4), lhsT_scale=w_scales[:, n0:n0 + N],
-                                    rhs=h_codes[:].bitcast(FP8X4), rhs_scale=h_scales[:], start=True, stop=True)
+                                    lhsT=w_codes[:, e * N:(e + 1) * N].bitcast(FP8X4),
+                                    lhsT_scale=w_scales[:, e * N:(e + 1) * N],
+                                    rhs=h_codes[:, s0:s0 + C].bitcast(FP8X4), rhs_scale=h_scales[:, s0:s0 + C],
+                                    start=True, stop=True)
 
-        def copy_y(experts):
-            nc.scalar.copy(y_sb[:, experts[0] * C:(experts[-1] + 1) * C], y_banks[experts][:])
+        def copy_y(experts, copy):
+            if 0 not in y_sb:
+                y_sb[0] = staged("y", [P, SLOTS], F32, "x10_0")
+            copy(y_sb[0][:, experts[0] * C:(experts[-1] + 1) * C], y_banks[experts][:])
 
-        load_plane(0, 0)
+        scalar, vector = nc.scalar.copy, nc.vector.tensor_copy
         nc.sync.dma_start(offs_sb[:], offs)
-        load_gate(0)
+        load_plane(0, 0)
+        load_gate(0, PAIR)
+        load_gate(PAIR, HALF)
         load_plane(0, 1)
-        load_gate(1)
-        for g in range(PASSES):
-            load_w1(0, g)
-            load_plane(0, 2 + g)
+        load_w1(0, 0)
+        load_plane(0, 2)
+        load_plane(0, 3)
+        load_w1(0, 1)
+        load_plane(1, 0)
+        load_w1(1, 0)
+        load_plane(1, 1)
+        load_w1(1, 1)
+        load_plane(1, 2)
+        load_w1(2, 0)
+        load_plane(1, 3)
+        load_gate(HALF, SLOTS)
+        load_w1(2, 1)
+        load_w1(3, 0)
+
+        gather(0, 0, 0, 0, PAIR)
+        gather(0, 0, 0, PAIR, HALF)
+        for t in range(1, PACK):
+            gather(0, 0, t)
+        scalar_w1(0)
+        load_w1(3, 1, after="w00")
+        round_x(0, 0, scalar, after="w01")
+        gather(0, 1, 0)
+        quantize_w1(0)
+        gather(0, 1, 1)
+        quantize_x(0, 0)
+        scalar_w1(1)
+        load_w1(4, 0, after="w10")
+        load_w1(4, 1, after="w11")
+        load_w2()
+        load_w1(5, 0, after="x00_0")
+        gather(0, 1, 2)
+        quantize_w1(1)
+        gather(0, 1, 3)
+        scalar_w1(2)
+        load_w1(5, 1, after="w20")
+        nc.sync.dma_start(pos1_sb[:], pos1)
+        nc.sync.dma_start(pos2_sb[:], pos2)
+        round_x(0, 1, scalar, after="w21")
         for t in range(PACK):
-            load_plane(1, t)
-            load_w1(1 + t // PASSES, t % PASSES)
-        load_gate(2)
-        for e in range(3, E):
-            for g in range(PASSES):
-                load_w1(e, g)
-            if e == 4:
-                load_gate(3)
-                load_w2()
-            if e == 5:
-                nc.sync.dma_start(pos1_sb[:], pos1)
-                nc.sync.dma_start(pos2_sb[:], pos2)
-
-        for plane in range(PLANES):
-            g, t = divmod(plane, PACK)
-            gather(0, g, t)
-            gather(1, g, t)
-            if plane < 3 * PASSES:
-                prepare_w1(*divmod(plane, PASSES))
-            if plane == PACK - 1:
-                prepare_x(0, 0)
-                prepare_x(1, 0)
-
-        prepare_x(0, 1)
-        gather_pass(2, 0)
-        prepare_w1(3, 0)
-        prepare_w1(3, 1)
-
-        prepare_x(1, 1)
-        gather_pass(2, 1)
-        prepare_w1(4, 0)
-        hidden(0)
+            gather(1, 0, t)
+        quantize_w1(2)
+        quantize_x(0, 1)
+        scalar_w1(3)
+        load_w1(6, 0, after="w30")
+        load_w1(6, 1, after="x01_0")
+        round_x(1, 0, scalar, after="w31")
+        for t in range(PACK):
+            gather(1, 1, t)
+        hidden(0, after="g10")
         hidden(1)
-
-        prepare_x(2, 0)
-        gather_pass(3, 0)
-        prepare_w1(4, 1)
         hidden(2)
+        quantize_w1(3)
+        quantize_x(1, 0)
+        scalar_w1(4)
+        load_w1(7, 0, after="w40")
+        load_w1(7, 1, after="w41")
+        round_x(1, 1, vector, "p00", 0, PAIR)
+        round_x(1, 1, vector, "p01", PAIR, HALF)
+        quantize_w1(4)
+        quantize_x(1, 1, 0, PAIR)
+        quantize_x(1, 1, PAIR, HALF)
         hidden(3)
-
-        prepare_x(2, 1)
-        gather_pass(3, 1)
-
-        prepare_w1(5, 0)
-        prepare_x(3, 0)
-        prepare_x(3, 1)
-        round_w2(0)
-        quantize_w2(0)
-        prepare_w1(5, 1)
-        hidden(4)
+        scalar_w1(5)
+        round_w1(6, 0, vector)
+        quantize_w1(5)
+        round_w1(6, 1, vector)
+        quantize_h(0, 4)
+        quantize_w1(6)
+        round_w2(0, E)
+        hidden(4, after="g11")
+        hidden(5)
+        hidden(6)
+        round_w1(7, 0, vector)
+        quantize_w2()
+        round_w1(7, 1, vector)
         second_layer((0, 1))
         second_layer((2, 3))
-        round_w2(1)
-        first_layer(5)
-        prepare_w1(6, 0, on_vector=True)
-        prepare_w1(6, 1, on_vector=True)
-        first_layer(6)
-        copy_y((0, 1))
-        copy_y((2, 3))
-
-        prepare_w1(7, 0, on_vector=True)
-        round_w1(7, 1, on_vector=True)
-        quantize_w1(7, 1, pieces=PACK)
-        quantize_w2(1)
-        quantize_h(5)
-        quantize_h(6)
+        quantize_w1(7, 0, H)
+        first_layer(7, [0])
+        quantize_w1(7, H, 2 * H)
+        first_layer(7, [1])
+        copy_y((0, 1), scalar)
+        copy_y((2, 3), scalar)
+        quantize_h(4, 6)
         second_layer((4, 5))
-        first_layer(7, share=True)
-        copy_y((4, 5))
+        quantize_h(6, 7)
+        relu(7, share=True)
+        copy_y((4, 5), scalar)
         second_layer((6,))
-        copy_y((6,))
-        quantize_h(7)
+        copy_y((6,), scalar)
+        quantize_h(7, 8)
         second_layer((7,))
-        copy_y((7,))
+        copy_y((7,), vector)
 
-        first = ring.tile([P, T], F32, name="first", tag="raw", bufs=RAW_BUFS)
-        nc.vector.tensor_copy(first[:], y_sb[:].indirect(pos1_sb[:]))
-        for t0, t1 in ((0, T - LAST_STORE), (T - LAST_STORE, T)):
-            both = ring.tile([P, t1 - t0], F32, name="both", tag="raw", bufs=RAW_BUFS)
-            nc.vector.tensor_tensor(both[:], y_sb[:].indirect(pos2_sb[:, t0 // ENTRIES:t1 // ENTRIES]),
+        first = staged("first", [P, T], F32, "w60")
+        nc.vector.tensor_copy(first[:], y_sb[0][:].indirect(pos1_sb[:]))
+        for t0, t1, after in ((0, T - LAST_STORE, "w61"), (T - LAST_STORE, T, "w70")):
+            both = staged("both%d" % t0, [P, t1 - t0], F32, after)
+            nc.vector.tensor_tensor(both[:], y_sb[0][:].indirect(pos2_sb[:, t0 // ENTRIES:t1 // ENTRIES]),
                                     first[:, t0:t1], ADD)
             nc.sync.dma_start(out[:, t0:t1], both[:])

@@ -92,18 +92,32 @@ def tile_moe_pre_mlp_relu_kernel(tc, xT, w1, w2, gate, offs, pos1, pos2, out):
             codes, scales = mx
             nc.vector.quantize_mx(out=codes[:, c0:c1].bitcast(FP8X4), scales=scales[:, c0:c1], in_=src)
 
-        def gather(half, g, t, s0=0, s1=HALF):
+        def gather(half, g, t, s0=0, s1=HALF, plain=False):
             if (half, g) not in gathered:
                 gathered[half, g] = staged("g%d%d" % (half, g), [P, PACK, HALF], F32, "g0%d" % g if half else None)
             a, b = half * HALF + s0, half * HALF + s1
-            nc.vector.tensor_tensor(gathered[half, g][:, t, s0:s1],
-                                    planes[g, t][:].indirect(offs_sb[:, a // ENTRIES:b // ENTRIES]),
-                                    gate_sb[:, a:b], MULT)
+            picked = planes[g, t][:].indirect(offs_sb[:, a // ENTRIES:b // ENTRIES])
+            if plain:
+                nc.vector.tensor_copy(gathered[half, g][:, t, s0:s1], picked)
+            else:
+                nc.vector.tensor_tensor(gathered[half, g][:, t, s0:s1], picked, gate_sb[:, a:b], MULT)
+
+        def gate_x(half, g, engine, after, s0, s1, piece):
+            x_bf[half, g, s0] = staged("x%d%d_%d" % (half, g, s0), [P, (s1 - s0) * PACK], BF16, after)
+            for a in range(s0, s1, piece):
+                weights = gate_sb[:, half * HALF + a:half * HALF + a + piece].rearrange("p (c i) -> p c i", i=RUN)
+                engine.tensor_tensor(
+                    x_bf[half, g, s0][:, (a - s0) * PACK:(a - s0 + piece) * PACK].rearrange("p (c i t) -> p c t i", i=RUN, t=PACK),
+                    gathered[half, g][:, :, a:a + piece].rearrange("p t (c i) -> p c t i", i=RUN),
+                    weights.unsqueeze(2).to_broadcast([P, piece // RUN, PACK, RUN]), MULT)
 
         def round_x(half, g, copy, after=None, s0=0, s1=HALF):
             x_bf[half, g, s0] = staged("x%d%d_%d" % (half, g, s0), [P, (s1 - s0) * PACK], BF16, after)
             copy(x_bf[half, g, s0][:].rearrange("p (c i t) -> p c t i", i=RUN, t=PACK),
                  gathered[half, g][:, :, s0:s1].rearrange("p t (c i) -> p c t i", i=RUN))
+
+        def gpsimd_copy(dst, src):
+            nc.gpsimd.tensor_scalar(dst, src, 1.0, 0.0, MULT, ADD)
 
         def quantize_x(half, g, s0=0, s1=HALF):
             if (half, g) not in x_mx:
@@ -126,12 +140,15 @@ def tile_moe_pre_mlp_relu_kernel(tc, xT, w1, w2, gate, offs, pos1, pos2, out):
             for g in range(PASSES):
                 round_w1(e, g, nc.scalar.copy)
 
-        def round_w2(e0, e1):
+        def round_w2(e0, e1, copy):
             if 0 not in w2_bf:
                 w2_bf[0] = ring.tile([P, E * N * PACK], BF16, name="w_bf", bufs=W_ROUNDED_BUFS, align_bytes=MX_ALIGN)
-            nc.scalar.copy(w2_bf[0][:, e0 * N * PACK:e1 * N * PACK].rearrange("p (e c i t) -> p e c t i", e=e1 - e0,
-                                                                              i=RUN, t=PACK),
-                           w2_raw[:, e0:e1].rearrange("p e t (c i) -> p e c t i", i=RUN))
+            dst = w2_bf[0][:, e0 * N * PACK:e1 * N * PACK].rearrange("p (e c i t) -> p e c t i", e=e1 - e0, i=RUN, t=PACK)
+            src = w2_raw[:, e0:e1].rearrange("p e t (c i) -> p e c t i", i=RUN)
+            if e1 - e0 == 1:
+                copy(dst[:, 0], src[:, 0])
+            else:
+                copy(dst, src)
 
         def quantize_w2():
             w2_mx[0] = mx_tiles(E * N, "w2", 1)
@@ -247,53 +264,51 @@ def tile_moe_pre_mlp_relu_kernel(tc, xT, w1, w2, gate, offs, pos1, pos2, out):
         quantize_x(0, 1)
         scalar_w1(3)
         load_w1(6, 0, after="w30")
-        load_w1(6, 1, after="x01_0")
-        round_x(1, 0, scalar, after="w31")
+        load_w1(6, 1, after="w31")
+        round_x(1, 0, gpsimd_copy, after="x01_0")
         for t in range(PACK):
-            gather(1, 1, t)
-        hidden(0, after="g10")
+            gather(1, 1, t, plain=True)
+        scalar_w1(4)
+        for e in range(4):
+            round_w2(e, e + 1, gpsimd_copy)
+        load_w1(7, 0, after="w40")
+        hidden(0, after="w41")
         hidden(1)
         hidden(2)
         quantize_w1(3)
+        gate_x(1, 1, nc.vector, "p01", 0, PAIR, PAIR)
         quantize_x(1, 0)
-        scalar_w1(4)
-        load_w1(7, 0, after="w40")
-        load_w1(7, 1, after="w41")
-        round_x(1, 1, vector, "p00", 0, PAIR)
-        round_x(1, 1, vector, "p01", PAIR, HALF)
+        gate_x(1, 1, nc.vector, "p02", PAIR, HALF, PAIR)
         quantize_w1(4)
         quantize_x(1, 1, 0, PAIR)
         quantize_x(1, 1, PAIR, HALF)
-        hidden(3)
         scalar_w1(5)
-        round_w1(6, 0, vector)
+        load_w1(7, 1, after="g10")
+        hidden(3)
+        round_w2(4, E, scalar)
+        scalar_w1(6)
+        scalar_w1(7)
         quantize_w1(5)
-        round_w1(6, 1, vector)
         quantize_h(0, 4)
+        quantize_w2()
         quantize_w1(6)
-        round_w2(0, E)
+        quantize_w1(7)
         hidden(4, after="g11")
         hidden(5)
-        hidden(6)
-        round_w1(7, 0, vector)
-        quantize_w2()
-        round_w1(7, 1, vector)
         second_layer((0, 1))
         second_layer((2, 3))
-        quantize_w1(7, 0, H)
-        first_layer(7, [0])
-        quantize_w1(7, H, 2 * H)
-        first_layer(7, [1])
+        hidden(6)
+        first_layer(7)
         copy_y((0, 1), scalar)
         copy_y((2, 3), scalar)
         quantize_h(4, 6)
         second_layer((4, 5))
-        quantize_h(6, 7)
         relu(7, share=True)
+        quantize_h(6, 7)
         copy_y((4, 5), scalar)
         second_layer((6,))
-        copy_y((6,), scalar)
         quantize_h(7, 8)
+        copy_y((6,), scalar)
         second_layer((7,))
         copy_y((7,), vector)
 

@@ -32,7 +32,6 @@ MX_ALIGN = 64
 FLOPS = 2 * SLOTS * (K * H + H * N)
 BYTES = 4 * (K * T + E * K * H + E * H * N + SLOTS + N * T) + 2 * P * (SLOTS + 2 * T) // ENTRIES
 
-W_ROUNDED_BUFS = 5
 X_CODE_BUFS = 3
 W1_CODE_BUFS = 4
 A_BANKS = 6
@@ -83,8 +82,11 @@ def tile_moe_pre_mlp_relu_kernel(tc, xT, w1, w2, gate, offs, pos1, pos2, out):
                 for t in range(PACK):
                     nc.sync.dma_start(w2_raw[r:P:2, :, t, :], w2_rows[r, t])
 
-        def mx_tiles(width, name, bufs):
-            codes = ring.tile([P, width], U32, name=name + "_codes", bufs=bufs, align_bytes=MX_ALIGN)
+        def mx_tiles(width, name, bufs, after=None):
+            if after:
+                codes = staged(name + "_codes_" + after, [P, width], U32, after)
+            else:
+                codes = ring.tile([P, width], U32, name=name + "_codes", bufs=bufs, align_bytes=MX_ALIGN)
             scales = ring.tile([P, width], U8, name=name + "_scales", bufs=bufs, align_bytes=MX_ALIGN)
             return codes, scales
 
@@ -117,17 +119,17 @@ def tile_moe_pre_mlp_relu_kernel(tc, xT, w1, w2, gate, offs, pos1, pos2, out):
                  gathered[half, g][:, :, s0:s1].rearrange("p t (c i) -> p c t i", i=RUN))
 
         def gpsimd_copy(dst, src):
-            nc.gpsimd.tensor_scalar(dst, src, 1.0, 0.0, MULT, ADD)
+            nc.gpsimd.tensor_scalar(dst.rearrange("p c t i -> p c i t"), src.rearrange("p c t i -> p c i t"),
+                                    1.0, 0.0, MULT, ADD)
 
         def quantize_x(half, g, s0=0, s1=HALF):
             if (half, g) not in x_mx:
                 x_mx[half, g] = mx_tiles(HALF, "x", X_CODE_BUFS)
             quantize(x_mx[half, g], s0, s1, x_bf[half, g, s0][:])
 
-        def round_w1(e, g, copy):
+        def round_w1(e, g, copy, after=None):
             if e not in w1_bf:
-                w1_bf[e] = ring.tile([P, PASSES * H * PACK], BF16, name="w_bf", bufs=W_ROUNDED_BUFS,
-                                     align_bytes=MX_ALIGN)
+                w1_bf[e] = staged("r%d" % e, [P, PASSES * H * PACK], BF16, after)
             copy(w1_bf[e][:, g * H * PACK:(g + 1) * H * PACK].rearrange("p (t u r j) -> p u t j r", t=PACK, r=2, j=PACK),
                  w1_raw[e, g][:].rearrange("p j (u t r) -> p u t j r", t=PACK, r=2))
 
@@ -136,13 +138,13 @@ def tile_moe_pre_mlp_relu_kernel(tc, xT, w1, w2, gate, offs, pos1, pos2, out):
                 w1_mx[e] = mx_tiles(PASSES * H, "w1", W1_CODE_BUFS)
             quantize(w1_mx[e], c0, c1, w1_bf[e][:, c0 * PACK:c1 * PACK])
 
-        def scalar_w1(e):
+        def scalar_w1(e, after=None):
             for g in range(PASSES):
-                round_w1(e, g, nc.scalar.copy)
+                round_w1(e, g, nc.scalar.copy, after)
 
-        def round_w2(e0, e1, copy):
+        def round_w2(e0, e1, copy, after=None):
             if 0 not in w2_bf:
-                w2_bf[0] = ring.tile([P, E * N * PACK], BF16, name="w_bf", bufs=W_ROUNDED_BUFS, align_bytes=MX_ALIGN)
+                w2_bf[0] = staged("rw2", [P, E * N * PACK], BF16, after)
             dst = w2_bf[0][:, e0 * N * PACK:e1 * N * PACK].rearrange("p (e c i t) -> p e c t i", e=e1 - e0, i=RUN, t=PACK)
             src = w2_raw[:, e0:e1].rearrange("p e t (c i) -> p e c t i", i=RUN)
             if e1 - e0 == 1:
@@ -150,8 +152,8 @@ def tile_moe_pre_mlp_relu_kernel(tc, xT, w1, w2, gate, offs, pos1, pos2, out):
             else:
                 copy(dst, src)
 
-        def quantize_w2():
-            w2_mx[0] = mx_tiles(E * N, "w2", 1)
+        def quantize_w2(after=None):
+            w2_mx[0] = mx_tiles(E * N, "w2", 1, after)
             quantize(w2_mx[0], 0, E * N, w2_bf[0][:])
 
         def first_layer(e, passes=range(PASSES)):
@@ -171,46 +173,48 @@ def tile_moe_pre_mlp_relu_kernel(tc, xT, w1, w2, gate, offs, pos1, pos2, out):
                                             rhs_scale=x_scales[:, s0:s0 + BANK],
                                             start=(g == 0 and t == 0), stop=(g == PASSES - 1 and t == PACK - 1))
 
-        def relu(e, after=None, share=False):
-            half = e * C // HALF
-            if half not in h_bf:
-                h_bf[half] = staged("h%d" % half, [P, HALF * PACK], BF16, after)
+        def open_h(e0, e1, after):
+            tile = staged("h%d" % e0, [P, (e1 - e0) * C * PACK], BF16, after)
+            for e in range(e0, e1):
+                h_bf[e] = (tile, (e - e0) * C * PACK)
+
+        def relu(e, share=False):
+            tile, first_column = h_bf[e]
             for b, bank in enumerate(a_banks[e]):
-                c0 = ((e * C) % HALF + b * BANK) * PACK
-                dst = h_bf[half][:, c0:c0 + BANK * PACK].rearrange("p (s t) -> p s t", t=PACK)
+                c0 = first_column + b * BANK * PACK
+                dst = tile[:, c0:c0 + BANK * PACK].rearrange("p (s t) -> p s t", t=PACK)
                 src = bank[:].rearrange("p t s -> p s t")
                 if share and b == 1:
                     nc.vector.tensor_scalar(dst, src, 0.0, None, MAX)
                 else:
                     nc.scalar.activation(dst, src, RELU)
 
-        def hidden(e, after=None):
+        def hidden(e):
             first_layer(e)
-            relu(e, after)
+            relu(e)
 
-        def quantize_h(e0, e1):
-            half = e0 * C // HALF
-            if half not in h_mx:
-                h_mx[half] = mx_tiles(HALF, "h", HALVES)
-            s0, s1 = e0 * C - half * HALF, e1 * C - half * HALF
-            quantize(h_mx[half], s0, s1, h_bf[half][:, s0 * PACK:s1 * PACK])
+        def quantize_h(e0, e1, after=None):
+            mx = mx_tiles((e1 - e0) * C, "h%d" % e0, 1, after)
+            tile, c0 = h_bf[e0]
+            quantize(mx, 0, (e1 - e0) * C, tile[:, c0:c0 + (e1 - e0) * C * PACK])
+            for e in range(e0, e1):
+                h_mx[e] = (mx, (e - e0) * C)
 
         def second_layer(experts):
             bank = psum.tile([P, len(experts) * C], F32, name="y_bank", bufs=Y_BANKS)
             y_banks[experts] = bank
             w_codes, w_scales = w2_mx[0]
             for place, e in enumerate(experts):
-                h_codes, h_scales = h_mx[e * C // HALF]
-                s0 = (e * C) % HALF
+                (h_codes, h_scales), s0 = h_mx[e]
                 nc.tensor.matmul_mx(out=bank[:, place * C:(place + 1) * C],
                                     lhsT=w_codes[:, e * N:(e + 1) * N].bitcast(FP8X4),
                                     lhsT_scale=w_scales[:, e * N:(e + 1) * N],
                                     rhs=h_codes[:, s0:s0 + C].bitcast(FP8X4), rhs_scale=h_scales[:, s0:s0 + C],
                                     start=True, stop=True)
 
-        def copy_y(experts, copy):
+        def copy_y(experts, copy, after=None):
             if 0 not in y_sb:
-                y_sb[0] = staged("y", [P, SLOTS], F32, "x10_0")
+                y_sb[0] = staged("y", [P, SLOTS], F32, after)
             copy(y_sb[0][:, experts[0] * C:(experts[-1] + 1) * C], y_banks[experts][:])
 
         scalar, vector = nc.scalar.copy, nc.vector.tensor_copy
@@ -270,11 +274,11 @@ def tile_moe_pre_mlp_relu_kernel(tc, xT, w1, w2, gate, offs, pos1, pos2, out):
             gather(1, 1, t, plain=True)
         scalar_w1(4)
         for e in range(4):
-            round_w2(e, e + 1, gpsimd_copy)
+            round_w2(e, e + 1, gpsimd_copy, "r0")
         load_w1(7, 0, after="w40")
-        hidden(0, after="w41")
+        open_h(0, 2, after="w41")
+        hidden(0)
         hidden(1)
-        hidden(2)
         quantize_w1(3)
         gate_x(1, 1, nc.vector, "p01", 0, PAIR, PAIR)
         quantize_x(1, 0)
@@ -282,39 +286,44 @@ def tile_moe_pre_mlp_relu_kernel(tc, xT, w1, w2, gate, offs, pos1, pos2, out):
         quantize_w1(4)
         quantize_x(1, 1, 0, PAIR)
         quantize_x(1, 1, PAIR, HALF)
-        scalar_w1(5)
+        scalar_w1(5, "r1")
         load_w1(7, 1, after="g10")
-        hidden(3)
         round_w2(4, E, scalar)
-        scalar_w1(6)
-        scalar_w1(7)
+        scalar_w1(6, "r2")
+        open_h(2, 4, after="w60")
+        hidden(2)
+        hidden(3)
+        scalar_w1(7, "r3")
         quantize_w1(5)
-        quantize_h(0, 4)
-        quantize_w2()
         quantize_w1(6)
-        quantize_w1(7)
-        hidden(4, after="g11")
+        open_h(4, 5, after="w70")
+        hidden(4)
+        open_h(5, 8, after="w71")
         hidden(5)
+        hidden(6)
+        quantize_w1(7, 0, H)
+        first_layer(7, [0])
+        quantize_h(0, 2, "r5")
+        quantize_w1(7, H, 2 * H)
+        first_layer(7, [1])
+        quantize_w2("r7")
+        quantize_h(2, 4, "r6")
+        quantize_h(4, 5)
         second_layer((0, 1))
         second_layer((2, 3))
-        hidden(6)
-        first_layer(7)
-        copy_y((0, 1), scalar)
-        copy_y((2, 3), scalar)
-        quantize_h(4, 6)
-        second_layer((4, 5))
         relu(7, share=True)
-        quantize_h(6, 7)
-        copy_y((4, 5), scalar)
-        second_layer((6,))
+        quantize_h(5, 7)
+        copy_y((0, 1), scalar, after="w61")
+        copy_y((2, 3), scalar)
         quantize_h(7, 8)
-        copy_y((6,), scalar)
-        second_layer((7,))
-        copy_y((7,), vector)
+        second_layer((4, 5))
+        second_layer((6, 7))
+        copy_y((4, 5), vector)
+        copy_y((6, 7), scalar)
 
-        first = staged("first", [P, T], F32, "w60")
+        first = staged("first", [P, T], F32, "w50")
         nc.vector.tensor_copy(first[:], y_sb[0][:].indirect(pos1_sb[:]))
-        for t0, t1, after in ((0, T - LAST_STORE, "w61"), (T - LAST_STORE, T, "w70")):
+        for t0, t1, after in ((0, T - LAST_STORE, "w51"), (T - LAST_STORE, T, "x10_0")):
             both = staged("both%d" % t0, [P, t1 - t0], F32, after)
             nc.vector.tensor_tensor(both[:], y_sb[0][:].indirect(pos2_sb[:, t0 // ENTRIES:t1 // ENTRIES]),
                                     first[:, t0:t1], ADD)

@@ -34,8 +34,7 @@ BYTES = 4 * (K * T + E * K * H + E * H * N + SLOTS + N * T) + 2 * P * (SLOTS + 2
 
 X_CODE_BUFS = 3
 W1_CODE_BUFS = 4
-A_BANKS = 6
-Y_BANKS = 2
+BANKS = 8
 
 
 def tile_moe_pre_mlp_relu_kernel(tc, xT, w1, w2, gate, offs, pos1, pos2, out):
@@ -48,14 +47,12 @@ def tile_moe_pre_mlp_relu_kernel(tc, xT, w1, w2, gate, offs, pos1, pos2, out):
         offs_sb = keep.tile([P, SLOTS // ENTRIES], U16, name="offs_sb")
         pos1_sb = keep.tile([P, T // ENTRIES], U16, name="pos1_sb")
         pos2_sb = keep.tile([P, T // ENTRIES], U16, name="pos2_sb")
-        gate_sb = keep.tile([P, SLOTS], F32, name="gate_sb")
-        w2_raw = keep.tile([P, E, PACK, N], F32, name="w2_raw")
 
         x_rows = xT.rearrange("(g p t) n -> g t p n", g=PASSES, t=PACK)
         w1_rows = w1.rearrange("e (g p j) c -> e g p j c", g=PASSES, j=PACK)
         w2_rows = w2.rearrange("e (u t r) n -> r t u e n", t=PACK, r=2)
 
-        planes, w1_raw, gathered = {}, {}, {}
+        planes, gates, w1_raw, w2_raw, gathered = {}, {}, {}, {}, {}
         x_bf, w1_bf, w2_bf, h_bf = {}, {}, {}, {}
         x_mx, w1_mx, w2_mx, h_mx, a_banks, y_banks, y_sb = {}, {}, {}, {}, {}, {}, {}
 
@@ -71,16 +68,20 @@ def tile_moe_pre_mlp_relu_kernel(tc, xT, w1, w2, gate, offs, pos1, pos2, out):
             nc.sync.dma_start(planes[g, t][:, :T], x_rows[g, t])
 
         def load_gate(s0, s1):
-            nc.sync.dma_start(gate_sb[:, s0:s1], gate[0:P, s0:s1])
+            half = s0 // HALF
+            if half not in gates:
+                gates[half] = staged("gate%d" % half, [P, HALF], F32)
+            nc.sync.dma_start(gates[half][:, s0 - half * HALF:s1 - half * HALF], gate[0:P, s0:s1])
 
         def load_w1(e, g, after=None):
             w1_raw[e, g] = staged("w%d%d" % (e, g), [P, PACK, H], F32, after)
             nc.sync.dma_start(w1_raw[e, g][:], w1_rows[e, g])
 
-        def load_w2():
+        def load_w2(after):
+            w2_raw[0] = staged("w2", [P, E, PACK, N], F32, after)
             for r in range(2):
                 for t in range(PACK):
-                    nc.sync.dma_start(w2_raw[r:P:2, :, t, :], w2_rows[r, t])
+                    nc.sync.dma_start(w2_raw[0][r:P:2, :, t, :], w2_rows[r, t])
 
         def mx_tiles(width, name, bufs, after=None):
             if after:
@@ -94,38 +95,53 @@ def tile_moe_pre_mlp_relu_kernel(tc, xT, w1, w2, gate, offs, pos1, pos2, out):
             codes, scales = mx
             nc.vector.quantize_mx(out=codes[:, c0:c1].bitcast(FP8X4), scales=scales[:, c0:c1], in_=src)
 
-        def gather(half, g, t, s0=0, s1=HALF, plain=False):
-            if (half, g) not in gathered:
-                gathered[half, g] = staged("g%d%d" % (half, g), [P, PACK, HALF], F32, "g0%d" % g if half else None)
-            a, b = half * HALF + s0, half * HALF + s1
+        def open_batch(name, s0, s1, g, after=None):
+            gathered[name] = (staged("g" + name, [P, PACK, s1 - s0], F32, after), s0, s1, g)
+
+        def gather(name, t, a=None, b=None, plain=False):
+            tile, s0, s1, g = gathered[name]
+            a, b = (s0, s1) if a is None else (a, b)
             picked = planes[g, t][:].indirect(offs_sb[:, a // ENTRIES:b // ENTRIES])
             if plain:
-                nc.vector.tensor_copy(gathered[half, g][:, t, s0:s1], picked)
+                nc.vector.tensor_copy(tile[:, t, a - s0:b - s0], picked)
             else:
-                nc.vector.tensor_tensor(gathered[half, g][:, t, s0:s1], picked, gate_sb[:, a:b], MULT)
+                nc.vector.tensor_tensor(tile[:, t, a - s0:b - s0], picked, gates[a // HALF][:, a % HALF:a % HALF + b - a], MULT)
 
-        def gate_x(half, g, engine, after, s0, s1, piece):
-            x_bf[half, g, s0] = staged("x%d%d_%d" % (half, g, s0), [P, (s1 - s0) * PACK], BF16, after)
-            for a in range(s0, s1, piece):
-                weights = gate_sb[:, half * HALF + a:half * HALF + a + piece].rearrange("p (c i) -> p c i", i=RUN)
-                engine.tensor_tensor(
-                    x_bf[half, g, s0][:, (a - s0) * PACK:(a - s0 + piece) * PACK].rearrange("p (c i t) -> p c t i", i=RUN, t=PACK),
-                    gathered[half, g][:, :, a:a + piece].rearrange("p t (c i) -> p c t i", i=RUN),
-                    weights.unsqueeze(2).to_broadcast([P, piece // RUN, PACK, RUN]), MULT)
+        def open_x(name, after=None):
+            tile, s0, s1, g = gathered[name]
+            x_bf[name] = staged("x" + name, [P, (s1 - s0) * PACK], BF16, after)
 
-        def round_x(half, g, copy, after=None, s0=0, s1=HALF):
-            x_bf[half, g, s0] = staged("x%d%d_%d" % (half, g, s0), [P, (s1 - s0) * PACK], BF16, after)
-            copy(x_bf[half, g, s0][:].rearrange("p (c i t) -> p c t i", i=RUN, t=PACK),
-                 gathered[half, g][:, :, s0:s1].rearrange("p t (c i) -> p c t i", i=RUN))
+        def x_views(name, a, b):
+            tile, s0, s1, g = gathered[name]
+            return (x_bf[name][:, (a - s0) * PACK:(b - s0) * PACK].rearrange("p (c i t) -> p c t i", i=RUN, t=PACK),
+                    tile[:, :, a - s0:b - s0].rearrange("p t (c i) -> p c t i", i=RUN))
+
+        def round_x(name, copy, a, b):
+            copy(*x_views(name, a, b))
+
+        def gate_x_vector(name, a, b):
+            dst, src = x_views(name, a, b)
+            weights = gates[a // HALF][:, a % HALF:a % HALF + b - a].rearrange("p (c i) -> p c i", i=RUN)
+            nc.vector.tensor_tensor(dst, src, weights.unsqueeze(2).to_broadcast([P, (b - a) // RUN, PACK, RUN]), MULT)
+
+        def gate_x_gpsimd(name, a, b):
+            tile, s0, s1, g = gathered[name]
+            weights = gates[a // HALF][:, a % HALF:a % HALF + b - a]
+            nc.gpsimd.tensor_tensor(x_bf[name][:, (a - s0) * PACK:(b - s0) * PACK].rearrange("p (s t) -> p s t", t=PACK),
+                                    tile[:, :, a - s0:b - s0].rearrange("p t s -> p s t"),
+                                    weights.unsqueeze(2).to_broadcast([P, b - a, PACK]), MULT)
 
         def gpsimd_copy(dst, src):
             nc.gpsimd.tensor_scalar(dst.rearrange("p c t i -> p c i t"), src.rearrange("p c t i -> p c i t"),
                                     1.0, 0.0, MULT, ADD)
 
-        def quantize_x(half, g, s0=0, s1=HALF):
+        def quantize_x(name, a=None, b=None):
+            tile, s0, s1, g = gathered[name]
+            a, b = (s0, s1) if a is None else (a, b)
+            half = s0 // HALF
             if (half, g) not in x_mx:
                 x_mx[half, g] = mx_tiles(HALF, "x", X_CODE_BUFS)
-            quantize(x_mx[half, g], s0, s1, x_bf[half, g, s0][:])
+            quantize(x_mx[half, g], a % HALF, a % HALF + b - a, x_bf[name][:, (a - s0) * PACK:(b - s0) * PACK])
 
         def round_w1(e, g, copy, after=None):
             if e not in w1_bf:
@@ -146,7 +162,7 @@ def tile_moe_pre_mlp_relu_kernel(tc, xT, w1, w2, gate, offs, pos1, pos2, out):
             if 0 not in w2_bf:
                 w2_bf[0] = staged("rw2", [P, E * N * PACK], BF16, after)
             dst = w2_bf[0][:, e0 * N * PACK:e1 * N * PACK].rearrange("p (e c i t) -> p e c t i", e=e1 - e0, i=RUN, t=PACK)
-            src = w2_raw[:, e0:e1].rearrange("p e t (c i) -> p e c t i", i=RUN)
+            src = w2_raw[0][:, e0:e1].rearrange("p e t (c i) -> p e c t i", i=RUN)
             if e1 - e0 == 1:
                 copy(dst[:, 0], src[:, 0])
             else:
@@ -158,7 +174,7 @@ def tile_moe_pre_mlp_relu_kernel(tc, xT, w1, w2, gate, offs, pos1, pos2, out):
 
         def first_layer(e, passes=range(PASSES)):
             if e not in a_banks:
-                a_banks[e] = [psum.tile([P, PACK, BANK], F32, name="a_bank", bufs=A_BANKS) for b in range(C // BANK)]
+                a_banks[e] = [psum.tile([P, PACK, BANK], F32, name="a_bank", tag="bank", bufs=BANKS) for b in range(C // BANK)]
             w_codes, w_scales = w1_mx[e]
             for b, bank in enumerate(a_banks[e]):
                 s0 = (e * C) % HALF + b * BANK
@@ -193,15 +209,18 @@ def tile_moe_pre_mlp_relu_kernel(tc, xT, w1, w2, gate, offs, pos1, pos2, out):
             first_layer(e)
             relu(e)
 
-        def quantize_h(e0, e1, after=None):
+        def open_h_codes(e0, e1, after=None):
             mx = mx_tiles((e1 - e0) * C, "h%d" % e0, 1, after)
-            tile, c0 = h_bf[e0]
-            quantize(mx, 0, (e1 - e0) * C, tile[:, c0:c0 + (e1 - e0) * C * PACK])
             for e in range(e0, e1):
                 h_mx[e] = (mx, (e - e0) * C)
 
+        def quantize_h(e0, e1):
+            tile, c0 = h_bf[e0]
+            mx, s0 = h_mx[e0]
+            quantize(mx, s0, s0 + (e1 - e0) * C, tile[:, c0:c0 + (e1 - e0) * C * PACK])
+
         def second_layer(experts):
-            bank = psum.tile([P, len(experts) * C], F32, name="y_bank", bufs=Y_BANKS)
+            bank = psum.tile([P, len(experts) * C], F32, name="y_bank", tag="bank", bufs=BANKS)
             y_banks[experts] = bank
             w_codes, w_scales = w2_mx[0]
             for place, e in enumerate(experts):
@@ -234,96 +253,110 @@ def tile_moe_pre_mlp_relu_kernel(tc, xT, w1, w2, gate, offs, pos1, pos2, out):
         load_plane(1, 2)
         load_w1(2, 0)
         load_plane(1, 3)
-        load_gate(HALF, SLOTS)
         load_w1(2, 1)
         load_w1(3, 0)
+        load_w1(3, 1)
+        load_gate(HALF, SLOTS)
 
-        gather(0, 0, 0, 0, PAIR)
-        gather(0, 0, 0, PAIR, HALF)
+        open_batch("A", 0, HALF, 0)
+        gather("A", 0, 0, PAIR)
+        gather("A", 0, PAIR, HALF)
         for t in range(1, PACK):
-            gather(0, 0, t)
+            gather("A", t)
         scalar_w1(0)
-        load_w1(3, 1, after="w00")
-        round_x(0, 0, scalar, after="w01")
-        gather(0, 1, 0)
+        load_w1(4, 0, after="w00")
+        open_x("A", after="w01")
+        round_x("A", scalar, 0, HALF)
+        load_w1(4, 1, after="gA")
+        open_batch("C", 0, HALF, 1)
+        gather("C", 0)
         quantize_w1(0)
-        gather(0, 1, 1)
-        quantize_x(0, 0)
+        gather("C", 1)
+        quantize_x("A")
+        load_w1(5, 0, after="xA")
         scalar_w1(1)
-        load_w1(4, 0, after="w10")
-        load_w1(4, 1, after="w11")
-        load_w2()
-        load_w1(5, 0, after="x00_0")
-        gather(0, 1, 2)
+        load_w1(5, 1, after="w10")
+        load_w1(6, 0, after="w11")
+        gather("C", 2)
         quantize_w1(1)
-        gather(0, 1, 3)
+        gather("C", 3)
+        open_batch("B2", HALF, HALF + PAIR, 0, after="gate0")
+        for t in range(PACK):
+            gather("B2", t, plain=True)
+        open_x("C")
+        round_x("C", gpsimd_copy, 0, HALF)
         scalar_w1(2)
-        load_w1(5, 1, after="w20")
-        nc.sync.dma_start(pos1_sb[:], pos1)
-        nc.sync.dma_start(pos2_sb[:], pos2)
-        round_x(0, 1, scalar, after="w21")
+        load_w1(6, 1, after="w20")
+        load_w1(7, 0, after="w21")
+        quantize_x("C")
+        open_batch("B3", HALF + PAIR, SLOTS, 0, after="gC")
         for t in range(PACK):
-            gather(1, 0, t)
+            gather("B3", t, plain=True)
+        open_x("B2", after="xC")
+        gate_x_gpsimd("B2", HALF, HALF + PAIR)
         quantize_w1(2)
-        quantize_x(0, 1)
         scalar_w1(3)
-        load_w1(6, 0, after="w30")
-        load_w1(6, 1, after="w31")
-        round_x(1, 0, gpsimd_copy, after="x01_0")
+        load_w1(7, 1, after="w30")
+        quantize_x("B2")
+        open_batch("D2", HALF, HALF + PAIR, 1, after="gB2")
         for t in range(PACK):
-            gather(1, 1, t, plain=True)
+            gather("D2", t, plain=True)
+        open_x("B3", after="xB2")
+        gate_x_gpsimd("B3", HALF + PAIR, SLOTS)
+        quantize_w1(3)
         scalar_w1(4)
-        for e in range(4):
-            round_w2(e, e + 1, gpsimd_copy, "r0")
-        load_w1(7, 0, after="w40")
-        open_h(0, 2, after="w41")
+        load_w2(after="w41")
+        round_w1(5, 0, scalar, "r0")
+        open_h(0, 2, after="w50")
         hidden(0)
         hidden(1)
-        quantize_w1(3)
-        gate_x(1, 1, nc.vector, "p01", 0, PAIR, PAIR)
-        quantize_x(1, 0)
-        gate_x(1, 1, nc.vector, "p02", PAIR, HALF, PAIR)
-        quantize_w1(4)
-        quantize_x(1, 1, 0, PAIR)
-        quantize_x(1, 1, PAIR, HALF)
-        scalar_w1(5, "r1")
-        load_w1(7, 1, after="g10")
-        round_w2(4, E, scalar)
-        scalar_w1(6, "r2")
-        open_h(2, 4, after="w60")
+        nc.sync.dma_start(pos1_sb[:], pos1)
+        nc.sync.dma_start(pos2_sb[:], pos2)
+        quantize_x("B3")
+        open_batch("D3", HALF + PAIR, SLOTS, 1, after="gB3")
+        for t in range(PACK):
+            gather("D3", t, plain=True)
+        open_x("D2", after="xB3")
+        gate_x_gpsimd("D2", HALF, HALF + PAIR)
+        round_w1(5, 1, scalar)
+        scalar_w1(6, "r1")
+        open_h(2, 4, after="w61")
         hidden(2)
         hidden(3)
-        scalar_w1(7, "r3")
+        scalar_w1(7, "r2")
+        quantize_x("D2")
+        quantize_w1(4)
         quantize_w1(5)
+        open_x("D3", after="r5")
+        gate_x_vector("D3", HALF + PAIR, SLOTS)
+        quantize_x("D3")
         quantize_w1(6)
-        open_h(4, 5, after="w70")
-        hidden(4)
-        open_h(5, 8, after="w71")
-        hidden(5)
-        hidden(6)
-        quantize_w1(7, 0, H)
-        first_layer(7, [0])
-        quantize_h(0, 2, "r5")
-        quantize_w1(7, H, 2 * H)
-        first_layer(7, [1])
-        quantize_w2("r7")
-        quantize_h(2, 4, "r6")
-        quantize_h(4, 5)
+        quantize_w1(7)
+        round_w2(0, E, scalar, "r3")
+        open_h(4, 8, after="w2")
+        for e in range(4, 8):
+            hidden(e)
+        open_h_codes(0, 4, after="r7")
+        quantize_h(0, 2)
+        quantize_h(2, 4)
+        quantize_w2("p01")
+        open_h_codes(4, 8, after="p02")
+        quantize_h(4, 6)
+        quantize_h(6, 8)
         second_layer((0, 1))
         second_layer((2, 3))
-        relu(7, share=True)
-        quantize_h(5, 7)
-        copy_y((0, 1), scalar, after="w61")
-        copy_y((2, 3), scalar)
-        quantize_h(7, 8)
         second_layer((4, 5))
         second_layer((6, 7))
-        copy_y((4, 5), vector)
-        copy_y((6, 7), scalar)
+        copy_y((0, 1), scalar, after="w71")
+        copy_y((2, 3), scalar)
+        copy_y((4, 5), scalar)
+        copy_y((6, 7), vector)
 
-        first = staged("first", [P, T], F32, "w50")
-        nc.vector.tensor_copy(first[:], y_sb[0][:].indirect(pos1_sb[:]))
-        for t0, t1, after in ((0, T - LAST_STORE, "w51"), (T - LAST_STORE, T, "x10_0")):
+        pieces = ((0, T - LAST_STORE, "w60"), (T - LAST_STORE, T, "xD2"))
+        first = staged("first", [P, T], F32, "w51")
+        for t0, t1, after in pieces:
+            nc.vector.tensor_copy(first[:, t0:t1], y_sb[0][:].indirect(pos1_sb[:, t0 // ENTRIES:t1 // ENTRIES]))
+        for t0, t1, after in pieces:
             both = staged("both%d" % t0, [P, t1 - t0], F32, after)
             nc.vector.tensor_tensor(both[:], y_sb[0][:].indirect(pos2_sb[:, t0 // ENTRIES:t1 // ENTRIES]),
                                     first[:, t0:t1], ADD)

@@ -32,7 +32,6 @@ MX_ALIGN = 64
 FLOPS = 2 * SLOTS * (K * H + H * N)
 BYTES = 4 * (K * T + E * K * H + E * H * N + SLOTS + N * T) + 2 * P * (SLOTS + 2 * T) // ENTRIES
 
-X_CODE_BUFS = 3
 W1_CODE_BUFS = 4
 BANKS = 8
 
@@ -135,13 +134,12 @@ def tile_moe_pre_mlp_relu_kernel(tc, xT, w1, w2, gate, offs, pos1, pos2, out):
             nc.gpsimd.tensor_scalar(dst.rearrange("p c t i -> p c i t"), src.rearrange("p c t i -> p c i t"),
                                     1.0, 0.0, MULT, ADD)
 
-        def quantize_x(name, a=None, b=None):
+        def quantize_x(name, after=None):
             tile, s0, s1, g = gathered[name]
-            a, b = (s0, s1) if a is None else (a, b)
-            half = s0 // HALF
-            if (half, g) not in x_mx:
-                x_mx[half, g] = mx_tiles(HALF, "x", X_CODE_BUFS)
-            quantize(x_mx[half, g], a % HALF, a % HALF + b - a, x_bf[name][:, (a - s0) * PACK:(b - s0) * PACK])
+            mx = mx_tiles(s1 - s0, "x" + name, 1, after)
+            quantize(mx, 0, s1 - s0, x_bf[name][:])
+            for e in range(s0 // C, s1 // C):
+                x_mx[e, g] = (mx, e * C - s0)
 
         def round_w1(e, g, copy, after=None):
             if e not in w1_bf:
@@ -177,9 +175,9 @@ def tile_moe_pre_mlp_relu_kernel(tc, xT, w1, w2, gate, offs, pos1, pos2, out):
                 a_banks[e] = [psum.tile([P, PACK, BANK], F32, name="a_bank", tag="bank", bufs=BANKS) for b in range(C // BANK)]
             w_codes, w_scales = w1_mx[e]
             for b, bank in enumerate(a_banks[e]):
-                s0 = (e * C) % HALF + b * BANK
                 for g in passes:
-                    x_codes, x_scales = x_mx[e * C // HALF, g]
+                    (x_codes, x_scales), s0 = x_mx[e, g]
+                    s0 += b * BANK
                     for t in range(PACK):
                         c0 = g * H + t * P
                         nc.tensor.matmul_mx(out=bank[:, t, :],
@@ -239,8 +237,8 @@ def tile_moe_pre_mlp_relu_kernel(tc, xT, w1, w2, gate, offs, pos1, pos2, out):
         scalar, vector = nc.scalar.copy, nc.vector.tensor_copy
         nc.sync.dma_start(offs_sb[:], offs)
         load_plane(0, 0)
-        load_gate(0, PAIR)
-        load_gate(PAIR, HALF)
+        load_gate(0, C)
+        load_gate(C, HALF)
         load_plane(0, 1)
         load_w1(0, 0)
         load_plane(0, 2)
@@ -259,8 +257,8 @@ def tile_moe_pre_mlp_relu_kernel(tc, xT, w1, w2, gate, offs, pos1, pos2, out):
         load_gate(HALF, SLOTS)
 
         open_batch("A", 0, HALF, 0)
-        gather("A", 0, 0, PAIR)
-        gather("A", 0, PAIR, HALF)
+        gather("A", 0, 0, C)
+        gather("A", 0, C, HALF)
         for t in range(1, PACK):
             gather("A", t)
         scalar_w1(0)
@@ -306,10 +304,6 @@ def tile_moe_pre_mlp_relu_kernel(tc, xT, w1, w2, gate, offs, pos1, pos2, out):
         quantize_w1(3)
         scalar_w1(4)
         load_w2(after="w41")
-        round_w1(5, 0, scalar, "r0")
-        open_h(0, 2, after="w50")
-        hidden(0)
-        hidden(1)
         nc.sync.dma_start(pos1_sb[:], pos1)
         nc.sync.dma_start(pos2_sb[:], pos2)
         quantize_x("B3")
@@ -318,27 +312,26 @@ def tile_moe_pre_mlp_relu_kernel(tc, xT, w1, w2, gate, offs, pos1, pos2, out):
             gather("D3", t, plain=True)
         open_x("D2", after="xB3")
         gate_x_gpsimd("D2", HALF, HALF + PAIR)
-        round_w1(5, 1, scalar)
+        scalar_w1(5, "r0")
+        open_h(0, 4, after="w51")
+        for e in range(4):
+            hidden(e)
         scalar_w1(6, "r1")
-        open_h(2, 4, after="w61")
-        hidden(2)
-        hidden(3)
         scalar_w1(7, "r2")
         quantize_x("D2")
         quantize_w1(4)
         quantize_w1(5)
-        open_x("D3", after="r5")
+        open_x("D3", after="w60")
         gate_x_vector("D3", HALF + PAIR, SLOTS)
-        quantize_x("D3")
         quantize_w1(6)
+        quantize_x("D3", after="w61")
         quantize_w1(7)
         round_w2(0, E, scalar, "r3")
         open_h(4, 8, after="w2")
         for e in range(4, 8):
             hidden(e)
-        open_h_codes(0, 4, after="r7")
-        quantize_h(0, 2)
-        quantize_h(2, 4)
+        open_h_codes(0, 4, after="w71")
+        quantize_h(0, 4)
         quantize_w2("p01")
         open_h_codes(4, 8, after="p02")
         quantize_h(4, 6)
@@ -347,13 +340,13 @@ def tile_moe_pre_mlp_relu_kernel(tc, xT, w1, w2, gate, offs, pos1, pos2, out):
         second_layer((2, 3))
         second_layer((4, 5))
         second_layer((6, 7))
-        copy_y((0, 1), scalar, after="w71")
+        copy_y((0, 1), scalar, after="w70")
         copy_y((2, 3), scalar)
         copy_y((4, 5), scalar)
         copy_y((6, 7), vector)
 
-        pieces = ((0, T - LAST_STORE, "w60"), (T - LAST_STORE, T, "xD2"))
-        first = staged("first", [P, T], F32, "w51")
+        pieces = ((0, T - LAST_STORE, "r6"), (T - LAST_STORE, T, "xD2"))
+        first = staged("first", [P, T], F32, "w50")
         for t0, t1, after in pieces:
             nc.vector.tensor_copy(first[:, t0:t1], y_sb[0][:].indirect(pos1_sb[:, t0 // ENTRIES:t1 // ENTRIES]))
         for t0, t1, after in pieces:

@@ -1,6 +1,7 @@
 from contextlib import ExitStack
 
 import concourse.mybir as mybir
+from concourse.masks import make_identity
 
 K, T, E, C, H, N = 1024, 1024, 8, 256, 512, 128
 SLOTS = E * C
@@ -26,6 +27,7 @@ BANK = C // 2
 RUN = 2
 ENTRIES = 16
 SPARE = 16
+W2_GROUP = 4
 LAST_STORE = 256
 MX_ALIGN = 64
 
@@ -61,9 +63,12 @@ def tile_moe_pre_mlp_relu_kernel(tc, xT, w1, w2, gate, offs, pos1, pos2, out):
             place[key] = place.pop(after) if after else "stage_%s" % (key,)
             return ring.tile(shape, dtype, name="staged", tag=place[key], bufs=1, align_bytes=MX_ALIGN)
 
+        for g in reversed(range(PASSES)):
+            for t in reversed(range(PACK)):
+                planes[g, t] = staged("p%d%d" % (g, t), [P, T + SPARE], F32)
+                nc.gpsimd.memset(planes[g, t][:, T:], 0.0)
+
         def load_plane(g, t):
-            planes[g, t] = staged("p%d%d" % (g, t), [P, T + SPARE], F32)
-            nc.gpsimd.memset(planes[g, t][:, T:], 0.0)
             nc.sync.dma_start(planes[g, t][:, :T], x_rows[g, t])
 
         def load_gate(s0, s1):
@@ -72,15 +77,35 @@ def tile_moe_pre_mlp_relu_kernel(tc, xT, w1, w2, gate, offs, pos1, pos2, out):
                 gates[half] = staged("gate%d" % half, [P, HALF], F32)
             nc.sync.dma_start(gates[half][:, s0 - half * HALF:s1 - half * HALF], gate[0:P, s0:s1])
 
+        def spread_gate():
+            identity = keep.tile([P, P], F32, name="identity")
+            make_identity(nc, identity[:])
+            chunks = SLOTS // P
+            rows = keep.tile([P, P], F32, name="gate_rows")
+            nc.sync.dma_start(rows[:], gate[0:P // chunks, :].rearrange("r (c p) -> (r c) p", p=P))
+            turned = psum.tile([P, P], F32, name="turned", tag="bank", bufs=BANKS)
+            nc.tensor.transpose(turned[:], rows[:], identity[:])
+            by_slot = keep.tile([P, chunks], F32, name="gate_by_slot")
+            nc.scalar.copy(by_slot[:], turned[:, :chunks])
+            gates[1] = staged("gate1", [P, HALF], F32)
+            for pair in range(HALF // PAIR, SLOTS // PAIR):
+                bank = psum.tile([P, PAIR], F32, name="spread", tag="bank", bufs=BANKS)
+                for c in range(PAIR // P):
+                    column = pair * PAIR // P + c
+                    nc.tensor.transpose(bank[:, c * P:(c + 1) * P], by_slot[:, column:column + 1].to_broadcast([P, P]),
+                                        identity[:])
+                s0 = pair * PAIR % HALF
+                nc.scalar.copy(gates[pair * PAIR // HALF][:, s0:s0 + PAIR], bank[:])
+
         def load_w1(e, g, after=None):
             w1_raw[e, g] = staged("w%d%d" % (e, g), [P, PACK, H], F32, after)
             nc.sync.dma_start(w1_raw[e, g][:], w1_rows[e, g])
 
-        def load_w2(after):
-            w2_raw[0] = staged("w2", [P, E, PACK, N], F32, after)
+        def load_w2(group, after):
+            w2_raw[group] = staged("w2_%d" % group, [P, PACK, W2_GROUP, N], F32, after)
             for r in range(2):
                 for t in range(PACK):
-                    nc.sync.dma_start(w2_raw[0][r:P:2, :, t, :], w2_rows[r, t])
+                    nc.sync.dma_start(w2_raw[group][r:P:2, t], w2_rows[r, t][:, group * W2_GROUP:(group + 1) * W2_GROUP])
 
         def mx_tiles(width, name, bufs, after=None):
             if after:
@@ -96,6 +121,10 @@ def tile_moe_pre_mlp_relu_kernel(tc, xT, w1, w2, gate, offs, pos1, pos2, out):
 
         def open_batch(name, s0, s1, g, after=None):
             gathered[name] = (staged("g" + name, [P, PACK, s1 - s0], F32, after), s0, s1, g)
+
+        def part_of(batch, name, s0, s1):
+            tile, first_slot, last_slot, g = gathered[batch]
+            gathered[name] = (tile[:, :, s0 - first_slot:s1 - first_slot], s0, s1, g)
 
         def gather(name, t, a=None, b=None, plain=False):
             tile, s0, s1, g = gathered[name]
@@ -147,24 +176,21 @@ def tile_moe_pre_mlp_relu_kernel(tc, xT, w1, w2, gate, offs, pos1, pos2, out):
             copy(w1_bf[e][:, g * H * PACK:(g + 1) * H * PACK].rearrange("p (t u r j) -> p u t j r", t=PACK, r=2, j=PACK),
                  w1_raw[e, g][:].rearrange("p j (u t r) -> p u t j r", t=PACK, r=2))
 
-        def quantize_w1(e, c0=0, c1=PASSES * H):
+        def quantize_w1(e, after=None, c0=0, c1=PASSES * H):
             if e not in w1_mx:
-                w1_mx[e] = mx_tiles(PASSES * H, "w1", W1_CODE_BUFS)
+                w1_mx[e] = mx_tiles(PASSES * H, "w1", W1_CODE_BUFS, after)
             quantize(w1_mx[e], c0, c1, w1_bf[e][:, c0 * PACK:c1 * PACK])
 
         def scalar_w1(e, after=None):
             for g in range(PASSES):
                 round_w1(e, g, nc.scalar.copy, after)
 
-        def round_w2(e0, e1, copy, after=None):
+        def round_w2(group, copy, after=None):
             if 0 not in w2_bf:
                 w2_bf[0] = staged("rw2", [P, E * N * PACK], BF16, after)
-            dst = w2_bf[0][:, e0 * N * PACK:e1 * N * PACK].rearrange("p (e c i t) -> p e c t i", e=e1 - e0, i=RUN, t=PACK)
-            src = w2_raw[0][:, e0:e1].rearrange("p e t (c i) -> p e c t i", i=RUN)
-            if e1 - e0 == 1:
-                copy(dst[:, 0], src[:, 0])
-            else:
-                copy(dst, src)
+            width = W2_GROUP * N * PACK
+            copy(w2_bf[0][:, group * width:(group + 1) * width].rearrange("p (c i t) -> p c t i", i=RUN, t=PACK),
+                 w2_raw[group][:].rearrange("p t e (c i) -> p (e c) t i", i=RUN))
 
         def quantize_w2(after=None):
             w2_mx[0] = mx_tiles(E * N, "w2", 1, after)
@@ -238,40 +264,47 @@ def tile_moe_pre_mlp_relu_kernel(tc, xT, w1, w2, gate, offs, pos1, pos2, out):
         nc.sync.dma_start(offs_sb[:], offs)
         load_plane(0, 0)
         load_gate(0, C)
-        load_gate(C, HALF)
+        load_gate(C, PAIR)
         load_plane(0, 1)
-        load_w1(0, 0)
+        spread_gate()
         load_plane(0, 2)
         load_plane(0, 3)
+        load_gate(PAIR, HALF)
+        load_w1(0, 0)
         load_w1(0, 1)
         load_plane(1, 0)
-        load_w1(1, 0)
         load_plane(1, 1)
+        load_w1(1, 0)
         load_w1(1, 1)
         load_plane(1, 2)
         load_w1(2, 0)
         load_plane(1, 3)
         load_w1(2, 1)
         load_w1(3, 0)
-        load_w1(3, 1)
-        load_gate(HALF, SLOTS)
 
-        open_batch("A", 0, HALF, 0)
-        gather("A", 0, 0, C)
-        gather("A", 0, C, HALF)
+        open_batch("A0", 0, PAIR, 0)
+        open_batch("A1", PAIR, HALF, 0)
+        gather("A0", 0, 0, C)
+        gather("A0", 0, C, PAIR)
         for t in range(1, PACK):
-            gather("A", t)
+            gather("A0", t)
+        for t in range(PACK):
+            gather("A1", t)
+        open_x("A0")
+        round_x("A0", scalar, 0, PAIR)
+        load_w1(3, 1, after="gA0")
         scalar_w1(0)
         load_w1(4, 0, after="w00")
-        open_x("A", after="w01")
-        round_x("A", scalar, 0, HALF)
-        load_w1(4, 1, after="gA")
+        open_x("A1", after="w01")
+        round_x("A1", scalar, PAIR, HALF)
+        load_w1(4, 1, after="gA1")
         open_batch("C", 0, HALF, 1)
         gather("C", 0)
+        quantize_x("A0")
         quantize_w1(0)
         gather("C", 1)
-        quantize_x("A")
-        load_w1(5, 0, after="xA")
+        quantize_x("A1")
+        load_w1(5, 0, after="xA1")
         scalar_w1(1)
         load_w1(5, 1, after="w10")
         load_w1(6, 0, after="w11")
@@ -303,7 +336,8 @@ def tile_moe_pre_mlp_relu_kernel(tc, xT, w1, w2, gate, offs, pos1, pos2, out):
         gate_x_gpsimd("B3", HALF + PAIR, SLOTS)
         quantize_w1(3)
         scalar_w1(4)
-        load_w2(after="w41")
+        load_w2(0, after="w31")
+        load_w2(1, after="w40")
         nc.sync.dma_start(pos1_sb[:], pos1)
         nc.sync.dma_start(pos2_sb[:], pos2)
         quantize_x("B3")
@@ -313,21 +347,22 @@ def tile_moe_pre_mlp_relu_kernel(tc, xT, w1, w2, gate, offs, pos1, pos2, out):
         open_x("D2", after="xB3")
         gate_x_gpsimd("D2", HALF, HALF + PAIR)
         scalar_w1(5, "r0")
-        open_h(0, 4, after="w51")
+        scalar_w1(6, "r1")
+        open_h(0, 4, after="w61")
         for e in range(4):
             hidden(e)
-        scalar_w1(6, "r1")
         scalar_w1(7, "r2")
         quantize_x("D2")
         quantize_w1(4)
         quantize_w1(5)
-        open_x("D3", after="w60")
+        open_x("D3", after="w51")
         gate_x_vector("D3", HALF + PAIR, SLOTS)
         quantize_w1(6)
-        quantize_x("D3", after="w61")
+        quantize_x("D3", after="w70")
         quantize_w1(7)
-        round_w2(0, E, scalar, "r3")
-        open_h(4, 8, after="w2")
+        round_w2(0, scalar, "r3")
+        round_w2(1, scalar)
+        open_h(4, 8, after="w2_1")
         for e in range(4, 8):
             hidden(e)
         open_h_codes(0, 4, after="w71")
@@ -340,7 +375,7 @@ def tile_moe_pre_mlp_relu_kernel(tc, xT, w1, w2, gate, offs, pos1, pos2, out):
         second_layer((2, 3))
         second_layer((4, 5))
         second_layer((6, 7))
-        copy_y((0, 1), scalar, after="w70")
+        copy_y((0, 1), scalar, after="w60")
         copy_y((2, 3), scalar)
         copy_y((4, 5), scalar)
         copy_y((6, 7), vector)

@@ -27,6 +27,7 @@ BANK = C // 2
 RUN = 2
 ENTRIES = 16
 SPARE = 16
+LINE = 4
 W2_GROUP = 4
 LAST_STORE = 256
 MX_ALIGN = 64
@@ -80,22 +81,22 @@ def tile_moe_pre_mlp_relu_kernel(tc, xT, w1, w2, gate, offs, pos1, pos2, out):
         def spread_gate():
             identity = keep.tile([P, P], F32, name="identity")
             make_identity(nc, identity[:])
-            chunks = SLOTS // P
+            chunks = HALF // P
             rows = keep.tile([P, P], F32, name="gate_rows")
-            nc.sync.dma_start(rows[:], gate[0:P // chunks, :].rearrange("r (c p) -> (r c) p", p=P))
+            nc.vector.memset(rows[:], 0.0)
+            nc.sync.dma_start(rows[:chunks, :], gate[0, HALF:].rearrange("(c p) -> c p", p=P))
             turned = psum.tile([P, P], F32, name="turned", tag="bank", bufs=BANKS)
             nc.tensor.transpose(turned[:], rows[:], identity[:])
             by_slot = keep.tile([P, chunks], F32, name="gate_by_slot")
             nc.scalar.copy(by_slot[:], turned[:, :chunks])
             gates[1] = staged("gate1", [P, HALF], F32)
-            for pair in range(HALF // PAIR, SLOTS // PAIR):
+            for s0 in range(0, HALF, PAIR):
                 bank = psum.tile([P, PAIR], F32, name="spread", tag="bank", bufs=BANKS)
                 for c in range(PAIR // P):
-                    column = pair * PAIR // P + c
+                    column = s0 // P + c
                     nc.tensor.transpose(bank[:, c * P:(c + 1) * P], by_slot[:, column:column + 1].to_broadcast([P, P]),
                                         identity[:])
-                s0 = pair * PAIR % HALF
-                nc.scalar.copy(gates[pair * PAIR // HALF][:, s0:s0 + PAIR], bank[:])
+                nc.scalar.copy(gates[1][:, s0:s0 + PAIR], bank[:])
 
         def load_w1(e, g, after=None):
             w1_raw[e, g] = staged("w%d%d" % (e, g), [P, PACK, H], F32, after)
@@ -139,18 +140,18 @@ def tile_moe_pre_mlp_relu_kernel(tc, xT, w1, w2, gate, offs, pos1, pos2, out):
             tile, s0, s1, g = gathered[name]
             x_bf[name] = staged("x" + name, [P, (s1 - s0) * PACK], BF16, after)
 
-        def x_views(name, a, b):
+        def x_views(name, a, b, run=RUN):
             tile, s0, s1, g = gathered[name]
-            return (x_bf[name][:, (a - s0) * PACK:(b - s0) * PACK].rearrange("p (c i t) -> p c t i", i=RUN, t=PACK),
-                    tile[:, :, a - s0:b - s0].rearrange("p t (c i) -> p c t i", i=RUN))
+            return (x_bf[name][:, (a - s0) * PACK:(b - s0) * PACK].rearrange("p (c i t) -> p c t i", i=run, t=PACK),
+                    tile[:, :, a - s0:b - s0].rearrange("p t (c i) -> p c t i", i=run))
 
         def round_x(name, copy, a, b):
             copy(*x_views(name, a, b))
 
         def gate_x_vector(name, a, b):
-            dst, src = x_views(name, a, b)
-            weights = gates[a // HALF][:, a % HALF:a % HALF + b - a].rearrange("p (c i) -> p c i", i=RUN)
-            nc.vector.tensor_tensor(dst, src, weights.unsqueeze(2).to_broadcast([P, (b - a) // RUN, PACK, RUN]), MULT)
+            dst, src = x_views(name, a, b, LINE)
+            weights = gates[a // HALF][:, a % HALF:a % HALF + b - a].rearrange("p (c i) -> p c i", i=LINE)
+            nc.vector.tensor_tensor(dst, src, weights.unsqueeze(2).to_broadcast([P, (b - a) // LINE, PACK, LINE]), MULT)
 
         def gate_x_gpsimd(name, a, b):
             tile, s0, s1, g = gathered[name]
@@ -265,8 +266,8 @@ def tile_moe_pre_mlp_relu_kernel(tc, xT, w1, w2, gate, offs, pos1, pos2, out):
         load_plane(0, 0)
         load_gate(0, C)
         load_gate(C, PAIR)
-        load_plane(0, 1)
         spread_gate()
+        load_plane(0, 1)
         load_plane(0, 2)
         load_plane(0, 3)
         load_gate(PAIR, HALF)

@@ -14,20 +14,18 @@ U8 = mybir.dt.uint8
 FP8X4 = mybir.dt.float8_e4m3fn_x4
 MULT = mybir.AluOpType.mult
 ADD = mybir.AluOpType.add
-MAX = mybir.AluOpType.max
 RELU = mybir.ActivationFunctionType.Relu
 
 P = 128
 PACK = 4
 PASSES = K // (P * PACK)
 PAIR = 2 * C
-HALVES = 2
-HALF = SLOTS // HALVES
+HALF = SLOTS // 2
 BANK = C // 2
 RUN = 2
+LINE = 4
 ENTRIES = 16
 SPARE = 16
-LINE = 4
 W2_GROUP = 4
 LAST_STORE = 256
 MX_ALIGN = 64
@@ -36,7 +34,6 @@ FLOPS = 2 * SLOTS * (K * H + H * N)
 BYTES = 4 * (K * T + E * K * H + E * H * N + SLOTS + N * T) + 2 * P * (SLOTS + 2 * T) // ENTRIES
 
 W1_CODE_BUFS = 4
-BANKS = 8
 
 
 def tile_moe_pre_mlp_relu_kernel(tc, xT, w1, w2, gate, offs, pos1, pos2, out):
@@ -54,15 +51,21 @@ def tile_moe_pre_mlp_relu_kernel(tc, xT, w1, w2, gate, offs, pos1, pos2, out):
         w1_rows = w1.rearrange("e (g p j) c -> e g p j c", g=PASSES, j=PACK)
         w2_rows = w2.rearrange("e (u t r) n -> r t u e n", t=PACK, r=2)
 
-        planes, gates, w1_raw, w2_raw, gathered = {}, {}, {}, {}, {}
-        x_bf, w1_bf, w2_bf, h_bf = {}, {}, {}, {}
-        x_mx, w1_mx, w2_mx, h_mx, a_banks, y_banks, y_sb = {}, {}, {}, {}, {}, {}, {}
-
+        planes, gates, w1_raw, w2_raw, batches = {}, {}, {}, {}, {}
+        x_bf, w1_bf, h_bf = {}, {}, {}
+        x_mx, w1_mx, h_mx, y_banks = {}, {}, {}, {}
         place = {}
 
         def staged(key, shape, dtype, after=None):
-            place[key] = place.pop(after) if after else "stage_%s" % (key,)
+            place[key] = place.pop(after) if after else "stage_" + key
             return ring.tile(shape, dtype, name="staged", tag=place[key], bufs=1, align_bytes=MX_ALIGN)
+
+        def in_bank(key, shape, after=None):
+            place[key] = place.pop(after) if after else "bank_" + key
+            return psum.tile(shape, F32, name="bank", tag=place[key], bufs=1)
+
+        earlier = {(e, b): "a%d%d" % (e - 4, b) for e in range(4, E) for b in range(C // BANK)}
+        earlier.update({(2, 1): "turned", (3, 0): "spread0", (3, 1): "spread1"})
 
         for g in reversed(range(PASSES)):
             for t in reversed(range(PACK)):
@@ -85,13 +88,13 @@ def tile_moe_pre_mlp_relu_kernel(tc, xT, w1, w2, gate, offs, pos1, pos2, out):
             rows = keep.tile([P, P], F32, name="gate_rows")
             nc.vector.memset(rows[:], 0.0)
             nc.sync.dma_start(rows[:chunks, :], gate[0, HALF:].rearrange("(c p) -> c p", p=P))
-            turned = psum.tile([P, P], F32, name="turned", tag="bank", bufs=BANKS)
+            turned = in_bank("turned", [P, P])
             nc.tensor.transpose(turned[:], rows[:], identity[:])
             by_slot = keep.tile([P, chunks], F32, name="gate_by_slot")
             nc.scalar.copy(by_slot[:], turned[:, :chunks])
             gates[1] = staged("gate1", [P, HALF], F32)
             for s0 in range(0, HALF, PAIR):
-                bank = psum.tile([P, PAIR], F32, name="spread", tag="bank", bufs=BANKS)
+                bank = in_bank("spread%d" % (s0 // PAIR), [P, PAIR])
                 for c in range(PAIR // P):
                     column = s0 // P + c
                     nc.tensor.transpose(bank[:, c * P:(c + 1) * P], by_slot[:, column:column + 1].to_broadcast([P, P]),
@@ -106,11 +109,12 @@ def tile_moe_pre_mlp_relu_kernel(tc, xT, w1, w2, gate, offs, pos1, pos2, out):
             w2_raw[group] = staged("w2_%d" % group, [P, PACK, W2_GROUP, N], F32, after)
             for r in range(2):
                 for t in range(PACK):
-                    nc.sync.dma_start(w2_raw[group][r:P:2, t], w2_rows[r, t][:, group * W2_GROUP:(group + 1) * W2_GROUP])
+                    nc.sync.dma_start(w2_raw[group][r:P:2, t],
+                                      w2_rows[r, t][:, group * W2_GROUP:(group + 1) * W2_GROUP])
 
-        def mx_tiles(width, name, bufs, after=None):
+        def mx_tiles(width, name, bufs=1, after=None):
             if after:
-                codes = staged(name + "_codes_" + after, [P, width], U32, after)
+                codes = staged(name + "_codes", [P, width], U32, after)
             else:
                 codes = ring.tile([P, width], U32, name=name + "_codes", bufs=bufs, align_bytes=MX_ALIGN)
             scales = ring.tile([P, width], U8, name=name + "_scales", bufs=bufs, align_bytes=MX_ALIGN)
@@ -121,155 +125,125 @@ def tile_moe_pre_mlp_relu_kernel(tc, xT, w1, w2, gate, offs, pos1, pos2, out):
             nc.vector.quantize_mx(out=codes[:, c0:c1].bitcast(FP8X4), scales=scales[:, c0:c1], in_=src)
 
         def open_batch(name, s0, s1, g, after=None):
-            gathered[name] = (staged("g" + name, [P, PACK, s1 - s0], F32, after), s0, s1, g)
+            batches[name] = (staged("g" + name, [P, PACK, s1 - s0], F32, after), s0, s1, g)
 
-        def part_of(batch, name, s0, s1):
-            tile, first_slot, last_slot, g = gathered[batch]
-            gathered[name] = (tile[:, :, s0 - first_slot:s1 - first_slot], s0, s1, g)
+        def gate_of(s0, s1):
+            return gates[s0 // HALF][:, s0 % HALF:s0 % HALF + s1 - s0]
 
-        def gather(name, t, a=None, b=None, plain=False):
-            tile, s0, s1, g = gathered[name]
-            a, b = (s0, s1) if a is None else (a, b)
-            picked = planes[g, t][:].indirect(offs_sb[:, a // ENTRIES:b // ENTRIES])
-            if plain:
-                nc.vector.tensor_copy(tile[:, t, a - s0:b - s0], picked)
-            else:
-                nc.vector.tensor_tensor(tile[:, t, a - s0:b - s0], picked, gates[a // HALF][:, a % HALF:a % HALF + b - a], MULT)
+        def picked(g, t, s0, s1):
+            return planes[g, t][:].indirect(offs_sb[:, s0 // ENTRIES:s1 // ENTRIES])
 
-        def open_x(name, after=None):
-            tile, s0, s1, g = gathered[name]
+        def gather_gated(name, t, part=None):
+            tile, s0, s1, g = batches[name]
+            a, b = part or (s0, s1)
+            nc.vector.tensor_tensor(tile[:, t, a - s0:b - s0], picked(g, t, a, b), gate_of(a, b), MULT)
+
+        def gather_plain(name):
+            tile, s0, s1, g = batches[name]
+            for t in range(PACK):
+                nc.vector.tensor_copy(tile[:, t, :], picked(g, t, s0, s1))
+
+        def open_x(name, run, after):
+            tile, s0, s1, g = batches[name]
             x_bf[name] = staged("x" + name, [P, (s1 - s0) * PACK], BF16, after)
+            return (x_bf[name][:].rearrange("p (c i t) -> p c t i", i=run, t=PACK),
+                    tile[:].rearrange("p t (c i) -> p c t i", i=run))
 
-        def x_views(name, a, b, run=RUN):
-            tile, s0, s1, g = gathered[name]
-            return (x_bf[name][:, (a - s0) * PACK:(b - s0) * PACK].rearrange("p (c i t) -> p c t i", i=run, t=PACK),
-                    tile[:, :, a - s0:b - s0].rearrange("p t (c i) -> p c t i", i=run))
+        def round_x_scalar(name, after=None):
+            nc.scalar.copy(*open_x(name, RUN, after))
 
-        def round_x(name, copy, a, b):
-            copy(*x_views(name, a, b))
-
-        def gate_x_vector(name, a, b):
-            dst, src = x_views(name, a, b, LINE)
-            weights = gates[a // HALF][:, a % HALF:a % HALF + b - a].rearrange("p (c i) -> p c i", i=LINE)
-            nc.vector.tensor_tensor(dst, src, weights.unsqueeze(2).to_broadcast([P, (b - a) // LINE, PACK, LINE]), MULT)
-
-        def gate_x_gpsimd(name, a, b):
-            tile, s0, s1, g = gathered[name]
-            weights = gates[a // HALF][:, a % HALF:a % HALF + b - a]
-            nc.gpsimd.tensor_tensor(x_bf[name][:, (a - s0) * PACK:(b - s0) * PACK].rearrange("p (s t) -> p s t", t=PACK),
-                                    tile[:, :, a - s0:b - s0].rearrange("p t s -> p s t"),
-                                    weights.unsqueeze(2).to_broadcast([P, b - a, PACK]), MULT)
-
-        def gpsimd_copy(dst, src):
+        def round_x_gpsimd(name):
+            dst, src = open_x(name, RUN, None)
             nc.gpsimd.tensor_scalar(dst.rearrange("p c t i -> p c i t"), src.rearrange("p c t i -> p c i t"),
                                     1.0, 0.0, MULT, ADD)
 
+        def gate_x_gpsimd(name, after):
+            tile, s0, s1, g = batches[name]
+            x_bf[name] = staged("x" + name, [P, (s1 - s0) * PACK], BF16, after)
+            nc.gpsimd.tensor_tensor(x_bf[name][:].rearrange("p (s t) -> p s t", t=PACK),
+                                    tile[:].rearrange("p t s -> p s t"),
+                                    gate_of(s0, s1).unsqueeze(2).to_broadcast([P, s1 - s0, PACK]), MULT)
+
+        def gate_x_vector(name, after):
+            tile, s0, s1, g = batches[name]
+            dst, src = open_x(name, LINE, after)
+            weights = gate_of(s0, s1).rearrange("p (c i) -> p c i", i=LINE)
+            nc.vector.tensor_tensor(dst, src, weights.unsqueeze(2).to_broadcast([P, (s1 - s0) // LINE, PACK, LINE]),
+                                    MULT)
+
         def quantize_x(name, after=None):
-            tile, s0, s1, g = gathered[name]
-            mx = mx_tiles(s1 - s0, "x" + name, 1, after)
+            tile, s0, s1, g = batches[name]
+            mx = mx_tiles(s1 - s0, "x" + name, after=after)
             quantize(mx, 0, s1 - s0, x_bf[name][:])
             for e in range(s0 // C, s1 // C):
                 x_mx[e, g] = (mx, e * C - s0)
 
-        def round_w1(e, g, copy, after=None):
-            if e not in w1_bf:
-                w1_bf[e] = staged("r%d" % e, [P, PASSES * H * PACK], BF16, after)
-            copy(w1_bf[e][:, g * H * PACK:(g + 1) * H * PACK].rearrange("p (t u r j) -> p u t j r", t=PACK, r=2, j=PACK),
-                 w1_raw[e, g][:].rearrange("p j (u t r) -> p u t j r", t=PACK, r=2))
-
-        def quantize_w1(e, after=None, c0=0, c1=PASSES * H):
-            if e not in w1_mx:
-                w1_mx[e] = mx_tiles(PASSES * H, "w1", W1_CODE_BUFS, after)
-            quantize(w1_mx[e], c0, c1, w1_bf[e][:, c0 * PACK:c1 * PACK])
-
-        def scalar_w1(e, after=None):
+        def round_w1(e, after=None):
+            w1_bf[e] = staged("r%d" % e, [P, PASSES, H * PACK], BF16, after)
             for g in range(PASSES):
-                round_w1(e, g, nc.scalar.copy, after)
+                nc.scalar.copy(w1_bf[e][:, g].rearrange("p (t u r j) -> p u t j r", t=PACK, r=2, j=PACK),
+                               w1_raw[e, g][:].rearrange("p j (u t r) -> p u t j r", t=PACK, r=2))
 
-        def round_w2(group, copy, after=None):
-            if 0 not in w2_bf:
-                w2_bf[0] = staged("rw2", [P, E * N * PACK], BF16, after)
-            width = W2_GROUP * N * PACK
-            copy(w2_bf[0][:, group * width:(group + 1) * width].rearrange("p (c i t) -> p c t i", i=RUN, t=PACK),
-                 w2_raw[group][:].rearrange("p t e (c i) -> p (e c) t i", i=RUN))
+        def quantize_w1(e):
+            w1_mx[e] = mx_tiles(PASSES * H, "w1", W1_CODE_BUFS)
+            quantize(w1_mx[e], 0, PASSES * H, w1_bf[e][:].rearrange("p g c -> p (g c)"))
 
-        def quantize_w2(after=None):
-            w2_mx[0] = mx_tiles(E * N, "w2", 1, after)
-            quantize(w2_mx[0], 0, E * N, w2_bf[0][:])
+        def round_w2(after):
+            w2_bf = staged("rw2", [P, E // W2_GROUP, W2_GROUP * N * PACK], BF16, after)
+            for group in range(E // W2_GROUP):
+                nc.scalar.copy(w2_bf[:, group].rearrange("p (c i t) -> p c t i", i=RUN, t=PACK),
+                               w2_raw[group][:].rearrange("p t e (c i) -> p (e c) t i", i=RUN))
+            return w2_bf
 
-        def first_layer(e, passes=range(PASSES)):
-            if e not in a_banks:
-                a_banks[e] = [psum.tile([P, PACK, BANK], F32, name="a_bank", tag="bank", bufs=BANKS) for b in range(C // BANK)]
-            w_codes, w_scales = w1_mx[e]
-            for b, bank in enumerate(a_banks[e]):
-                for g in passes:
-                    (x_codes, x_scales), s0 = x_mx[e, g]
-                    s0 += b * BANK
-                    for t in range(PACK):
-                        c0 = g * H + t * P
-                        nc.tensor.matmul_mx(out=bank[:, t, :],
-                                            lhsT=w_codes[:, c0:c0 + P].bitcast(FP8X4),
-                                            lhsT_scale=w_scales[:, c0:c0 + P],
-                                            rhs=x_codes[:, s0:s0 + BANK].bitcast(FP8X4),
-                                            rhs_scale=x_scales[:, s0:s0 + BANK],
-                                            start=(g == 0 and t == 0), stop=(g == PASSES - 1 and t == PACK - 1))
-
-        def open_h(e0, e1, after):
-            tile = staged("h%d" % e0, [P, (e1 - e0) * C * PACK], BF16, after)
+        def hidden(e0, e1, after):
+            h_bf[e0] = staged("h%d" % e0, [P, (e1 - e0) * C * PACK], BF16, after)
             for e in range(e0, e1):
-                h_bf[e] = (tile, (e - e0) * C * PACK)
+                banks = [in_bank("a%d%d" % (e, b), [P, PACK, BANK], earlier.get((e, b))) for b in range(C // BANK)]
+                w_codes, w_scales = w1_mx[e]
+                for b, bank in enumerate(banks):
+                    for g in range(PASSES):
+                        (x_codes, x_scales), s0 = x_mx[e, g]
+                        s0 += b * BANK
+                        for t in range(PACK):
+                            c0 = g * H + t * P
+                            nc.tensor.matmul_mx(out=bank[:, t, :],
+                                                lhsT=w_codes[:, c0:c0 + P].bitcast(FP8X4),
+                                                lhsT_scale=w_scales[:, c0:c0 + P],
+                                                rhs=x_codes[:, s0:s0 + BANK].bitcast(FP8X4),
+                                                rhs_scale=x_scales[:, s0:s0 + BANK],
+                                                start=(g == 0 and t == 0),
+                                                stop=(g == PASSES - 1 and t == PACK - 1))
+                for b, bank in enumerate(banks):
+                    c0 = ((e - e0) * C + b * BANK) * PACK
+                    nc.scalar.activation(h_bf[e0][:, c0:c0 + BANK * PACK].rearrange("p (s t) -> p s t", t=PACK),
+                                         bank[:].rearrange("p t s -> p s t"), RELU)
 
-        def relu(e, share=False):
-            tile, first_column = h_bf[e]
-            for b, bank in enumerate(a_banks[e]):
-                c0 = first_column + b * BANK * PACK
-                dst = tile[:, c0:c0 + BANK * PACK].rearrange("p (s t) -> p s t", t=PACK)
-                src = bank[:].rearrange("p t s -> p s t")
-                if share and b == 1:
-                    nc.vector.tensor_scalar(dst, src, 0.0, None, MAX)
-                else:
-                    nc.scalar.activation(dst, src, RELU)
-
-        def hidden(e):
-            first_layer(e)
-            relu(e)
-
-        def open_h_codes(e0, e1, after=None):
-            mx = mx_tiles((e1 - e0) * C, "h%d" % e0, 1, after)
+        def quantize_h(e0, e1, pieces, after):
+            mx = mx_tiles((e1 - e0) * C, "h%d" % e0, after=after)
+            width = (e1 - e0) * C // pieces
+            for c0 in range(0, (e1 - e0) * C, width):
+                quantize(mx, c0, c0 + width, h_bf[e0][:, c0 * PACK:(c0 + width) * PACK])
             for e in range(e0, e1):
                 h_mx[e] = (mx, (e - e0) * C)
 
-        def quantize_h(e0, e1):
-            tile, c0 = h_bf[e0]
-            mx, s0 = h_mx[e0]
-            quantize(mx, s0, s0 + (e1 - e0) * C, tile[:, c0:c0 + (e1 - e0) * C * PACK])
-
-        def second_layer(experts):
-            bank = psum.tile([P, len(experts) * C], F32, name="y_bank", tag="bank", bufs=BANKS)
-            y_banks[experts] = bank
-            w_codes, w_scales = w2_mx[0]
-            for place, e in enumerate(experts):
+        def second_layer(e0, e1, after):
+            y_banks[e0] = in_bank("y%d" % e0, [P, (e1 - e0) * C], after)
+            w_codes, w_scales = w2_mx
+            for e in range(e0, e1):
                 (h_codes, h_scales), s0 = h_mx[e]
-                nc.tensor.matmul_mx(out=bank[:, place * C:(place + 1) * C],
+                nc.tensor.matmul_mx(out=y_banks[e0][:, (e - e0) * C:(e - e0 + 1) * C],
                                     lhsT=w_codes[:, e * N:(e + 1) * N].bitcast(FP8X4),
                                     lhsT_scale=w_scales[:, e * N:(e + 1) * N],
                                     rhs=h_codes[:, s0:s0 + C].bitcast(FP8X4), rhs_scale=h_scales[:, s0:s0 + C],
                                     start=True, stop=True)
 
-        def copy_y(experts, copy, after=None):
-            if 0 not in y_sb:
-                y_sb[0] = staged("y", [P, SLOTS], F32, after)
-            copy(y_sb[0][:, experts[0] * C:(experts[-1] + 1) * C], y_banks[experts][:])
-
-        scalar, vector = nc.scalar.copy, nc.vector.tensor_copy
         nc.sync.dma_start(offs_sb[:], offs)
         load_plane(0, 0)
         load_gate(0, C)
         load_gate(C, PAIR)
         spread_gate()
-        load_plane(0, 1)
-        load_plane(0, 2)
-        load_plane(0, 3)
+        for t in range(1, PACK):
+            load_plane(0, t)
         load_gate(PAIR, HALF)
         load_w1(0, 0)
         load_w1(0, 1)
@@ -285,108 +259,94 @@ def tile_moe_pre_mlp_relu_kernel(tc, xT, w1, w2, gate, offs, pos1, pos2, out):
 
         open_batch("A0", 0, PAIR, 0)
         open_batch("A1", PAIR, HALF, 0)
-        gather("A0", 0, 0, C)
-        gather("A0", 0, C, PAIR)
+        gather_gated("A0", 0, (0, C))
+        gather_gated("A0", 0, (C, PAIR))
         for t in range(1, PACK):
-            gather("A0", t)
+            gather_gated("A0", t)
         for t in range(PACK):
-            gather("A1", t)
-        open_x("A0")
-        round_x("A0", scalar, 0, PAIR)
+            gather_gated("A1", t)
+        round_x_scalar("A0")
         load_w1(3, 1, after="gA0")
-        scalar_w1(0)
+        round_w1(0)
         load_w1(4, 0, after="w00")
-        open_x("A1", after="w01")
-        round_x("A1", scalar, PAIR, HALF)
+        round_x_scalar("A1", after="w01")
         load_w1(4, 1, after="gA1")
         open_batch("C", 0, HALF, 1)
-        gather("C", 0)
+        gather_gated("C", 0)
         quantize_x("A0")
         quantize_w1(0)
-        gather("C", 1)
+        gather_gated("C", 1)
         quantize_x("A1")
         load_w1(5, 0, after="xA1")
-        scalar_w1(1)
+        round_w1(1)
         load_w1(5, 1, after="w10")
         load_w1(6, 0, after="w11")
-        gather("C", 2)
+        gather_gated("C", 2)
         quantize_w1(1)
-        gather("C", 3)
+        gather_gated("C", 3)
+
         open_batch("B2", HALF, HALF + PAIR, 0, after="gate0")
-        for t in range(PACK):
-            gather("B2", t, plain=True)
-        open_x("C")
-        round_x("C", gpsimd_copy, 0, HALF)
-        scalar_w1(2)
+        gather_plain("B2")
+        round_x_gpsimd("C")
+        round_w1(2)
         load_w1(6, 1, after="w20")
         load_w1(7, 0, after="w21")
+
         quantize_x("C")
         open_batch("B3", HALF + PAIR, SLOTS, 0, after="gC")
-        for t in range(PACK):
-            gather("B3", t, plain=True)
-        open_x("B2", after="xC")
-        gate_x_gpsimd("B2", HALF, HALF + PAIR)
+        gather_plain("B3")
+        gate_x_gpsimd("B2", after="xC")
         quantize_w1(2)
-        scalar_w1(3)
+        round_w1(3)
         load_w1(7, 1, after="w30")
+
         quantize_x("B2")
         open_batch("D2", HALF, HALF + PAIR, 1, after="gB2")
-        for t in range(PACK):
-            gather("D2", t, plain=True)
-        open_x("B3", after="xB2")
-        gate_x_gpsimd("B3", HALF + PAIR, SLOTS)
+        gather_plain("D2")
+        gate_x_gpsimd("B3", after="xB2")
         quantize_w1(3)
-        scalar_w1(4)
+        round_w1(4)
         load_w2(0, after="w31")
         load_w2(1, after="w40")
         nc.sync.dma_start(pos1_sb[:], pos1)
         nc.sync.dma_start(pos2_sb[:], pos2)
+
         quantize_x("B3")
         open_batch("D3", HALF + PAIR, SLOTS, 1, after="gB3")
-        for t in range(PACK):
-            gather("D3", t, plain=True)
-        open_x("D2", after="xB3")
-        gate_x_gpsimd("D2", HALF, HALF + PAIR)
-        scalar_w1(5, "r0")
-        scalar_w1(6, "r1")
-        open_h(0, 4, after="w61")
-        for e in range(4):
-            hidden(e)
-        scalar_w1(7, "r2")
+        gather_plain("D3")
+        gate_x_gpsimd("D2", after="xB3")
+        round_w1(5, after="r0")
+        round_w1(6, after="r1")
+        hidden(0, 4, after="w61")
+        round_w1(7, after="r2")
+
         quantize_x("D2")
         quantize_w1(4)
         quantize_w1(5)
-        open_x("D3", after="w51")
-        gate_x_vector("D3", HALF + PAIR, SLOTS)
+        gate_x_vector("D3", after="w51")
         quantize_w1(6)
         quantize_x("D3", after="w70")
         quantize_w1(7)
-        round_w2(0, scalar, "r3")
-        round_w2(1, scalar)
-        open_h(4, 8, after="w2_1")
-        for e in range(4, 8):
-            hidden(e)
-        open_h_codes(0, 4, after="w71")
-        quantize_h(0, 4)
-        quantize_w2("p01")
-        open_h_codes(4, 8, after="p02")
-        quantize_h(4, 6)
-        quantize_h(6, 8)
-        second_layer((0, 1))
-        second_layer((2, 3))
-        second_layer((4, 5))
-        second_layer((6, 7))
-        copy_y((0, 1), scalar, after="w60")
-        copy_y((2, 3), scalar)
-        copy_y((4, 5), scalar)
-        copy_y((6, 7), vector)
+        w2_bf = round_w2(after="r3")
+        hidden(4, 8, after="w2_1")
+        quantize_h(0, 4, 1, after="w71")
+        w2_mx = mx_tiles(E * N, "w2", after="p01")
+        quantize(w2_mx, 0, E * N, w2_bf[:].rearrange("p g c -> p (g c)"))
+        quantize_h(4, 8, 2, after="p02")
+        y_parts = ((0, 2, "a40", nc.scalar.copy), (2, 4, "a41", nc.scalar.copy), (4, 6, "a71", nc.vector.tensor_copy),
+                   (6, 7, "a50", nc.vector.tensor_copy), (7, 8, "a51", nc.scalar.copy))
+        for e0, e1, after, copy in y_parts:
+            second_layer(e0, e1, after)
+        y_sb = staged("y", [P, SLOTS], F32, after="w60")
+        for e0, e1, after, copy in y_parts:
+            copy(y_sb[:, e0 * C:e1 * C], y_banks[e0][:])
 
         pieces = ((0, T - LAST_STORE, "r6"), (T - LAST_STORE, T, "xD2"))
-        first = staged("first", [P, T], F32, "w50")
+        first = staged("first", [P, T], F32, after="w50")
         for t0, t1, after in pieces:
-            nc.vector.tensor_copy(first[:, t0:t1], y_sb[0][:].indirect(pos1_sb[:, t0 // ENTRIES:t1 // ENTRIES]))
+            nc.vector.tensor_copy(first[:, t0:t1], y_sb[:].indirect(pos1_sb[:, t0 // ENTRIES:t1 // ENTRIES]))
         for t0, t1, after in pieces:
             both = staged("both%d" % t0, [P, t1 - t0], F32, after)
-            nc.vector.tensor_tensor(both[:], y_sb[0][:].indirect(pos2_sb[:, t0 // ENTRIES:t1 // ENTRIES]),
+            nc.vector.tensor_tensor(both[:], y_sb[:].indirect(pos2_sb[:, t0 // ENTRIES:t1 // ENTRIES]),
                                     first[:, t0:t1], ADD)
             nc.sync.dma_start(out[:, t0:t1], both[:])

@@ -15,33 +15,30 @@ FP8X4 = mybir.dt.float8_e4m3fn_x4
 MULT = mybir.AluOpType.mult
 ADD = mybir.AluOpType.add
 RELU = mybir.ActivationFunctionType.Relu
+COPY = mybir.ActivationFunctionType.Copy
 
 P = 128
 PACK = 4
 PASSES = K // (P * PACK)
 PAIR = 2 * C
-HALF = SLOTS // 2
+PAIRS = SLOTS // PAIR
 BANK = C // 2
 RUN = 2
 LINE = 4
 ENTRIES = 16
-SPARE = 16
 W2_GROUP = 4
-LAST_STORE = 256
 MX_ALIGN = 64
 
 FLOPS = 2 * SLOTS * (K * H + H * N)
 BYTES = 4 * (K * T + E * K * H + E * H * N + SLOTS + N * T) + 2 * P * (SLOTS + 2 * T) // ENTRIES
-
-W1_CODE_BUFS = 4
 
 
 def tile_moe_pre_mlp_relu_kernel(tc, xT, w1, w2, gate, offs, pos1, pos2, out):
     nc = tc.nc
     with ExitStack() as ctx:
         keep = ctx.enter_context(tc.tile_pool(name="keep", bufs=1))
-        ring = ctx.enter_context(tc.tile_pool(name="ring", bufs=2))
-        psum = ctx.enter_context(tc.psum_pool(name="psum", bufs=2))
+        ring = ctx.enter_context(tc.tile_pool(name="ring", bufs=1))
+        psum = ctx.enter_context(tc.psum_pool(name="psum", bufs=1))
 
         offs_sb = keep.tile([P, SLOTS // ENTRIES], U16, name="offs_sb")
         pos1_sb = keep.tile([P, T // ENTRIES], U16, name="pos1_sb")
@@ -51,302 +48,226 @@ def tile_moe_pre_mlp_relu_kernel(tc, xT, w1, w2, gate, offs, pos1, pos2, out):
         w1_rows = w1.rearrange("e (g p j) c -> e g p j c", g=PASSES, j=PACK)
         w2_rows = w2.rearrange("e (u t r) n -> r t u e n", t=PACK, r=2)
 
-        planes, gates, w1_raw, w2_raw, batches = {}, {}, {}, {}, {}
-        x_bf, w1_bf, h_bf = {}, {}, {}
-        x_mx, w1_mx, h_mx, y_banks = {}, {}, {}, {}
+        tiles, gates, codes_of, y_banks = {}, {}, {}, {}
         place = {}
 
         def staged(key, shape, dtype, after=None):
             place[key] = place.pop(after) if after else "stage_" + key
-            return ring.tile(shape, dtype, name="staged", tag=place[key], bufs=1, align_bytes=MX_ALIGN)
+            tiles[key] = ring.tile(shape, dtype, name="staged", tag=place[key], align_bytes=MX_ALIGN)
+            return tiles[key]
 
         def in_bank(key, shape, after=None):
             place[key] = place.pop(after) if after else "bank_" + key
-            return psum.tile(shape, F32, name="bank", tag=place[key], bufs=1)
-
-        earlier = {(e, b): "a%d%d" % (e - 4, b) for e in range(4, E) for b in range(C // BANK)}
-        earlier.update({(2, 1): "turned", (3, 0): "spread0", (3, 1): "spread1"})
-
-        for g in reversed(range(PASSES)):
-            for t in reversed(range(PACK)):
-                planes[g, t] = staged("p%d%d" % (g, t), [P, T + SPARE], F32)
-                nc.gpsimd.memset(planes[g, t][:, T:], 0.0)
+            return psum.tile(shape, F32, name="bank", tag=place[key])
 
         def load_plane(g, t):
-            nc.sync.dma_start(planes[g, t][:, :T], x_rows[g, t])
+            nc.sync.dma_start(staged("p%d%d" % (g, t), [P, T], F32)[:], x_rows[g, t])
 
-        def load_gate(s0, s1):
-            half = s0 // HALF
-            if half not in gates:
-                gates[half] = staged("gate%d" % half, [P, HALF], F32)
-            nc.sync.dma_start(gates[half][:, s0 - half * HALF:s1 - half * HALF], gate[0:P, s0:s1])
+        def load_w1(e, g, after=None):
+            nc.sync.dma_start(staged("w%d%d" % (e, g), [P, PACK, H], F32, after)[:], w1_rows[e, g])
+
+        def load_w2(group, after=None):
+            raw = staged("v%d" % group, [P, PACK, W2_GROUP, N], F32, after)
+            for r in range(2):
+                for t in range(PACK):
+                    nc.sync.dma_start(raw[r:P:2, t], w2_rows[r, t][:, group * W2_GROUP:(group + 1) * W2_GROUP])
 
         def spread_gate():
             identity = keep.tile([P, P], F32, name="identity")
-            make_identity(nc, identity[:])
-            chunks = HALF // P
+            chunks = SLOTS // P
             rows = keep.tile([P, P], F32, name="gate_rows")
             nc.vector.memset(rows[:], 0.0)
-            nc.sync.dma_start(rows[:chunks, :], gate[0, HALF:].rearrange("(c p) -> c p", p=P))
+            make_identity(nc, identity[:])
+            nc.sync.dma_start(rows[:chunks, :], gate[0].rearrange("(c p) -> c p", p=P))
             turned = in_bank("turned", [P, P])
             nc.tensor.transpose(turned[:], rows[:], identity[:])
             by_slot = keep.tile([P, chunks], F32, name="gate_by_slot")
-            nc.scalar.copy(by_slot[:], turned[:, :chunks])
-            gates[1] = staged("gate1", [P, HALF], F32)
-            for s0 in range(0, HALF, PAIR):
-                bank = in_bank("spread%d" % (s0 // PAIR), [P, PAIR])
+            nc.vector.tensor_copy(by_slot[:], turned[:, :chunks])
+            for pair in range(PAIRS):
+                gates[pair] = in_bank("gate%d" % pair, [P, PAIR])
                 for c in range(PAIR // P):
-                    column = s0 // P + c
-                    nc.tensor.transpose(bank[:, c * P:(c + 1) * P], by_slot[:, column:column + 1].to_broadcast([P, P]),
-                                        identity[:])
-                nc.scalar.copy(gates[1][:, s0:s0 + PAIR], bank[:])
+                    column = pair * PAIR // P + c
+                    nc.tensor.transpose(gates[pair][:, c * P:(c + 1) * P],
+                                        by_slot[:, column:column + 1].to_broadcast([P, P]), identity[:])
 
-        def load_w1(e, g, after=None):
-            w1_raw[e, g] = staged("w%d%d" % (e, g), [P, PACK, H], F32, after)
-            nc.sync.dma_start(w1_raw[e, g][:], w1_rows[e, g])
+        def picked(g, t, pair):
+            return tiles["p%d%d" % (g, t)][:].indirect(offs_sb[:, pair * PAIR // ENTRIES:(pair + 1) * PAIR // ENTRIES])
 
-        def load_w2(group, after):
-            w2_raw[group] = staged("w2_%d" % group, [P, PACK, W2_GROUP, N], F32, after)
-            for r in range(2):
-                for t in range(PACK):
-                    nc.sync.dma_start(w2_raw[group][r:P:2, t],
-                                      w2_rows[r, t][:, group * W2_GROUP:(group + 1) * W2_GROUP])
-
-        def mx_tiles(width, name, bufs=1, after=None):
-            if after:
-                codes = staged(name + "_codes", [P, width], U32, after)
-            else:
-                codes = ring.tile([P, width], U32, name=name + "_codes", bufs=bufs, align_bytes=MX_ALIGN)
-            scales = ring.tile([P, width], U8, name=name + "_scales", bufs=bufs, align_bytes=MX_ALIGN)
-            return codes, scales
-
-        def quantize(mx, c0, c1, src):
-            codes, scales = mx
-            nc.vector.quantize_mx(out=codes[:, c0:c1].bitcast(FP8X4), scales=scales[:, c0:c1], in_=src)
-
-        def open_batch(name, s0, s1, g, after=None):
-            batches[name] = (staged("g" + name, [P, PACK, s1 - s0], F32, after), s0, s1, g)
-
-        def gate_of(s0, s1):
-            return gates[s0 // HALF][:, s0 % HALF:s0 % HALF + s1 - s0]
-
-        def picked(g, t, s0, s1):
-            return planes[g, t][:].indirect(offs_sb[:, s0 // ENTRIES:s1 // ENTRIES])
-
-        def gather_gated(name, t, part=None):
-            tile, s0, s1, g = batches[name]
-            a, b = part or (s0, s1)
-            nc.vector.tensor_tensor(tile[:, t, a - s0:b - s0], picked(g, t, a, b), gate_of(a, b), MULT)
-
-        def gather_plain(name):
-            tile, s0, s1, g = batches[name]
+        def gather_scalar(g, pair, after=None):
+            tile = staged("g%d%d" % (g, pair), [P, PACK, PAIR], F32, after)
             for t in range(PACK):
-                nc.vector.tensor_copy(tile[:, t, :], picked(g, t, s0, s1))
+                nc.scalar.activation(tile[:, t, :], picked(g, t, pair), COPY)
 
-        def open_x(name, run, after):
-            tile, s0, s1, g = batches[name]
-            x_bf[name] = staged("x" + name, [P, (s1 - s0) * PACK], BF16, after)
-            return (x_bf[name][:].rearrange("p (c i t) -> p c t i", i=run, t=PACK),
-                    tile[:].rearrange("p t (c i) -> p c t i", i=run))
+        def gather_vector(g, pair, after=None):
+            tile = staged("g%d%d" % (g, pair), [P, PACK, PAIR], F32, after)
+            for t in range(PACK):
+                nc.vector.tensor_copy(tile[:, t, :], picked(g, t, pair))
 
-        def round_x_scalar(name, after=None):
-            nc.scalar.copy(*open_x(name, RUN, after))
+        def times_gate(g, pair, after=None):
+            dst = staged("x%d%d" % (g, pair), [P, PAIR * PACK], BF16, after)
+            weights = gates[pair][:].rearrange("p (c i) -> p c i", i=LINE)
+            nc.vector.tensor_tensor(dst[:].rearrange("p (c i t) -> p c t i", i=LINE, t=PACK),
+                                    tiles["g%d%d" % (g, pair)][:].rearrange("p t (c i) -> p c t i", i=LINE),
+                                    weights.unsqueeze(2).to_broadcast([P, PAIR // LINE, PACK, LINE]), MULT)
 
-        def round_x_gpsimd(name):
-            dst, src = open_x(name, RUN, None)
-            nc.gpsimd.tensor_scalar(dst.rearrange("p c t i -> p c i t"), src.rearrange("p c t i -> p c i t"),
-                                    1.0, 0.0, MULT, ADD)
+        def round_w1(copy, e, g, after=None):
+            dst = staged("r%d%d" % (e, g), [P, H * PACK], BF16, after)
+            copy(dst[:].rearrange("p (t u r j) -> p u t j r", t=PACK, r=2, j=PACK),
+                 tiles["w%d%d" % (e, g)][:].rearrange("p j (u t r) -> p u t j r", t=PACK, r=2))
 
-        def gate_x_gpsimd(name, after):
-            tile, s0, s1, g = batches[name]
-            x_bf[name] = staged("x" + name, [P, (s1 - s0) * PACK], BF16, after)
-            nc.gpsimd.tensor_tensor(x_bf[name][:].rearrange("p (s t) -> p s t", t=PACK),
-                                    tile[:].rearrange("p t s -> p s t"),
-                                    gate_of(s0, s1).unsqueeze(2).to_broadcast([P, s1 - s0, PACK]), MULT)
+        def round_w2(copy, group, after=None):
+            dst = staged("s%d" % group, [P, W2_GROUP * N * PACK], BF16, after)
+            copy(dst[:].rearrange("p (c i t) -> p c t i", i=RUN, t=PACK),
+                 tiles["v%d" % group][:].rearrange("p t e (c i) -> p (e c) t i", i=RUN))
 
-        def gate_x_vector(name, after):
-            tile, s0, s1, g = batches[name]
-            dst, src = open_x(name, LINE, after)
-            weights = gate_of(s0, s1).rearrange("p (c i) -> p c i", i=LINE)
-            nc.vector.tensor_tensor(dst, src, weights.unsqueeze(2).to_broadcast([P, (s1 - s0) // LINE, PACK, LINE]),
-                                    MULT)
+        def quantize(key, after=None):
+            source = tiles[key]
+            width = source.shape[1] // PACK
+            codes = staged("codes_" + key, [P, width], U32, after)
+            scales = staged("scales_" + key, [P, width], U8)
+            nc.vector.quantize_mx(out=codes[:].bitcast(FP8X4), scales=scales[:], in_=source[:])
+            codes_of[key] = (codes, scales)
 
-        def quantize_x(name, after=None):
-            tile, s0, s1, g = batches[name]
-            mx = mx_tiles(s1 - s0, "x" + name, after=after)
-            quantize(mx, 0, s1 - s0, x_bf[name][:])
-            for e in range(s0 // C, s1 // C):
-                x_mx[e, g] = (mx, e * C - s0)
+        def matmul(dst, left, l0, right, r0, width, start, stop):
+            (l_codes, l_scales), (r_codes, r_scales) = codes_of[left], codes_of[right]
+            nc.tensor.matmul_mx(out=dst, lhsT=l_codes[:, l0:l0 + P].bitcast(FP8X4), lhsT_scale=l_scales[:, l0:l0 + P],
+                                rhs=r_codes[:, r0:r0 + width].bitcast(FP8X4), rhs_scale=r_scales[:, r0:r0 + width],
+                                start=start, stop=stop)
 
-        def round_w1(e, after=None):
-            w1_bf[e] = staged("r%d" % e, [P, PASSES, H * PACK], BF16, after)
-            for g in range(PASSES):
-                nc.scalar.copy(w1_bf[e][:, g].rearrange("p (t u r j) -> p u t j r", t=PACK, r=2, j=PACK),
-                               w1_raw[e, g][:].rearrange("p j (u t r) -> p u t j r", t=PACK, r=2))
-
-        def quantize_w1(e):
-            w1_mx[e] = mx_tiles(PASSES * H, "w1", W1_CODE_BUFS)
-            quantize(w1_mx[e], 0, PASSES * H, w1_bf[e][:].rearrange("p g c -> p (g c)"))
-
-        def round_w2(after):
-            w2_bf = staged("rw2", [P, E // W2_GROUP, W2_GROUP * N * PACK], BF16, after)
-            for group in range(E // W2_GROUP):
-                nc.scalar.copy(w2_bf[:, group].rearrange("p (c i t) -> p c t i", i=RUN, t=PACK),
-                               w2_raw[group][:].rearrange("p t e (c i) -> p (e c) t i", i=RUN))
-            return w2_bf
-
-        def hidden(e0, e1, after):
-            h_bf[e0] = staged("h%d" % e0, [P, (e1 - e0) * C * PACK], BF16, after)
+        def hidden(e0, e1, banks_after, after=None):
+            h_bf = staged("h%d" % e0, [P, (e1 - e0) * C * PACK], BF16, after)
             for e in range(e0, e1):
-                banks = [in_bank("a%d%d" % (e, b), [P, PACK, BANK], earlier.get((e, b))) for b in range(C // BANK)]
-                w_codes, w_scales = w1_mx[e]
-                for b, bank in enumerate(banks):
+                for b in range(C // BANK):
+                    bank = in_bank("a%d%d" % (e, b), [P, PACK, BANK], banks_after[(e - e0) * 2 + b])
                     for g in range(PASSES):
-                        (x_codes, x_scales), s0 = x_mx[e, g]
-                        s0 += b * BANK
                         for t in range(PACK):
-                            c0 = g * H + t * P
-                            nc.tensor.matmul_mx(out=bank[:, t, :],
-                                                lhsT=w_codes[:, c0:c0 + P].bitcast(FP8X4),
-                                                lhsT_scale=w_scales[:, c0:c0 + P],
-                                                rhs=x_codes[:, s0:s0 + BANK].bitcast(FP8X4),
-                                                rhs_scale=x_scales[:, s0:s0 + BANK],
-                                                start=(g == 0 and t == 0),
-                                                stop=(g == PASSES - 1 and t == PACK - 1))
-                for b, bank in enumerate(banks):
+                            matmul(bank[:, t, :], "r%d%d" % (e, g), t * P, "x%d%d" % (g, e // 2),
+                                   e % 2 * C + b * BANK, BANK, g == 0 and t == 0, g == PASSES - 1 and t == PACK - 1)
                     c0 = ((e - e0) * C + b * BANK) * PACK
-                    nc.scalar.activation(h_bf[e0][:, c0:c0 + BANK * PACK].rearrange("p (s t) -> p s t", t=PACK),
+                    nc.scalar.activation(h_bf[:, c0:c0 + BANK * PACK].rearrange("p (s t) -> p s t", t=PACK),
                                          bank[:].rearrange("p t s -> p s t"), RELU)
 
-        def quantize_h(e0, e1, pieces, after):
-            mx = mx_tiles((e1 - e0) * C, "h%d" % e0, after=after)
-            width = (e1 - e0) * C // pieces
-            for c0 in range(0, (e1 - e0) * C, width):
-                quantize(mx, c0, c0 + width, h_bf[e0][:, c0 * PACK:(c0 + width) * PACK])
+        def second_layer(e0, e1, bank_after, copy):
+            bank = in_bank("y%d" % e0, [P, (e1 - e0) * C], bank_after)
             for e in range(e0, e1):
-                h_mx[e] = (mx, (e - e0) * C)
+                matmul(bank[:, (e - e0) * C:(e - e0 + 1) * C], "s%d" % (e // W2_GROUP), e % W2_GROUP * N,
+                       "h%d" % e0, (e - e0) * C, C, True, True)
+            copy(tiles["y"][:, e0 * C:e1 * C], bank[:])
 
-        def second_layer(e0, e1, after):
-            y_banks[e0] = in_bank("y%d" % e0, [P, (e1 - e0) * C], after)
-            w_codes, w_scales = w2_mx
-            for e in range(e0, e1):
-                (h_codes, h_scales), s0 = h_mx[e]
-                nc.tensor.matmul_mx(out=y_banks[e0][:, (e - e0) * C:(e - e0 + 1) * C],
-                                    lhsT=w_codes[:, e * N:(e + 1) * N].bitcast(FP8X4),
-                                    lhsT_scale=w_scales[:, e * N:(e + 1) * N],
-                                    rhs=h_codes[:, s0:s0 + C].bitcast(FP8X4), rhs_scale=h_scales[:, s0:s0 + C],
-                                    start=True, stop=True)
+        on_vector, on_scalar = nc.vector.tensor_copy, nc.scalar.copy
 
         nc.sync.dma_start(offs_sb[:], offs)
         load_plane(0, 0)
-        load_gate(0, C)
-        load_gate(C, PAIR)
+        load_plane(0, 1)
         spread_gate()
-        for t in range(1, PACK):
-            load_plane(0, t)
-        load_gate(PAIR, HALF)
+        load_plane(0, 2)
+        load_plane(0, 3)
         load_w1(0, 0)
-        load_w1(0, 1)
-        load_plane(1, 0)
-        load_plane(1, 1)
-        load_w1(1, 0)
-        load_w1(1, 1)
-        load_plane(1, 2)
-        load_w1(2, 0)
-        load_plane(1, 3)
-        load_w1(2, 1)
-        load_w1(3, 0)
-
-        open_batch("A0", 0, PAIR, 0)
-        open_batch("A1", PAIR, HALF, 0)
-        gather_gated("A0", 0, (0, C))
-        gather_gated("A0", 0, (C, PAIR))
-        for t in range(1, PACK):
-            gather_gated("A0", t)
         for t in range(PACK):
-            gather_gated("A1", t)
-        round_x_scalar("A0")
-        load_w1(3, 1, after="gA0")
-        round_w1(0)
-        load_w1(4, 0, after="w00")
-        round_x_scalar("A1", after="w01")
-        load_w1(4, 1, after="gA1")
-        open_batch("C", 0, HALF, 1)
-        gather_gated("C", 0)
-        quantize_x("A0")
-        quantize_w1(0)
-        gather_gated("C", 1)
-        quantize_x("A1")
-        load_w1(5, 0, after="xA1")
-        round_w1(1)
-        load_w1(5, 1, after="w10")
-        load_w1(6, 0, after="w11")
-        gather_gated("C", 2)
-        quantize_w1(1)
-        gather_gated("C", 3)
+            load_plane(1, t)
+        for e, g in ((0, 1), (1, 0), (1, 1), (2, 0), (2, 1), (3, 0), (3, 1), (5, 0), (4, 0)):
+            load_w1(e, g)
+        load_w2(0)
 
-        open_batch("B2", HALF, HALF + PAIR, 0, after="gate0")
-        gather_plain("B2")
-        round_x_gpsimd("C")
-        round_w1(2)
-        load_w1(6, 1, after="w20")
-        load_w1(7, 0, after="w21")
+        gather_vector(0, 1)
+        gather_scalar(0, 0)
+        gather_scalar(0, 2)
+        times_gate(0, 1)
+        gather_scalar(0, 3, after="g01")
 
-        quantize_x("C")
-        open_batch("B3", HALF + PAIR, SLOTS, 0, after="gC")
-        gather_plain("B3")
-        gate_x_gpsimd("B2", after="xC")
-        quantize_w1(2)
-        round_w1(3)
-        load_w1(7, 1, after="w30")
+        round_w1(on_vector, 0, 0)
+        quantize("x01")
+        times_gate(0, 0, after="w00")
+        quantize("r00")
+        load_w1(6, 1, after="g00")
 
-        quantize_x("B2")
-        open_batch("D2", HALF, HALF + PAIR, 1, after="gB2")
-        gather_plain("D2")
-        gate_x_gpsimd("B3", after="xB2")
-        quantize_w1(3)
-        round_w1(4)
-        load_w2(0, after="w31")
-        load_w2(1, after="w40")
+        round_w1(on_vector, 0, 1, after="x01")
+        gather_scalar(1, 0, after="w01")
+        quantize("x00")
+        quantize("r01")
+        times_gate(0, 2, after="r01")
+        load_w1(4, 1, after="x00")
+        load_w1(7, 1, after="g02")
+
+        round_w1(on_vector, 1, 0, after="r00")
+        gather_scalar(1, 1, after="w10")
+        quantize("x02")
+        quantize("r10")
+        times_gate(0, 3, after="r10")
+        round_w1(on_scalar, 1, 1, after="g03")
+        load_w1(5, 1, after="w11")
+
+        round_w1(on_vector, 2, 0, after="x02")
+        gather_scalar(1, 2, after="w20")
+        quantize("x03")
+        quantize("r20")
+        times_gate(1, 0, after="r20")
+        load_w1(6, 0, after="g10")
+
+        round_w1(on_vector, 2, 1, after="x03")
+        gather_scalar(1, 3, after="w21")
+        quantize("x10")
+        quantize("r21")
+        quantize("r11", after="x10")
+        times_gate(1, 1, after="r21")
+        round_w1(on_scalar, 3, 0, after="g11")
+
+        round_w1(on_vector, 3, 1, after="r11")
+        hidden(0, 2, ["turned", None, None, None], after="w31")
+        load_w1(7, 0, after="w30")
+        quantize("x11")
+        quantize("r31")
+        times_gate(1, 2, after="r31")
+        round_w1(on_scalar, 5, 0, after="g12")
+        load_w2(1, after="w50")
         nc.sync.dma_start(pos1_sb[:], pos1)
         nc.sync.dma_start(pos2_sb[:], pos2)
 
-        quantize_x("B3")
-        open_batch("D3", HALF + PAIR, SLOTS, 1, after="gB3")
-        gather_plain("D3")
-        gate_x_gpsimd("D2", after="xB3")
-        round_w1(5, after="r0")
-        round_w1(6, after="r1")
-        hidden(0, 4, after="w61")
-        round_w1(7, after="r2")
+        round_w1(on_vector, 4, 0, after="x11")
+        quantize("x12")
+        quantize("r40")
+        quantize("r30", after="x12")
+        times_gate(1, 3, after="r40")
+        round_w2(on_scalar, 0, after="r30")
+        hidden(2, 4, ["gate0", "gate1", "a00", "a01"], after="w40")
 
-        quantize_x("D2")
-        quantize_w1(4)
-        quantize_w1(5)
-        gate_x_vector("D3", after="w51")
-        quantize_w1(6)
-        quantize_x("D3", after="w70")
-        quantize_w1(7)
-        w2_bf = round_w2(after="r3")
-        hidden(4, 8, after="w2_1")
-        quantize_h(0, 4, 1, after="w71")
-        w2_mx = mx_tiles(E * N, "w2", after="p01")
-        quantize(w2_mx, 0, E * N, w2_bf[:].rearrange("p g c -> p (g c)"))
-        quantize_h(4, 8, 2, after="p02")
-        y_parts = ((0, 2, "a40", nc.scalar.copy), (2, 4, "a41", nc.scalar.copy), (4, 6, "a71", nc.vector.tensor_copy),
-                   (6, 7, "a50", nc.vector.tensor_copy), (7, 8, "a51", nc.scalar.copy))
-        for e0, e1, after, copy in y_parts:
-            second_layer(e0, e1, after)
-        y_sb = staged("y", [P, SLOTS], F32, after="w60")
-        for e0, e1, after, copy in y_parts:
-            copy(y_sb[:, e0 * C:e1 * C], y_banks[e0][:])
+        round_w1(on_vector, 4, 1)
+        round_w1(on_scalar, 6, 1, after="w41")
+        quantize("x13", after="codes_r01")
+        quantize("h0", after="g13")
+        quantize("r41", after="codes_r10")
+        quantize("r50", after="x13")
 
-        pieces = ((0, T - LAST_STORE, "r6"), (T - LAST_STORE, T, "xD2"))
-        first = staged("first", [P, T], F32, after="w50")
-        for t0, t1, after in pieces:
-            nc.vector.tensor_copy(first[:, t0:t1], y_sb[:].indirect(pos1_sb[:, t0 // ENTRIES:t1 // ENTRIES]))
-        for t0, t1, after in pieces:
-            both = staged("both%d" % t0, [P, t1 - t0], F32, after)
-            nc.vector.tensor_tensor(both[:], y_sb[:].indirect(pos2_sb[:, t0 // ENTRIES:t1 // ENTRIES]),
-                                    first[:, t0:t1], ADD)
+        round_w1(on_vector, 5, 1, after="h0")
+        round_w1(on_scalar, 7, 1, after="w51")
+        quantize("s0", after="r41")
+        quantize("r51", after="codes_x00")
+        quantize("h2", after="r50")
+
+        round_w1(on_vector, 6, 0, after="s0")
+        hidden(4, 6, ["a10", "a11", "gate2", "a20"], after="w60")
+        quantize("r61", after="r51")
+        quantize("r60", after="codes_x10")
+
+        round_w1(on_vector, 7, 0, after="h2")
+        quantize("r71", after="r61")
+        quantize("r70", after="codes_r20")
+        round_w2(on_vector, 1, after="r60")
+        hidden(6, 8, ["a21", "a30", "a31", "gate3"], after="w70")
+        staged("y", [P, SLOTS], F32, after="v1")
+        quantize("h4", after="r70")
+        quantize("s1", after="codes_r21")
+        quantize("h6", after="codes_x11")
+        second_layer(0, 2, "a60", on_scalar)
+        second_layer(2, 4, "a61", on_scalar)
+        second_layer(4, 6, "a70", on_scalar)
+        second_layer(6, 8, "a40", on_vector)
+
+        y_sb = tiles["y"]
+        for t0, t1, a, b in ((0, 128, "p00", "p10"), (128, 384, "p01", "p11"), (384, 768, "p02", "p12"),
+                             (768, 1024, "p03", "p13")):
+            first = staged("first%d" % t0, [P, t1 - t0], F32, a)
+            nc.scalar.activation(first[:], y_sb[:].indirect(pos1_sb[:, t0 // ENTRIES:t1 // ENTRIES]), COPY)
+            both = staged("both%d" % t0, [P, t1 - t0], F32, b)
+            nc.vector.tensor_tensor(both[:], y_sb[:].indirect(pos2_sb[:, t0 // ENTRIES:t1 // ENTRIES]), first[:], ADD)
             nc.sync.dma_start(out[:, t0:t1], both[:])

@@ -194,49 +194,48 @@ def tile_moe_pre_mlp_relu_kernel(tc, xT, w1, w2, gate, offs, pos1, pos2, out):
         quantize("x02")
         quantize("r10")
         times_gate(0, 3, after="r10")
-        round_w1(on_scalar, 1, 1, after="g03")
+        round_w1(on_vector, 1, 1)
         load_w1(5, 1, after="w11")
-
-        round_w1(on_vector, 2, 0, after="x02")
-        gather_scalar(1, 2, after="w20")
         quantize("x03")
+        round_w1(on_vector, 2, 0, after="x02")
+        gather_scalar(1, 2, after="g03")
+        quantize("r11")
         quantize("r20")
         times_gate(1, 0, after="r20")
         load_w1(6, 0, after="g10")
 
         round_w1(on_vector, 2, 1, after="x03")
-        gather_scalar(1, 3, after="w21")
+        gather_scalar(1, 3, after="w20")
         quantize("x10")
         quantize("r21")
-        quantize("r11", after="x10")
         times_gate(1, 1, after="r21")
-        round_w1(on_scalar, 3, 0, after="g11")
 
-        round_w1(on_vector, 3, 1, after="r11")
-        hidden(0, 2, ["turned", None, None, None], after="w31")
+        round_w1(on_vector, 3, 0, after="r11")
+        hidden(0, 2, ["turned", None, None, None], after="w21")
         load_w1(7, 0, after="w30")
         quantize("x11")
+        round_w1(on_vector, 3, 1, after="x10")
+        quantize("r30")
         quantize("r31")
         times_gate(1, 2, after="r31")
-        round_w1(on_scalar, 5, 0, after="g12")
+        round_w1(on_vector, 5, 0, after="g11")
         load_w2(1, after="w50")
         nc.sync.dma_start(pos1_sb[:], pos1)
         nc.sync.dma_start(pos2_sb[:], pos2)
 
-        round_w1(on_vector, 4, 0, after="x11")
         quantize("x12")
+        round_w1(on_vector, 4, 0, after="x11")
+        hidden(2, 4, ["gate0", "gate1", "a00", "a01"], after="g12")
+        round_w2(on_scalar, 0, after="w40")
+        quantize("r50")
         quantize("r40")
-        quantize("r30", after="x12")
         times_gate(1, 3, after="r40")
-        round_w2(on_scalar, 0, after="r30")
-        hidden(2, 4, ["gate0", "gate1", "a00", "a01"], after="w40")
 
         round_w1(on_vector, 4, 1)
         round_w1(on_scalar, 6, 1, after="w41")
         quantize("x13", after="codes_r01")
         quantize("h0", after="g13")
         quantize("r41", after="codes_r10")
-        quantize("r50", after="x13")
 
         round_w1(on_vector, 5, 1, after="h0")
         round_w1(on_scalar, 7, 1, after="w51")

@@ -1,4 +1,5 @@
 from contextlib import ExitStack
+from math import prod
 
 import concourse.mybir as mybir
 from concourse.masks import make_identity
@@ -31,6 +32,7 @@ MX_ALIGN = 64
 
 FLOPS = 2 * SLOTS * (K * H + H * N)
 BYTES = 4 * (K * T + E * K * H + E * H * N + SLOTS + N * T) + 2 * P * (SLOTS + 2 * T) // ENTRIES
+WIDTH = {F32: 4, U32: 4, BF16: 2, U8: 1}
 
 
 def tile_moe_pre_mlp_relu_kernel(tc, xT, w1, w2, gate, offs, pos1, pos2, out):
@@ -49,11 +51,17 @@ def tile_moe_pre_mlp_relu_kernel(tc, xT, w1, w2, gate, offs, pos1, pos2, out):
         w2_rows = w2.rearrange("e (u t r) n -> r t u e n", t=PACK, r=2)
 
         tiles, gates, codes_of, y_banks = {}, {}, {}, {}
-        place = {}
+        place = {"free": 0}
 
         def staged(key, shape, dtype, after=None):
-            place[key] = place.pop(after) if after else "stage_" + key
-            tiles[key] = ring.tile(shape, dtype, name="staged", tag=place[key], align_bytes=MX_ALIGN)
+            if after is None:
+                place[key] = place["free"]
+                place["free"] += prod(shape[1:]) * WIDTH[dtype]
+            elif isinstance(after, str):
+                place[key] = place[after]
+            else:
+                place[key] = place[after[0]] + after[1] * 1024
+            tiles[key] = ring.tile(shape, dtype, name=key, offset=place[key], align_bytes=MX_ALIGN)
             return tiles[key]
 
         def in_bank(key, shape, after=None):
@@ -64,6 +72,11 @@ def tile_moe_pre_mlp_relu_kernel(tc, xT, w1, w2, gate, offs, pos1, pos2, out):
             nc.sync.dma_start(staged("p%d%d" % (g, t), [P, T], F32)[:], x_rows[g, t])
 
         def load_w1(e, g, after=None):
+            if g == 0:
+                staged("w%d" % e, [P, PASSES, PACK, H], F32, after)
+            nc.sync.dma_start(tiles["w%d" % e][:, g], w1_rows[e, g])
+
+        def load_w1_pass(e, g, after=None):
             nc.sync.dma_start(staged("w%d%d" % (e, g), [P, PACK, H], F32, after)[:], w1_rows[e, g])
 
         def load_w2(group, after=None):
@@ -93,15 +106,16 @@ def tile_moe_pre_mlp_relu_kernel(tc, xT, w1, w2, gate, offs, pos1, pos2, out):
         def picked(g, t, pair):
             return tiles["p%d%d" % (g, t)][:].indirect(offs_sb[:, pair * PAIR // ENTRIES:(pair + 1) * PAIR // ENTRIES])
 
-        def gather_scalar(g, pair, after=None):
-            tile = staged("g%d%d" % (g, pair), [P, PACK, PAIR], F32, after)
-            for t in range(PACK):
-                nc.scalar.activation(tile[:, t, :], picked(g, t, pair), COPY)
+        def open_batch(g, pair, after=None):
+            staged("g%d%d" % (g, pair), [P, PACK, PAIR], F32, after)
 
-        def gather_vector(g, pair, after=None):
-            tile = staged("g%d%d" % (g, pair), [P, PACK, PAIR], F32, after)
-            for t in range(PACK):
-                nc.vector.tensor_copy(tile[:, t, :], picked(g, t, pair))
+        def gather_scalar(g, pair, rows):
+            for t in rows:
+                nc.scalar.activation(tiles["g%d%d" % (g, pair)][:, t, :], picked(g, t, pair), COPY)
+
+        def gather_vector(g, pair, rows):
+            for t in rows:
+                nc.vector.tensor_copy(tiles["g%d%d" % (g, pair)][:, t, :], picked(g, t, pair))
 
         def times_gate(g, pair, after=None):
             dst = staged("x%d%d" % (g, pair), [P, PAIR * PACK], BF16, after)
@@ -115,16 +129,22 @@ def tile_moe_pre_mlp_relu_kernel(tc, xT, w1, w2, gate, offs, pos1, pos2, out):
             copy(dst[:].rearrange("p (t u r j) -> p u t j r", t=PACK, r=2, j=PACK),
                  tiles["w%d%d" % (e, g)][:].rearrange("p j (u t r) -> p u t j r", t=PACK, r=2))
 
+        def round_w1_gpsimd(e, after=None):
+            dst = staged("r%d" % e, [P, PASSES * H * PACK], BF16, after)
+            nc.gpsimd.tensor_scalar(
+                dst[:].rearrange("p (t g u r j) -> p g u t r j", t=PACK, g=PASSES, r=2, j=PACK),
+                tiles["w%d" % e][:].rearrange("p g j (u t r) -> p g u t r j", t=PACK, r=2), 1.0, 0.0, MULT, ADD)
+
         def round_w2(copy, group, after=None):
             dst = staged("s%d" % group, [P, W2_GROUP * N * PACK], BF16, after)
             copy(dst[:].rearrange("p (c i t) -> p c t i", i=RUN, t=PACK),
                  tiles["v%d" % group][:].rearrange("p t e (c i) -> p (e c) t i", i=RUN))
 
-        def quantize(key, after=None):
+        def quantize(key, after=None, scales_after=None):
             source = tiles[key]
             width = source.shape[1] // PACK
             codes = staged("codes_" + key, [P, width], U32, after)
-            scales = staged("scales_" + key, [P, width], U8)
+            scales = staged("scales_" + key, [P, width], U8, scales_after)
             nc.vector.quantize_mx(out=codes[:].bitcast(FP8X4), scales=scales[:], in_=source[:])
             codes_of[key] = (codes, scales)
 
@@ -134,18 +154,27 @@ def tile_moe_pre_mlp_relu_kernel(tc, xT, w1, w2, gate, offs, pos1, pos2, out):
                                 rhs=r_codes[:, r0:r0 + width].bitcast(FP8X4), rhs_scale=r_scales[:, r0:r0 + width],
                                 start=start, stop=stop)
 
-        def hidden(e0, e1, banks_after, after=None):
-            h_bf = staged("h%d" % e0, [P, (e1 - e0) * C * PACK], BF16, after)
-            for e in range(e0, e1):
-                for b in range(C // BANK):
-                    bank = in_bank("a%d%d" % (e, b), [P, PACK, BANK], banks_after[(e - e0) * 2 + b])
-                    for g in range(PASSES):
-                        for t in range(PACK):
-                            matmul(bank[:, t, :], "r%d%d" % (e, g), t * P, "x%d%d" % (g, e // 2),
-                                   e % 2 * C + b * BANK, BANK, g == 0 and t == 0, g == PASSES - 1 and t == PACK - 1)
-                    c0 = ((e - e0) * C + b * BANK) * PACK
-                    nc.scalar.activation(h_bf[:, c0:c0 + BANK * PACK].rearrange("p (s t) -> p s t", t=PACK),
-                                         bank[:].rearrange("p t s -> p s t"), RELU)
+        def relu_scalar(dst, src):
+            nc.scalar.activation(dst, src, RELU)
+
+        def relu_vector(dst, src):
+            nc.vector.tensor_scalar_max(dst, src, 0.0)
+
+        def open_h(e0, after=None):
+            staged("h%d" % e0, [P, PAIR * PACK], BF16, after)
+
+        def hidden(e, banks_after, relu):
+            h_bf = tiles["h%d" % (e - e % 2)]
+            for b in range(C // BANK):
+                bank = in_bank("a%d%d" % (e, b), [P, PACK, BANK], banks_after[b])
+                for g in range(PASSES):
+                    for t in range(PACK):
+                        left, l0 = ("r%d" % e, (t * PASSES + g) * P) if "r%d" % e in tiles else ("r%d%d" % (e, g), t * P)
+                        matmul(bank[:, t, :], left, l0, "x%d%d" % (g, e // 2),
+                               e % 2 * C + b * BANK, BANK, g == 0 and t == 0, g == PASSES - 1 and t == PACK - 1)
+                c0 = (e % 2 * C + b * BANK) * PACK
+                relu(h_bf[:, c0:c0 + BANK * PACK].rearrange("p (s t) -> p s t", t=PACK),
+                     bank[:].rearrange("p t s -> p s t"))
 
         def second_layer(e0, e1, bank_after, copy):
             bank = in_bank("y%d" % e0, [P, (e1 - e0) * C], bank_after)
@@ -160,107 +189,111 @@ def tile_moe_pre_mlp_relu_kernel(tc, xT, w1, w2, gate, offs, pos1, pos2, out):
         load_plane(0, 0)
         load_plane(0, 1)
         spread_gate()
+        load_w1(0, 0)
         load_plane(0, 2)
         load_plane(0, 3)
-        load_w1(0, 0)
-        for t in range(PACK):
+        load_w1(0, 1)
+        load_plane(1, 0)
+        load_w1(1, 0)
+        for t in range(1, PACK):
             load_plane(1, t)
-        for e, g in ((0, 1), (1, 0), (1, 1), (2, 0), (2, 1), (3, 0), (3, 1), (5, 0), (4, 0)):
-            load_w1(e, g)
-        load_w2(0)
+        load_w1(1, 1)
+        for g in range(PASSES):
+            load_w1(2, g)
+        for g in range(PASSES):
+            load_w1_pass(4, g)
+        for g in range(PASSES):
+            load_w1(3, g)
+        for g in range(PASSES):
+            load_w1_pass(5, g)
 
-        gather_vector(0, 1)
-        gather_scalar(0, 0)
-        gather_scalar(0, 2)
+        for pair in range(PAIRS):
+            open_batch(0, pair)
+        gather_vector(0, 1, range(PACK))
+        gather_vector(0, 3, range(PACK))
+        gather_scalar(0, 0, range(PACK))
+        gather_scalar(0, 2, range(PACK))
+        round_w1_gpsimd(0)
         times_gate(0, 1)
-        gather_scalar(0, 3, after="g01")
-
-        round_w1(on_vector, 0, 0)
+        times_gate(0, 3)
+        open_batch(1, 0, after="g01")
+        gather_scalar(1, 0, range(PACK))
+        open_batch(1, 2, after="g03")
+        gather_scalar(1, 2, range(PACK))
         quantize("x01")
-        times_gate(0, 0, after="w00")
-        quantize("r00")
-        load_w1(6, 1, after="g00")
-
-        round_w1(on_vector, 0, 1, after="x01")
-        gather_scalar(1, 0, after="w01")
-        quantize("x00")
-        quantize("r01")
-        times_gate(0, 2, after="r01")
-        load_w1(4, 1, after="x00")
-        load_w1(7, 1, after="g02")
-
-        round_w1(on_vector, 1, 0, after="r00")
-        gather_scalar(1, 1, after="w10")
-        quantize("x02")
-        quantize("r10")
-        times_gate(0, 3, after="r10")
-        round_w1(on_vector, 1, 1)
-        load_w1(5, 1, after="w11")
         quantize("x03")
-        round_w1(on_vector, 2, 0, after="x02")
-        gather_scalar(1, 2, after="g03")
-        quantize("r11")
-        quantize("r20")
-        times_gate(1, 0, after="r20")
-        load_w1(6, 0, after="g10")
+        quantize("r0")
 
-        round_w1(on_vector, 2, 1, after="x03")
-        gather_scalar(1, 3, after="w20")
-        quantize("x10")
-        quantize("r21")
-        times_gate(1, 1, after="r21")
+        round_w1_gpsimd(1, after="r0")
+        open_batch(1, 1, after=("w0", 8))
+        gather_vector(1, 1, range(PACK))
+        times_gate(0, 0, after="w0")
+        quantize("x00", after=("w1", 12))
+        quantize("r1")
+        open_batch(1, 3, after="x00")
+        gather_scalar(1, 3, range(PACK))
 
-        round_w1(on_vector, 3, 0, after="r11")
-        hidden(0, 2, ["turned", None, None, None], after="w21")
-        load_w1(7, 0, after="w30")
-        quantize("x11")
-        round_w1(on_vector, 3, 1, after="x10")
-        quantize("r30")
-        quantize("r31")
-        times_gate(1, 2, after="r31")
-        round_w1(on_vector, 5, 0, after="g11")
-        load_w2(1, after="w50")
+        round_w1_gpsimd(2, after="r1")
+        times_gate(0, 2, after="w1")
+        times_gate(1, 0, after=("w1", 4))
+        times_gate(1, 1, after=("w1", 8))
+        round_w1(on_scalar, 4, 0, after="g02")
+        round_w1(on_scalar, 4, 1, after=("g02", 4))
+        quantize("x02", after=("w2", 8))
+        quantize("x10", after=("w2", 10))
+        quantize("x11", after=("w2", 12))
+        quantize("r2")
+        load_w2(0, after="x01")
+        load_w1_pass(7, 0, after="g00")
+        load_w1_pass(6, 0, after="g10")
+        load_w1_pass(6, 1, after="g11")
+        load_w1_pass(7, 1, after="w1")
+        load_w2(1, after="w40")
         nc.sync.dma_start(pos1_sb[:], pos1)
         nc.sync.dma_start(pos2_sb[:], pos2)
 
-        quantize("x12")
-        round_w1(on_vector, 4, 0, after="x11")
-        hidden(2, 4, ["gate0", "gate1", "a00", "a01"], after="g12")
-        round_w2(on_scalar, 0, after="w40")
-        quantize("r50")
-        quantize("r40")
-        times_gate(1, 3, after="r40")
-
-        round_w1(on_vector, 4, 1)
-        round_w1(on_scalar, 6, 1, after="w41")
-        quantize("x13", after="codes_r01")
-        quantize("h0", after="g13")
-        quantize("r41", after="codes_r10")
-
-        round_w1(on_vector, 5, 1, after="h0")
-        round_w1(on_scalar, 7, 1, after="w51")
-        quantize("s0", after="r41")
-        quantize("r51", after="codes_x00")
-        quantize("h2", after="r50")
-
-        round_w1(on_vector, 6, 0, after="s0")
-        hidden(4, 6, ["a10", "a11", "gate2", "a20"], after="w60")
-        quantize("r61", after="r51")
-        quantize("r60", after="codes_x10")
-
-        round_w1(on_vector, 7, 0, after="h2")
-        quantize("r71", after="r61")
-        quantize("r70", after="codes_r20")
-        round_w2(on_vector, 1, after="r60")
-        hidden(6, 8, ["a21", "a30", "a31", "gate3"], after="w70")
-        staged("y", [P, SLOTS], F32, after="v1")
-        quantize("h4", after="r70")
-        quantize("s1", after="codes_r21")
-        quantize("h6", after="codes_x11")
-        second_layer(0, 2, "a60", on_scalar)
-        second_layer(2, 4, "a61", on_scalar)
-        second_layer(4, 6, "a70", on_scalar)
-        second_layer(6, 8, "a40", on_vector)
+        round_w1_gpsimd(3, after="r2")
+        times_gate(1, 2, after="w2")
+        times_gate(1, 3, after=("w2", 4))
+        open_h(0, after="w41")
+        hidden(0, ["turned", None], relu_vector)
+        hidden(1, [None, None], relu_scalar)
+        round_w1(on_scalar, 5, 0, after="g12")
+        round_w1(on_scalar, 5, 1, after=("g12", 4))
+        quantize("r3", after="codes_r0")
+        for n, key in enumerate(("x12", "r40", "r41", "x13", "h0")):
+            quantize(key, after=("w3", 2 * n))
+        open_h(2, after="w50")
+        hidden(2, ["gate0", "gate1"], relu_scalar)
+        quantize("r50", after="x12")
+        quantize("r51", after=("x12", 2))
+        hidden(3, ["a00", "a01"], relu_scalar)
+        open_h(4, after="w51")
+        hidden(4, ["a10", "a11"], relu_scalar)
+        round_w1(on_scalar, 7, 0, after="r41")
+        hidden(5, ["gate2", "gate3"], relu_scalar)
+        round_w1(on_vector, 6, 0, after="r40")
+        round_w1(on_vector, 6, 1, after="h0")
+        quantize("r60", after="x13")
+        round_w2(on_scalar, 0, after="w60")
+        quantize("r61", after=("x13", 2))
+        round_w1(on_vector, 7, 1, after="r50")
+        quantize("r70", after="w61")
+        quantize("r71", after=("w61", 2))
+        open_h(6, after="r60")
+        hidden(6, ["a20", "a21"], relu_scalar)
+        hidden(7, ["a30", "a31"], relu_scalar)
+        quantize("h2", after="w71")
+        quantize("h4", after=("w71", 2))
+        round_w2(on_vector, 1, after="r70")
+        quantize("s0", after="r71")
+        quantize("s1", after="h2")
+        quantize("h6", after="v1")
+        staged("y", [P, SLOTS], F32, after="v0")
+        second_layer(0, 2, "a40", on_scalar)
+        second_layer(2, 4, "a41", on_scalar)
+        second_layer(4, 6, "a50", on_vector)
+        second_layer(6, 8, "a51", on_scalar)
 
         y_sb = tiles["y"]
         for t0, t1, a, b in ((0, 128, "p00", "p10"), (128, 384, "p01", "p11"), (384, 768, "p02", "p12"),

@@ -23,6 +23,8 @@ PACK = 4
 PASSES = K // (P * PACK)
 PAIR = 2 * C
 PAIRS = SLOTS // PAIR
+HALF = 2 * PAIR
+SPARE = 16
 BANK = C // 2
 RUN = 2
 LINE = 4
@@ -68,8 +70,12 @@ def tile_moe_pre_mlp_relu_kernel(tc, xT, w1, w2, gate, offs, pos1, pos2, out):
             place[key] = place.pop(after) if after else "bank_" + key
             return psum.tile(shape, F32, name="bank", tag=place[key])
 
+        for g in reversed(range(PASSES)):
+            for t in reversed(range(PACK)):
+                nc.gpsimd.memset(staged("p%d%d" % (g, t), [P, T + SPARE], F32)[:, T:], 0.0)
+
         def load_plane(g, t):
-            nc.sync.dma_start(staged("p%d%d" % (g, t), [P, T], F32)[:], x_rows[g, t])
+            nc.sync.dma_start(tiles["p%d%d" % (g, t)][:, :T], x_rows[g, t])
 
         def load_w1(e, g, after=None):
             if g == 0:
@@ -103,25 +109,22 @@ def tile_moe_pre_mlp_relu_kernel(tc, xT, w1, w2, gate, offs, pos1, pos2, out):
                     nc.tensor.transpose(gates[pair][:, c * P:(c + 1) * P],
                                         by_slot[:, column:column + 1].to_broadcast([P, P]), identity[:])
 
-        def picked(g, t, pair):
-            return tiles["p%d%d" % (g, t)][:].indirect(offs_sb[:, pair * PAIR // ENTRIES:(pair + 1) * PAIR // ENTRIES])
+        def open_batch(g, half, after=None):
+            staged("g%d%d" % (g, half), [P, PACK, HALF], F32, after)
 
-        def open_batch(g, pair, after=None):
-            staged("g%d%d" % (g, pair), [P, PACK, PAIR], F32, after)
+        def gather(copy, g, t, s0, s1):
+            copy(tiles["g%d%d" % (g, s0 // HALF)][:, t, s0 % HALF:s0 % HALF + s1 - s0],
+                 tiles["p%d%d" % (g, t)][:].indirect(offs_sb[:, s0 // ENTRIES:s1 // ENTRIES]))
 
-        def gather_scalar(g, pair, rows):
-            for t in rows:
-                nc.scalar.activation(tiles["g%d%d" % (g, pair)][:, t, :], picked(g, t, pair), COPY)
-
-        def gather_vector(g, pair, rows):
-            for t in rows:
-                nc.vector.tensor_copy(tiles["g%d%d" % (g, pair)][:, t, :], picked(g, t, pair))
+        def pick_on_scalar(dst, src):
+            nc.scalar.activation(dst, src, COPY)
 
         def times_gate(g, pair, after=None):
             dst = staged("x%d%d" % (g, pair), [P, PAIR * PACK], BF16, after)
+            src = tiles["g%d%d" % (g, pair // 2)][:, :, pair % 2 * PAIR:(pair % 2 + 1) * PAIR]
             weights = gates[pair][:].rearrange("p (c i) -> p c i", i=LINE)
             nc.vector.tensor_tensor(dst[:].rearrange("p (c i t) -> p c t i", i=LINE, t=PACK),
-                                    tiles["g%d%d" % (g, pair)][:].rearrange("p t (c i) -> p c t i", i=LINE),
+                                    src.rearrange("p t (c i) -> p c t i", i=LINE),
                                     weights.unsqueeze(2).to_broadcast([P, PAIR // LINE, PACK, LINE]), MULT)
 
         def round_w1(copy, e, g, after=None):
@@ -135,10 +138,12 @@ def tile_moe_pre_mlp_relu_kernel(tc, xT, w1, w2, gate, offs, pos1, pos2, out):
                 dst[:].rearrange("p (t g u r j) -> p g u t r j", t=PACK, g=PASSES, r=2, j=PACK),
                 tiles["w%d" % e][:].rearrange("p g j (u t r) -> p g u t r j", t=PACK, r=2), 1.0, 0.0, MULT, ADD)
 
-        def round_w2(copy, group, after=None):
-            dst = staged("s%d" % group, [P, W2_GROUP * N * PACK], BF16, after)
-            copy(dst[:].rearrange("p (c i t) -> p c t i", i=RUN, t=PACK),
-                 tiles["v%d" % group][:].rearrange("p t e (c i) -> p (e c) t i", i=RUN))
+        def open_w2(group, after):
+            staged("s%d" % group, [P, W2_GROUP * N * PACK], BF16, after)
+
+        def round_w2(copy, group, c0=0, c1=W2_GROUP * N // RUN):
+            copy(tiles["s%d" % group][:].rearrange("p (c i t) -> p c t i", i=RUN, t=PACK)[:, c0:c1],
+                 tiles["v%d" % group][:].rearrange("p t e (c i) -> p (e c) t i", i=RUN)[:, c0:c1])
 
         def quantize(key, after=None, scales_after=None):
             source = tiles[key]
@@ -163,7 +168,7 @@ def tile_moe_pre_mlp_relu_kernel(tc, xT, w1, w2, gate, offs, pos1, pos2, out):
         def open_h(e0, after=None):
             staged("h%d" % e0, [P, PAIR * PACK], BF16, after)
 
-        def hidden(e, banks_after, relu):
+        def hidden(e, banks_after, *relus):
             h_bf = tiles["h%d" % (e - e % 2)]
             for b in range(C // BANK):
                 bank = in_bank("a%d%d" % (e, b), [P, PACK, BANK], banks_after[b])
@@ -173,14 +178,14 @@ def tile_moe_pre_mlp_relu_kernel(tc, xT, w1, w2, gate, offs, pos1, pos2, out):
                         matmul(bank[:, t, :], left, l0, "x%d%d" % (g, e // 2),
                                e % 2 * C + b * BANK, BANK, g == 0 and t == 0, g == PASSES - 1 and t == PACK - 1)
                 c0 = (e % 2 * C + b * BANK) * PACK
-                relu(h_bf[:, c0:c0 + BANK * PACK].rearrange("p (s t) -> p s t", t=PACK),
-                     bank[:].rearrange("p t s -> p s t"))
+                relus[b % len(relus)](h_bf[:, c0:c0 + BANK * PACK].rearrange("p (s t) -> p s t", t=PACK),
+                                      bank[:].rearrange("p t s -> p s t"))
 
         def second_layer(e0, e1, bank_after, copy):
             bank = in_bank("y%d" % e0, [P, (e1 - e0) * C], bank_after)
             for e in range(e0, e1):
                 matmul(bank[:, (e - e0) * C:(e - e0 + 1) * C], "s%d" % (e // W2_GROUP), e % W2_GROUP * N,
-                       "h%d" % e0, (e - e0) * C, C, True, True)
+                       "h%d" % (e - e % 2), e % 2 * C, C, True, True)
             copy(tiles["y"][:, e0 * C:e1 * C], bank[:])
 
         on_vector, on_scalar = nc.vector.tensor_copy, nc.scalar.copy
@@ -207,47 +212,44 @@ def tile_moe_pre_mlp_relu_kernel(tc, xT, w1, w2, gate, offs, pos1, pos2, out):
         for g in range(PASSES):
             load_w1_pass(5, g)
 
-        for pair in range(PAIRS):
-            open_batch(0, pair)
-        gather_vector(0, 1, range(PACK))
-        gather_vector(0, 3, range(PACK))
-        gather_scalar(0, 0, range(PACK))
-        gather_scalar(0, 2, range(PACK))
+        open_batch(0, 0)
+        open_batch(0, 1)
+        open_batch(1, 0)
+        for t in range(PACK):
+            gather(on_vector, 0, t, HALF, SLOTS)
+            gather(pick_on_scalar, 0, t, 0, HALF)
         round_w1_gpsimd(0)
-        times_gate(0, 1)
+        times_gate(0, 2)
         times_gate(0, 3)
-        open_batch(1, 0, after="g01")
-        gather_scalar(1, 0, range(PACK))
-        open_batch(1, 2, after="g03")
-        gather_scalar(1, 2, range(PACK))
-        quantize("x01")
+        for t in range(PACK):
+            gather(pick_on_scalar, 1, t, 0, HALF)
+        quantize("x02")
         quantize("x03")
         quantize("r0")
 
         round_w1_gpsimd(1, after="r0")
-        open_batch(1, 1, after=("w0", 8))
-        gather_vector(1, 1, range(PACK))
         times_gate(0, 0, after="w0")
-        quantize("x00", after=("w1", 12))
+        times_gate(0, 1, after=("w0", 4))
+        open_batch(1, 1, after="g00")
+        for t in range(PACK):
+            gather(pick_on_scalar, 1, t, HALF, SLOTS)
+        quantize("x00", after=("w1", 4))
+        quantize("x01", after=("w1", 6))
         quantize("r1")
-        open_batch(1, 3, after="x00")
-        gather_scalar(1, 3, range(PACK))
 
         round_w1_gpsimd(2, after="r1")
-        times_gate(0, 2, after="w1")
-        times_gate(1, 0, after=("w1", 4))
+        times_gate(1, 0, after="w1")
         times_gate(1, 1, after=("w1", 8))
-        round_w1(on_scalar, 4, 0, after="g02")
-        round_w1(on_scalar, 4, 1, after=("g02", 4))
-        quantize("x02", after=("w2", 8))
-        quantize("x10", after=("w2", 10))
-        quantize("x11", after=("w2", 12))
+        round_w1(on_scalar, 4, 0, after="g10")
+        round_w1(on_scalar, 4, 1, after=("g10", 4))
+        quantize("x10", after=("w2", 8))
+        quantize("x11", after=("w2", 10))
         quantize("r2")
-        load_w2(0, after="x01")
-        load_w1_pass(7, 0, after="g00")
-        load_w1_pass(6, 0, after="g10")
-        load_w1_pass(6, 1, after="g11")
-        load_w1_pass(7, 1, after="w1")
+        load_w2(0, after="g01")
+        load_w1_pass(7, 0, after=("g01", 8))
+        load_w1_pass(6, 0, after="x02")
+        load_w1_pass(6, 1, after=("w0", 8))
+        load_w1_pass(7, 1, after="w0")
         load_w2(1, after="w40")
         nc.sync.dma_start(pos1_sb[:], pos1)
         nc.sync.dma_start(pos2_sb[:], pos2)
@@ -258,8 +260,8 @@ def tile_moe_pre_mlp_relu_kernel(tc, xT, w1, w2, gate, offs, pos1, pos2, out):
         open_h(0, after="w41")
         hidden(0, ["turned", None], relu_vector)
         hidden(1, [None, None], relu_scalar)
-        round_w1(on_scalar, 5, 0, after="g12")
-        round_w1(on_scalar, 5, 1, after=("g12", 4))
+        round_w1(on_scalar, 5, 0, after=("w41", 4))
+        round_w1(on_scalar, 5, 1, after=("w1", 12))
         quantize("r3", after="codes_r0")
         for n, key in enumerate(("x12", "r40", "r41", "x13", "h0")):
             quantize(key, after=("w3", 2 * n))
@@ -275,7 +277,8 @@ def tile_moe_pre_mlp_relu_kernel(tc, xT, w1, w2, gate, offs, pos1, pos2, out):
         round_w1(on_vector, 6, 0, after="r40")
         round_w1(on_vector, 6, 1, after="h0")
         quantize("r60", after="x13")
-        round_w2(on_scalar, 0, after="w60")
+        open_w2(0, after="w60")
+        round_w2(on_scalar, 0)
         quantize("r61", after=("x13", 2))
         round_w1(on_vector, 7, 1, after="r50")
         quantize("r70", after="w61")
@@ -285,10 +288,11 @@ def tile_moe_pre_mlp_relu_kernel(tc, xT, w1, w2, gate, offs, pos1, pos2, out):
         hidden(7, ["a30", "a31"], relu_scalar)
         quantize("h2", after="w71")
         quantize("h4", after=("w71", 2))
-        round_w2(on_vector, 1, after="r70")
         quantize("s0", after="r71")
+        quantize("h6", after="s0")
+        open_w2(1, after="r70")
+        round_w2(on_vector, 1)
         quantize("s1", after="h2")
-        quantize("h6", after="v1")
         staged("y", [P, SLOTS], F32, after="v0")
         second_layer(0, 2, "a40", on_scalar)
         second_layer(2, 4, "a41", on_scalar)
@@ -296,10 +300,13 @@ def tile_moe_pre_mlp_relu_kernel(tc, xT, w1, w2, gate, offs, pos1, pos2, out):
         second_layer(6, 8, "a51", on_scalar)
 
         y_sb = tiles["y"]
-        for t0, t1, a, b in ((0, 128, "p00", "p10"), (128, 384, "p01", "p11"), (384, 768, "p02", "p12"),
-                             (768, 1024, "p03", "p13")):
+        pieces = ((0, 192, "p00", "p10"), (192, 512, "p01", "p11"), (512, 896, "p02", "p12"), (896, T, "p03", "p13"))
+        for t0, t1, a, b in pieces:
             first = staged("first%d" % t0, [P, t1 - t0], F32, a)
-            nc.scalar.activation(first[:], y_sb[:].indirect(pos1_sb[:, t0 // ENTRIES:t1 // ENTRIES]), COPY)
+            picked_first = y_sb[:].indirect(pos1_sb[:, t0 // ENTRIES:t1 // ENTRIES])
+            (pick_on_scalar if t0 else on_vector)(first[:], picked_first)
+        for t0, t1, a, b in pieces:
             both = staged("both%d" % t0, [P, t1 - t0], F32, b)
-            nc.vector.tensor_tensor(both[:], y_sb[:].indirect(pos2_sb[:, t0 // ENTRIES:t1 // ENTRIES]), first[:], ADD)
+            nc.vector.tensor_tensor(both[:], y_sb[:].indirect(pos2_sb[:, t0 // ENTRIES:t1 // ENTRIES]),
+                                    tiles["first%d" % t0][:], ADD)
             nc.sync.dma_start(out[:, t0:t1], both[:])

@@ -35,6 +35,7 @@ MX_ALIGN = 64
 FLOPS = 2 * SLOTS * (K * H + H * N)
 BYTES = 4 * (K * T + E * K * H + E * H * N + SLOTS + N * T) + 2 * P * (SLOTS + 2 * T) // ENTRIES
 WIDTH = {F32: 4, U32: 4, BF16: 2, U8: 1}
+TOKEN_PIECES = ((0, 128), (128, 320), (320, 640), (640, 896), (896, T))
 
 
 def tile_moe_pre_mlp_relu_kernel(tc, xT, w1, w2, gate, offs, pos1, pos2, out):
@@ -52,7 +53,7 @@ def tile_moe_pre_mlp_relu_kernel(tc, xT, w1, w2, gate, offs, pos1, pos2, out):
         w1_rows = w1.rearrange("e (g p j) c -> e g p j c", g=PASSES, j=PACK)
         w2_rows = w2.rearrange("e (u t r) n -> r t u e n", t=PACK, r=2)
 
-        tiles, gates, codes_of, y_banks = {}, {}, {}, {}
+        tiles, batches, gates, codes_of, h_first = {}, {}, {}, {}, {}
         place = {"free": 0}
 
         def staged(key, shape, dtype, after=None):
@@ -109,19 +110,23 @@ def tile_moe_pre_mlp_relu_kernel(tc, xT, w1, w2, gate, offs, pos1, pos2, out):
                     nc.tensor.transpose(gates[pair][:, c * P:(c + 1) * P],
                                         by_slot[:, column:column + 1].to_broadcast([P, P]), identity[:])
 
-        def open_batch(g, half, after=None):
-            staged("g%d%d" % (g, half), [P, PACK, HALF], F32, after)
+        def open_batch(g, pair0, pair1, after=None):
+            tile = staged("g%d%d" % (g, pair0), [P, PACK, (pair1 - pair0) * PAIR], F32, after)
+            for pair in range(pair0, pair1):
+                batches[g, pair] = (tile, pair0, pair1)
 
-        def gather(copy, g, t, s0, s1):
-            copy(tiles["g%d%d" % (g, s0 // HALF)][:, t, s0 % HALF:s0 % HALF + s1 - s0],
-                 tiles["p%d%d" % (g, t)][:].indirect(offs_sb[:, s0 // ENTRIES:s1 // ENTRIES]))
+        def gather(copy, g, pair, t):
+            tile, pair0, pair1 = batches[g, pair]
+            copy(tile[:, t, :],
+                 tiles["p%d%d" % (g, t)][:].indirect(offs_sb[:, pair0 * PAIR // ENTRIES:pair1 * PAIR // ENTRIES]))
 
         def pick_on_scalar(dst, src):
             nc.scalar.activation(dst, src, COPY)
 
         def times_gate(g, pair, after=None):
             dst = staged("x%d%d" % (g, pair), [P, PAIR * PACK], BF16, after)
-            src = tiles["g%d%d" % (g, pair // 2)][:, :, pair % 2 * PAIR:(pair % 2 + 1) * PAIR]
+            tile, pair0, pair1 = batches[g, pair]
+            src = tile[:, :, (pair - pair0) * PAIR:(pair - pair0 + 1) * PAIR]
             weights = gates[pair][:].rearrange("p (c i) -> p c i", i=LINE)
             nc.vector.tensor_tensor(dst[:].rearrange("p (c i t) -> p c t i", i=LINE, t=PACK),
                                     src.rearrange("p t (c i) -> p c t i", i=LINE),
@@ -165,11 +170,13 @@ def tile_moe_pre_mlp_relu_kernel(tc, xT, w1, w2, gate, offs, pos1, pos2, out):
         def relu_vector(dst, src):
             nc.vector.tensor_scalar_max(dst, src, 0.0)
 
-        def open_h(e0, after=None):
-            staged("h%d" % e0, [P, PAIR * PACK], BF16, after)
+        def open_h(e0, e1, after=None):
+            staged("h%d" % e0, [P, (e1 - e0) * C * PACK], BF16, after)
+            for e in range(e0, e1):
+                h_first[e] = e0
 
         def hidden(e, banks_after, *relus):
-            h_bf = tiles["h%d" % (e - e % 2)]
+            h_bf = tiles["h%d" % h_first[e]]
             for b in range(C // BANK):
                 bank = in_bank("a%d%d" % (e, b), [P, PACK, BANK], banks_after[b])
                 for g in range(PASSES):
@@ -177,7 +184,7 @@ def tile_moe_pre_mlp_relu_kernel(tc, xT, w1, w2, gate, offs, pos1, pos2, out):
                         left, l0 = ("r%d" % e, (t * PASSES + g) * P) if "r%d" % e in tiles else ("r%d%d" % (e, g), t * P)
                         matmul(bank[:, t, :], left, l0, "x%d%d" % (g, e // 2),
                                e % 2 * C + b * BANK, BANK, g == 0 and t == 0, g == PASSES - 1 and t == PACK - 1)
-                c0 = (e % 2 * C + b * BANK) * PACK
+                c0 = ((e - h_first[e]) * C + b * BANK) * PACK
                 relus[b % len(relus)](h_bf[:, c0:c0 + BANK * PACK].rearrange("p (s t) -> p s t", t=PACK),
                                       bank[:].rearrange("p t s -> p s t"))
 
@@ -185,7 +192,7 @@ def tile_moe_pre_mlp_relu_kernel(tc, xT, w1, w2, gate, offs, pos1, pos2, out):
             bank = in_bank("y%d" % e0, [P, (e1 - e0) * C], bank_after)
             for e in range(e0, e1):
                 matmul(bank[:, (e - e0) * C:(e - e0 + 1) * C], "s%d" % (e // W2_GROUP), e % W2_GROUP * N,
-                       "h%d" % (e - e % 2), e % 2 * C, C, True, True)
+                       "h%d" % h_first[e], (e - h_first[e]) * C, C, True, True)
             copy(tiles["y"][:, e0 * C:e1 * C], bank[:])
 
         on_vector, on_scalar = nc.vector.tensor_copy, nc.scalar.copy
@@ -200,29 +207,28 @@ def tile_moe_pre_mlp_relu_kernel(tc, xT, w1, w2, gate, offs, pos1, pos2, out):
         load_w1(0, 1)
         load_plane(1, 0)
         load_w1(1, 0)
+        open_batch(0, 2, 4)
         for t in range(1, PACK):
             load_plane(1, t)
         load_w1(1, 1)
         for g in range(PASSES):
             load_w1(2, g)
-        for g in range(PASSES):
-            load_w1_pass(4, g)
+        for e in (4, 5):
+            for g in range(PASSES):
+                load_w1_pass(e, g)
         for g in range(PASSES):
             load_w1(3, g)
-        for g in range(PASSES):
-            load_w1_pass(5, g)
 
-        open_batch(0, 0)
-        open_batch(0, 1)
-        open_batch(1, 0)
+        open_batch(0, 0, 2)
+        open_batch(1, 0, 2)
         for t in range(PACK):
-            gather(on_vector, 0, t, HALF, SLOTS)
-            gather(pick_on_scalar, 0, t, 0, HALF)
+            gather(on_vector, 0, 2, t)
+            gather(pick_on_scalar, 0, 0, t)
         round_w1_gpsimd(0)
         times_gate(0, 2)
         times_gate(0, 3)
         for t in range(PACK):
-            gather(pick_on_scalar, 1, t, 0, HALF)
+            gather(pick_on_scalar, 1, 0, t)
         quantize("x02")
         quantize("x03")
         quantize("r0")
@@ -230,83 +236,88 @@ def tile_moe_pre_mlp_relu_kernel(tc, xT, w1, w2, gate, offs, pos1, pos2, out):
         round_w1_gpsimd(1, after="r0")
         times_gate(0, 0, after="w0")
         times_gate(0, 1, after=("w0", 4))
-        open_batch(1, 1, after="g00")
+        open_batch(1, 2, 3, after="g00")
         for t in range(PACK):
-            gather(pick_on_scalar, 1, t, HALF, SLOTS)
-        quantize("x00", after=("w1", 4))
-        quantize("x01", after=("w1", 6))
+            gather(on_vector if t < 2 else pick_on_scalar, 1, 2, t)
+        quantize("x00", after=("w1", 8))
+        quantize("x01", after=("w1", 10))
         quantize("r1")
 
         round_w1_gpsimd(2, after="r1")
+        open_batch(1, 3, 4, after=("w1", 12))
         times_gate(1, 0, after="w1")
-        times_gate(1, 1, after=("w1", 8))
-        round_w1(on_scalar, 4, 0, after="g10")
-        round_w1(on_scalar, 4, 1, after=("g10", 4))
+        for t in range(PACK):
+            gather(on_vector if t < 2 else pick_on_scalar, 1, 3, t)
+        times_gate(1, 1, after=("w1", 4))
+        round_w1(on_scalar, 4, 0, after=("g00", 8))
+        round_w1(on_scalar, 4, 1, after=("g00", 12))
+        round_w1(on_scalar, 5, 0, after="w40")
+        round_w1(on_scalar, 5, 1, after=("w40", 4))
         quantize("x10", after=("w2", 8))
         quantize("x11", after=("w2", 10))
         quantize("r2")
-        load_w2(0, after="g01")
-        load_w1_pass(7, 0, after=("g01", 8))
+        load_w2(0, after=("g02", 8))
+        load_w1_pass(7, 0, after=("w0", 8))
         load_w1_pass(6, 0, after="x02")
-        load_w1_pass(6, 1, after=("w0", 8))
-        load_w1_pass(7, 1, after="w0")
-        load_w2(1, after="w40")
+        load_w1_pass(6, 1, after="w0")
+        load_w1_pass(7, 1, after="g10")
+        load_w2(1, after=("g10", 8))
         nc.sync.dma_start(pos1_sb[:], pos1)
         nc.sync.dma_start(pos2_sb[:], pos2)
 
         round_w1_gpsimd(3, after="r2")
         times_gate(1, 2, after="w2")
         times_gate(1, 3, after=("w2", 4))
-        open_h(0, after="w41")
+        open_h(0, 2, after="w51")
         hidden(0, ["turned", None], relu_vector)
         hidden(1, [None, None], relu_scalar)
-        round_w1(on_scalar, 5, 0, after=("w41", 4))
-        round_w1(on_scalar, 5, 1, after=("w1", 12))
-        quantize("r3", after="codes_r0")
-        for n, key in enumerate(("x12", "r40", "r41", "x13", "h0")):
-            quantize(key, after=("w3", 2 * n))
-        open_h(2, after="w50")
+        open_h(2, 3, after=("w51", 4))
         hidden(2, ["gate0", "gate1"], relu_scalar)
-        quantize("r50", after="x12")
-        quantize("r51", after=("x12", 2))
-        hidden(3, ["a00", "a01"], relu_scalar)
-        open_h(4, after="w51")
-        hidden(4, ["a10", "a11"], relu_scalar)
-        round_w1(on_scalar, 7, 0, after="r41")
-        hidden(5, ["gate2", "gate3"], relu_scalar)
-        round_w1(on_vector, 6, 0, after="r40")
-        round_w1(on_vector, 6, 1, after="h0")
-        quantize("r60", after="x13")
-        open_w2(0, after="w60")
+        open_w2(0, after="w41")
         round_w2(on_scalar, 0)
-        quantize("r61", after=("x13", 2))
-        round_w1(on_vector, 7, 1, after="r50")
-        quantize("r70", after="w61")
-        quantize("r71", after=("w61", 2))
-        open_h(6, after="r60")
-        hidden(6, ["a20", "a21"], relu_scalar)
+        round_w1(on_scalar, 7, 0, after=("w41", 4))
+        round_w1(on_scalar, 6, 0, after="g12")
+        quantize("r3", after="codes_r0")
+        for n, key in enumerate(("x12", "r40", "r41", "r50", "r51", "x13", "h0")):
+            quantize(key, after=("w3", 2 * n))
+        open_h(3, 5, after="w60")
+        open_h(5, 6, after=("w60", 4))
+        hidden(3, ["a00", "a01"], relu_scalar)
+        hidden(4, ["a10", "a11"], relu_scalar)
+        hidden(5, ["a20", "a21"], relu_scalar)
+        quantize("h2", after=("w3", 14))
+        quantize("s0", after="x12")
+        quantize("r70", after=("x12", 2))
+        round_w1(on_scalar, 7, 1, after="r70")
+        round_w1(on_vector, 6, 1, after="r50")
+        quantize("r60", after="w61")
+        quantize("r61", after="x13")
+        quantize("r71", after="h2")
+        open_h(6, 8, after="w71")
+        quantize("h3", after=("w71", 4))
+        quantize("h5", after=("w71", 6))
+        hidden(6, ["gate2", "gate3"], relu_scalar)
         hidden(7, ["a30", "a31"], relu_scalar)
-        quantize("h2", after="w71")
-        quantize("h4", after=("w71", 2))
-        quantize("s0", after="r71")
-        quantize("h6", after="s0")
-        open_w2(1, after="r70")
-        round_w2(on_vector, 1)
-        quantize("s1", after="h2")
-        staged("y", [P, SLOTS], F32, after="v0")
+        staged("y", [P, SLOTS], F32, after="r71")
         second_layer(0, 2, "a40", on_scalar)
         second_layer(2, 4, "a41", on_scalar)
-        second_layer(4, 6, "a50", on_vector)
-        second_layer(6, 8, "a51", on_scalar)
+        open_w2(1, after="r60")
+        round_w2(on_vector, 1)
+        quantize("s1", after="h3")
+        quantize("h6", after="v1")
+        second_layer(4, 6, "a50", on_scalar)
+        second_layer(6, 7, "a51", on_vector)
+        second_layer(7, 8, "a60", on_scalar)
 
         y_sb = tiles["y"]
-        pieces = ((0, 192, "p00", "p10"), (192, 512, "p01", "p11"), (512, 896, "p02", "p12"), (896, T, "p03", "p13"))
-        for t0, t1, a, b in pieces:
-            first = staged("first%d" % t0, [P, t1 - t0], F32, a)
-            picked_first = y_sb[:].indirect(pos1_sb[:, t0 // ENTRIES:t1 // ENTRIES])
-            (pick_on_scalar if t0 else on_vector)(first[:], picked_first)
-        for t0, t1, a, b in pieces:
-            both = staged("both%d" % t0, [P, t1 - t0], F32, b)
-            nc.vector.tensor_tensor(both[:], y_sb[:].indirect(pos2_sb[:, t0 // ENTRIES:t1 // ENTRIES]),
+        both = staged("both", [P, T], F32, after="p10")
+        for n, (t0, t1) in enumerate(TOKEN_PIECES):
+            first = staged("first%d" % t0, [P, t1 - t0], F32, after="p0%d" % n if n < PACK else "p11")
+            (on_vector if n == 1 else pick_on_scalar)(first[:], y_sb[:].indirect(pos1_sb[:, t0 // ENTRIES:t1 // ENTRIES]))
+        stored = 0
+        for n, (t0, t1) in enumerate(TOKEN_PIECES):
+            nc.vector.tensor_tensor(both[:, t0:t1], y_sb[:].indirect(pos2_sb[:, t0 // ENTRIES:t1 // ENTRIES]),
                                     tiles["first%d" % t0][:], ADD)
-            nc.sync.dma_start(out[:, t0:t1], both[:])
+            if n >= 2:
+                nc.sync.dma_start(out[:, stored:t1], both[:, stored:t1])
+                stored = t1

@@ -52,6 +52,7 @@ def tile_moe_pre_mlp_relu_kernel(tc, xT, w1, w2, gate, offs, pos1, pos2, out):
         x_rows = xT.rearrange("(g p t) n -> g t p n", g=PASSES, t=PACK)
         w1_rows = w1.rearrange("e (g p j) c -> e g p j c", g=PASSES, j=PACK)
         w2_rows = w2.rearrange("e (u t r) n -> r t u e n", t=PACK, r=2)
+        w2_runs = w2.rearrange("e (p t) n -> p e t n", t=PACK)
 
         tiles, batches, gates, codes_of, h_first = {}, {}, {}, {}, {}
         place = {"free": 0}
@@ -91,6 +92,9 @@ def tile_moe_pre_mlp_relu_kernel(tc, xT, w1, w2, gate, offs, pos1, pos2, out):
             for r in range(2):
                 for t in range(PACK):
                     nc.sync.dma_start(raw[r:P:2, t], w2_rows[r, t][:, group * W2_GROUP:(group + 1) * W2_GROUP])
+
+        def load_w2_runs(after):
+            nc.sync.dma_start(staged("v0", [P, W2_GROUP, PACK, N], F32, after)[:], w2_runs[:, :W2_GROUP])
 
         def spread_gate():
             identity = keep.tile([P, P], F32, name="identity")
@@ -137,18 +141,19 @@ def tile_moe_pre_mlp_relu_kernel(tc, xT, w1, w2, gate, offs, pos1, pos2, out):
             copy(dst[:].rearrange("p (t u r j) -> p u t j r", t=PACK, r=2, j=PACK),
                  tiles["w%d%d" % (e, g)][:].rearrange("p j (u t r) -> p u t j r", t=PACK, r=2))
 
-        def round_w1_gpsimd(e, after=None):
+        def round_w1_gpsimd(e, after=None, passes=(slice(0, PASSES),)):
             dst = staged("r%d" % e, [P, PASSES * H * PACK], BF16, after)
-            nc.gpsimd.tensor_scalar(
-                dst[:].rearrange("p (t g u r j) -> p g u t r j", t=PACK, g=PASSES, r=2, j=PACK),
-                tiles["w%d" % e][:].rearrange("p g j (u t r) -> p g u t r j", t=PACK, r=2), 1.0, 0.0, MULT, ADD)
+            for g in passes:
+                nc.gpsimd.tensor_scalar(dst[:].rearrange("p (t g q j) -> p g q t j", t=PACK, g=PASSES, j=PACK)[:, g],
+                                        tiles["w%d" % e][:].rearrange("p g j (q t) -> p g q t j", t=PACK)[:, g],
+                                        1.0, 0.0, MULT, ADD)
 
         def open_w2(group, after):
             staged("s%d" % group, [P, W2_GROUP * N * PACK], BF16, after)
 
-        def round_w2(copy, group, c0=0, c1=W2_GROUP * N // RUN):
-            copy(tiles["s%d" % group][:].rearrange("p (c i t) -> p c t i", i=RUN, t=PACK)[:, c0:c1],
-                 tiles["v%d" % group][:].rearrange("p t e (c i) -> p (e c) t i", i=RUN)[:, c0:c1])
+        def round_w2(copy, group, pattern, experts=slice(0, W2_GROUP)):
+            copy(tiles["s%d" % group][:].rearrange("p (e c i t) -> p e c t i", e=W2_GROUP, i=RUN, t=PACK)[:, experts],
+                 tiles["v%d" % group][:].rearrange(pattern + " (c i) -> p e c t i", i=RUN)[:, experts])
 
         def quantize(key, after=None, scales_after=None):
             source = tiles[key]
@@ -224,7 +229,7 @@ def tile_moe_pre_mlp_relu_kernel(tc, xT, w1, w2, gate, offs, pos1, pos2, out):
         for t in range(PACK):
             gather(on_vector, 0, 2, t)
             gather(pick_on_scalar, 0, 0, t)
-        round_w1_gpsimd(0)
+        round_w1_gpsimd(0, passes=range(PASSES))
         times_gate(0, 2)
         times_gate(0, 3)
         for t in range(PACK):
@@ -233,7 +238,7 @@ def tile_moe_pre_mlp_relu_kernel(tc, xT, w1, w2, gate, offs, pos1, pos2, out):
         quantize("x03")
         quantize("r0")
 
-        round_w1_gpsimd(1, after="r0")
+        round_w1_gpsimd(1, after="r0", passes=range(PASSES))
         times_gate(0, 0, after="w0")
         times_gate(0, 1, after=("w0", 4))
         open_batch(1, 2, 3, after="g00")
@@ -256,16 +261,16 @@ def tile_moe_pre_mlp_relu_kernel(tc, xT, w1, w2, gate, offs, pos1, pos2, out):
         quantize("x10", after=("w2", 8))
         quantize("x11", after=("w2", 10))
         quantize("r2")
-        load_w2(0, after=("g02", 8))
-        load_w1_pass(7, 0, after=("w0", 8))
-        load_w1_pass(6, 0, after="x02")
-        load_w1_pass(6, 1, after="w0")
-        load_w1_pass(7, 1, after="g10")
-        load_w2(1, after=("g10", 8))
+        load_w1_pass(6, 0, after=("g02", 8))
+        load_w1_pass(6, 1, after=("w0", 8))
+        load_w1_pass(7, 0, after="x02")
+        load_w1_pass(7, 1, after="w0")
+        load_w2(1, after="g10")
+        load_w2_runs(after=("g10", 8))
         nc.sync.dma_start(pos1_sb[:], pos1)
         nc.sync.dma_start(pos2_sb[:], pos2)
 
-        round_w1_gpsimd(3, after="r2")
+        round_w1_gpsimd(3, after="r2", passes=range(PASSES))
         times_gate(1, 2, after="w2")
         times_gate(1, 3, after=("w2", 4))
         open_h(0, 2, after="w51")
@@ -273,41 +278,40 @@ def tile_moe_pre_mlp_relu_kernel(tc, xT, w1, w2, gate, offs, pos1, pos2, out):
         hidden(1, [None, None], relu_scalar)
         open_h(2, 3, after=("w51", 4))
         hidden(2, ["gate0", "gate1"], relu_scalar)
-        open_w2(0, after="w41")
-        round_w2(on_scalar, 0)
-        round_w1(on_scalar, 7, 0, after=("w41", 4))
-        round_w1(on_scalar, 6, 0, after="g12")
+        round_w1(on_scalar, 6, 0, after="w41")
+        round_w1(on_scalar, 6, 1, after=("w41", 4))
         quantize("r3", after="codes_r0")
-        for n, key in enumerate(("x12", "r40", "r41", "r50", "r51", "x13", "h0")):
+        for n, key in enumerate(("x12", "r40", "r41", "r50", "r51", "x13", "r60", "h0")):
             quantize(key, after=("w3", 2 * n))
-        open_h(3, 5, after="w60")
-        open_h(5, 6, after=("w60", 4))
+        round_w1(on_scalar, 7, 0, after="w61")
+        open_h(3, 5, after="w70")
+        open_h(5, 6, after=("w70", 4))
         hidden(3, ["a00", "a01"], relu_scalar)
         hidden(4, ["a10", "a11"], relu_scalar)
         hidden(5, ["a20", "a21"], relu_scalar)
-        quantize("h2", after=("w3", 14))
-        quantize("s0", after="x12")
-        quantize("r70", after=("x12", 2))
-        round_w1(on_scalar, 7, 1, after="r70")
-        round_w1(on_vector, 6, 1, after="r50")
-        quantize("r60", after="w61")
-        quantize("r61", after="x13")
-        quantize("r71", after="h2")
-        open_h(6, 8, after="w71")
-        quantize("h3", after=("w71", 4))
-        quantize("h5", after=("w71", 6))
+        round_w1(on_vector, 7, 1, after="r40")
+        quantize("r61", after="x12")
+        quantize("h2", after=("x12", 2))
+        quantize("r70", after="x13")
+        open_w2(1, after="r70")
+        round_w2(on_scalar, 1, "p t e")
+        quantize("r71", after="r50")
+        open_h(6, 8, after="v1")
         hidden(6, ["gate2", "gate3"], relu_scalar)
         hidden(7, ["a30", "a31"], relu_scalar)
-        staged("y", [P, SLOTS], F32, after="r71")
-        second_layer(0, 2, "a40", on_scalar)
-        second_layer(2, 4, "a41", on_scalar)
-        open_w2(1, after="r60")
-        round_w2(on_vector, 1)
-        quantize("s1", after="h3")
-        quantize("h6", after="v1")
-        second_layer(4, 6, "a50", on_scalar)
-        second_layer(6, 7, "a51", on_vector)
-        second_layer(7, 8, "a60", on_scalar)
+        quantize("h3", after="w71")
+        quantize("h5", after=("w71", 2))
+        open_w2(0, after="r71")
+        round_w2(on_vector, 0, "p e t")
+        quantize("s1", after="v0")
+        quantize("s0", after="h3")
+        quantize("h6", after=("v0", 2))
+        staged("y", [P, SLOTS], F32, after="w60")
+        second_layer(4, 6, "a40", on_scalar)
+        second_layer(0, 2, "a50", on_scalar)
+        second_layer(2, 4, "a51", on_vector)
+        second_layer(6, 7, "a41", on_scalar)
+        second_layer(7, 8, "a60", on_vector)
 
         y_sb = tiles["y"]
         both = staged("both", [P, T], F32, after="p10")

@@ -27,7 +27,6 @@ HALF = 2 * PAIR
 SPARE = 16
 BANK = C // 2
 RUN = 2
-LINE = 4
 ENTRIES = 16
 W2_GROUP = 4
 MX_ALIGN = 64
@@ -68,6 +67,10 @@ def tile_moe_pre_mlp_relu_kernel(tc, xT, w1, w2, gate, offs, pos1, pos2, out):
             tiles[key] = ring.tile(shape, dtype, name=key, offset=place[key], align_bytes=MX_ALIGN)
             return tiles[key]
 
+        def reserve(key, kib):
+            place[key] = place["free"]
+            place["free"] += kib * 1024
+
         def in_bank(key, shape, after=None):
             place[key] = place.pop(after) if after else "bank_" + key
             return psum.tile(shape, F32, name="bank", tag=place[key])
@@ -80,11 +83,6 @@ def tile_moe_pre_mlp_relu_kernel(tc, xT, w1, w2, gate, offs, pos1, pos2, out):
             nc.sync.dma_start(tiles["p%d%d" % (g, t)][:, :T], x_rows[g, t])
 
         def load_w1(e, g, after=None):
-            if g == 0:
-                staged("w%d" % e, [P, PASSES, PACK, H], F32, after)
-            nc.sync.dma_start(tiles["w%d" % e][:, g], w1_rows[e, g])
-
-        def load_w1_pass(e, g, after=None):
             nc.sync.dma_start(staged("w%d%d" % (e, g), [P, PACK, H], F32, after)[:], w1_rows[e, g])
 
         def load_w2(group, after=None):
@@ -117,11 +115,11 @@ def tile_moe_pre_mlp_relu_kernel(tc, xT, w1, w2, gate, offs, pos1, pos2, out):
         def open_batch(g, pair0, pair1, after=None):
             tile = staged("g%d%d" % (g, pair0), [P, PACK, (pair1 - pair0) * PAIR], F32, after)
             for pair in range(pair0, pair1):
-                batches[g, pair] = (tile, pair0, pair1)
+                batches[g, pair] = (tile, pair0)
 
-        def gather(copy, g, pair, t):
-            tile, pair0, pair1 = batches[g, pair]
-            copy(tile[:, t, :],
+        def gather(copy, g, t, pair0, pair1):
+            tile, first = batches[g, pair0]
+            copy(tile[:, t, (pair0 - first) * PAIR:(pair1 - first) * PAIR],
                  tiles["p%d%d" % (g, t)][:].indirect(offs_sb[:, pair0 * PAIR // ENTRIES:pair1 * PAIR // ENTRIES]))
 
         def pick_on_scalar(dst, src):
@@ -129,31 +127,28 @@ def tile_moe_pre_mlp_relu_kernel(tc, xT, w1, w2, gate, offs, pos1, pos2, out):
 
         def times_gate(g, pair, after=None):
             dst = staged("x%d%d" % (g, pair), [P, PAIR * PACK], BF16, after)
-            tile, pair0, pair1 = batches[g, pair]
-            src = tile[:, :, (pair - pair0) * PAIR:(pair - pair0 + 1) * PAIR]
-            weights = gates[pair][:].rearrange("p (c i) -> p c i", i=LINE)
-            nc.vector.tensor_tensor(dst[:].rearrange("p (c i t) -> p c t i", i=LINE, t=PACK),
-                                    src.rearrange("p t (c i) -> p c t i", i=LINE),
-                                    weights.unsqueeze(2).to_broadcast([P, PAIR // LINE, PACK, LINE]), MULT)
+            tile, first = batches[g, pair]
+            src = tile[:, :, (pair - first) * PAIR:(pair - first + 1) * PAIR]
+            weights = gates[pair][:].rearrange("p (c i) -> p c i", i=RUN)
+            nc.vector.tensor_tensor(dst[:].rearrange("p (c i t) -> p c t i", i=RUN, t=PACK),
+                                    src.rearrange("p t (c i) -> p c t i", i=RUN),
+                                    weights.unsqueeze(2).to_broadcast([P, PAIR // RUN, PACK, RUN]), MULT)
 
         def round_w1(copy, e, g, after=None):
             dst = staged("r%d%d" % (e, g), [P, H * PACK], BF16, after)
             copy(dst[:].rearrange("p (t u r j) -> p u t j r", t=PACK, r=2, j=PACK),
                  tiles["w%d%d" % (e, g)][:].rearrange("p j (u t r) -> p u t j r", t=PACK, r=2))
 
-        def round_w1_gpsimd(e, after=None, passes=(slice(0, PASSES),)):
-            dst = staged("r%d" % e, [P, PASSES * H * PACK], BF16, after)
-            for g in passes:
-                nc.gpsimd.tensor_scalar(dst[:].rearrange("p (t g q j) -> p g q t j", t=PACK, g=PASSES, j=PACK)[:, g],
-                                        tiles["w%d" % e][:].rearrange("p g j (q t) -> p g q t j", t=PACK)[:, g],
-                                        1.0, 0.0, MULT, ADD)
+        def round_w1_gpsimd(e, g, after=None):
+            dst = staged("r%d%d" % (e, g), [P, H * PACK], BF16, after)
+            nc.gpsimd.tensor_scalar(dst[:].rearrange("p (t q j) -> p q t j", t=PACK, j=PACK),
+                                    tiles["w%d%d" % (e, g)][:].rearrange("p j (q t) -> p q t j", t=PACK),
+                                    1.0, 0.0, MULT, ADD)
 
-        def open_w2(group, after):
-            staged("s%d" % group, [P, W2_GROUP * N * PACK], BF16, after)
-
-        def round_w2(copy, group, pattern, experts=slice(0, W2_GROUP)):
-            copy(tiles["s%d" % group][:].rearrange("p (e c i t) -> p e c t i", e=W2_GROUP, i=RUN, t=PACK)[:, experts],
-                 tiles["v%d" % group][:].rearrange(pattern + " (c i) -> p e c t i", i=RUN)[:, experts])
+        def round_w2(copy, group, pattern, after):
+            dst = staged("s%d" % group, [P, W2_GROUP * N * PACK], BF16, after)
+            copy(dst[:].rearrange("p (e c i t) -> p e c t i", e=W2_GROUP, i=RUN, t=PACK),
+                 tiles["v%d" % group][:].rearrange(pattern + " (c i) -> p e c t i", i=RUN))
 
         def quantize(key, after=None, scales_after=None):
             source = tiles[key]
@@ -186,8 +181,7 @@ def tile_moe_pre_mlp_relu_kernel(tc, xT, w1, w2, gate, offs, pos1, pos2, out):
                 bank = in_bank("a%d%d" % (e, b), [P, PACK, BANK], banks_after[b])
                 for g in range(PASSES):
                     for t in range(PACK):
-                        left, l0 = ("r%d" % e, (t * PASSES + g) * P) if "r%d" % e in tiles else ("r%d%d" % (e, g), t * P)
-                        matmul(bank[:, t, :], left, l0, "x%d%d" % (g, e // 2),
+                        matmul(bank[:, t, :], "r%d%d" % (e, g), t * P, "x%d%d" % (g, e // 2),
                                e % 2 * C + b * BANK, BANK, g == 0 and t == 0, g == PASSES - 1 and t == PACK - 1)
                 c0 = ((e - h_first[e]) * C + b * BANK) * PACK
                 relus[b % len(relus)](h_bf[:, c0:c0 + BANK * PACK].rearrange("p (s t) -> p s t", t=PACK),
@@ -211,105 +205,113 @@ def tile_moe_pre_mlp_relu_kernel(tc, xT, w1, w2, gate, offs, pos1, pos2, out):
         load_plane(0, 3)
         load_w1(0, 1)
         load_plane(1, 0)
+        reserve("before_w10", 2)
         load_w1(1, 0)
-        open_batch(0, 2, 4)
+        reserve("behind_w10", 6)
         for t in range(1, PACK):
             load_plane(1, t)
         load_w1(1, 1)
-        for g in range(PASSES):
-            load_w1(2, g)
-        for e in (4, 5):
-            for g in range(PASSES):
-                load_w1_pass(e, g)
-        for g in range(PASSES):
-            load_w1(3, g)
+        load_w1(4, 0)
+        reserve("before_w20", 4)
+        load_w1(2, 0)
+        open_batch(0, 2, 4)
+        for e, g in ((2, 1), (3, 0), (4, 1), (5, 0), (5, 1), (3, 1)):
+            load_w1(e, g)
 
         open_batch(0, 0, 2)
         open_batch(1, 0, 2)
         for t in range(PACK):
-            gather(on_vector, 0, 2, t)
-            gather(pick_on_scalar, 0, 0, t)
-        round_w1_gpsimd(0, passes=range(PASSES))
-        times_gate(0, 2)
+            gather(on_vector, 0, t, 2, 4)
+            gather(pick_on_scalar, 0, t, 0, 2)
+        round_w1_gpsimd(0, 0)
+        round_w1_gpsimd(0, 1)
+        round_w1_gpsimd(1, 0, after="w00")
+        times_gate(0, 2, after="before_w20")
         times_gate(0, 3)
         for t in range(PACK):
-            gather(pick_on_scalar, 1, 0, t)
-        quantize("x02")
-        quantize("x03")
-        quantize("r0")
+            gather(pick_on_scalar, 1, t, 0, 2)
+        quantize("x02", after=("w00", 4))
+        quantize("x03", after=("w00", 6))
+        quantize("r00", after="w01")
+        quantize("r01", after=("w01", 2))
+        quantize("r10")
 
-        round_w1_gpsimd(1, after="r0", passes=range(PASSES))
-        times_gate(0, 0, after="w0")
-        times_gate(0, 1, after=("w0", 4))
-        open_batch(1, 2, 3, after="g00")
+        round_w1_gpsimd(1, 1, after="r10")
+        round_w1_gpsimd(2, 0, after="w11")
+        times_gate(0, 0, after=("w10", -2))
+        times_gate(0, 1, after=("w10", 2))
+        open_batch(1, 2, 3, after=("w10", 6))
         for t in range(PACK):
-            gather(on_vector if t < 2 else pick_on_scalar, 1, 2, t)
-        quantize("x00", after=("w1", 8))
-        quantize("x01", after=("w1", 10))
-        quantize("r1")
-
-        round_w1_gpsimd(2, after="r1")
-        open_batch(1, 3, 4, after=("w1", 12))
-        times_gate(1, 0, after="w1")
-        for t in range(PACK):
-            gather(on_vector if t < 2 else pick_on_scalar, 1, 3, t)
-        times_gate(1, 1, after=("w1", 4))
+            gather(on_vector if t < 2 else pick_on_scalar, 1, t, 2, 3)
         round_w1(on_scalar, 4, 0, after=("g00", 8))
+        quantize("x00", after=("w11", 4))
+        quantize("x01", after=("w11", 6))
+        quantize("r11", after=("w01", 4))
+        quantize("r20")
+
+        round_w1_gpsimd(2, 1, after="r20")
+        round_w1_gpsimd(3, 0, after="w21")
+        open_batch(1, 3, 4, after=("w20", 6))
+        times_gate(1, 0, after=("w20", 2))
+        for t in range(PACK):
+            gather(on_vector if t < 2 else pick_on_scalar, 1, t, 3, 4)
+        times_gate(1, 1, after=("w20", -2))
         round_w1(on_scalar, 4, 1, after=("g00", 12))
         round_w1(on_scalar, 5, 0, after="w40")
         round_w1(on_scalar, 5, 1, after=("w40", 4))
-        quantize("x10", after=("w2", 8))
-        quantize("x11", after=("w2", 10))
-        quantize("r2")
-        load_w1_pass(6, 0, after=("g02", 8))
-        load_w1_pass(6, 1, after=("w0", 8))
-        load_w1_pass(7, 0, after="x02")
-        load_w1_pass(7, 1, after="w0")
-        load_w2(1, after="g10")
+        quantize("x10", after=("w21", 4))
+        quantize("x11", after=("w21", 6))
+        quantize("r21", after=("w01", 6))
+        quantize("r30")
+        load_w1(6, 0, after=("g02", 8))
+        load_w1(6, 1, after="r00")
+        load_w1(7, 0, after="g00")
+        load_w1(7, 1, after="g10")
         load_w2_runs(after=("g10", 8))
+        load_w2(1, after="w50")
         nc.sync.dma_start(pos1_sb[:], pos1)
         nc.sync.dma_start(pos2_sb[:], pos2)
 
-        round_w1_gpsimd(3, after="r2", passes=range(PASSES))
-        times_gate(1, 2, after="w2")
-        times_gate(1, 3, after=("w2", 4))
+        round_w1_gpsimd(3, 1, after="r30")
+        times_gate(1, 2, after="w30")
+        times_gate(1, 3, after=("w30", 4))
         open_h(0, 2, after="w51")
-        hidden(0, ["turned", None], relu_vector)
+        hidden(0, ["turned", None], relu_scalar)
         hidden(1, [None, None], relu_scalar)
         open_h(2, 3, after=("w51", 4))
         hidden(2, ["gate0", "gate1"], relu_scalar)
         round_w1(on_scalar, 6, 0, after="w41")
         round_w1(on_scalar, 6, 1, after=("w41", 4))
-        quantize("r3", after="codes_r0")
-        for n, key in enumerate(("x12", "r40", "r41", "r50", "r51", "x13", "r60", "h0")):
-            quantize(key, after=("w3", 2 * n))
+        for n, key in enumerate(("r31", "x12", "r40", "r41")):
+            quantize(key, after=("g12", 2 * n))
+        for n, key in enumerate(("r50", "r51", "x13", "h0")):
+            quantize(key, after=("g13", 2 * n))
         round_w1(on_scalar, 7, 0, after="w61")
         open_h(3, 5, after="w70")
         open_h(5, 6, after=("w70", 4))
         hidden(3, ["a00", "a01"], relu_scalar)
         hidden(4, ["a10", "a11"], relu_scalar)
         hidden(5, ["a20", "a21"], relu_scalar)
-        round_w1(on_vector, 7, 1, after="r40")
-        quantize("r61", after="x12")
+        quantize("r60", after="x12")
         quantize("h2", after=("x12", 2))
-        quantize("r70", after="x13")
-        open_w2(1, after="r70")
-        round_w2(on_scalar, 1, "p t e")
+        quantize("r61", after="x13")
+        quantize("r70", after=("x13", 2))
+        round_w1(on_vector, 7, 1, after="r40")
+        round_w2(on_scalar, 1, "p t e", after="r70")
         quantize("r71", after="r50")
         open_h(6, 8, after="v1")
         hidden(6, ["gate2", "gate3"], relu_scalar)
-        hidden(7, ["a30", "a31"], relu_scalar)
         quantize("h3", after="w71")
         quantize("h5", after=("w71", 2))
-        open_w2(0, after="r71")
-        round_w2(on_vector, 0, "p e t")
-        quantize("s1", after="v0")
+        round_w2(on_vector, 0, "p e t", after="r71")
         quantize("s0", after="h3")
-        quantize("h6", after=("v0", 2))
-        staged("y", [P, SLOTS], F32, after="w60")
-        second_layer(4, 6, "a40", on_scalar)
-        second_layer(0, 2, "a50", on_scalar)
+        quantize("s1", after="v0")
+        staged("y", [P, SLOTS], F32, after=("v1", 4))
         second_layer(2, 4, "a51", on_vector)
+        hidden(7, ["a30", "a31"], relu_scalar, relu_vector)
+        quantize("h6", after=("v0", 2))
+        second_layer(0, 2, "a50", on_scalar)
+        second_layer(4, 6, "a40", on_scalar)
         second_layer(6, 7, "a41", on_scalar)
         second_layer(7, 8, "a60", on_vector)
 

@@ -23,25 +23,27 @@ PACK = 4
 PASSES = K // (P * PACK)
 PAIR = 2 * C
 PAIRS = SLOTS // PAIR
-HALF = 2 * PAIR
-SPARE = 16
 BANK = C // 2
 RUN = 2
 ENTRIES = 16
-W2_GROUP = 4
+SPARE = 16
+GROUP = 4
 MX_ALIGN = 64
+WIDTH = {F32: 4, U32: 4, BF16: 2, U8: 1}
+VECTOR_PLANES = 2
+TOKEN_RANGES = ((0, 128), (128, 256), (256, 576), (576, 896), (896, T))
+VECTOR_RANGE = 1
+FIRST_STORE = 2
 
 FLOPS = 2 * SLOTS * (K * H + H * N)
 BYTES = 4 * (K * T + E * K * H + E * H * N + SLOTS + N * T) + 2 * P * (SLOTS + 2 * T) // ENTRIES
-WIDTH = {F32: 4, U32: 4, BF16: 2, U8: 1}
-TOKEN_PIECES = ((0, 128), (128, 320), (320, 640), (640, 896), (896, T))
 
 
 def tile_moe_pre_mlp_relu_kernel(tc, xT, w1, w2, gate, offs, pos1, pos2, out):
     nc = tc.nc
     with ExitStack() as ctx:
         keep = ctx.enter_context(tc.tile_pool(name="keep", bufs=1))
-        ring = ctx.enter_context(tc.tile_pool(name="ring", bufs=1))
+        stage = ctx.enter_context(tc.tile_pool(name="stage", bufs=1))
         psum = ctx.enter_context(tc.psum_pool(name="psum", bufs=1))
 
         offs_sb = keep.tile([P, SLOTS // ENTRIES], U16, name="offs_sb")
@@ -50,11 +52,17 @@ def tile_moe_pre_mlp_relu_kernel(tc, xT, w1, w2, gate, offs, pos1, pos2, out):
 
         x_rows = xT.rearrange("(g p t) n -> g t p n", g=PASSES, t=PACK)
         w1_rows = w1.rearrange("e (g p j) c -> e g p j c", g=PASSES, j=PACK)
-        w2_rows = w2.rearrange("e (u t r) n -> r t u e n", t=PACK, r=2)
         w2_runs = w2.rearrange("e (p t) n -> p e t n", t=PACK)
+        w2_rows = w2.rearrange("e (u t r) n -> r t u e n", t=PACK, r=2)
 
-        tiles, batches, gates, codes_of, h_first = {}, {}, {}, {}, {}
+        tiles, gates, codes_of = {}, {}, {}
+        batch_of, piece_at, h_first = {}, {}, {}
         place = {"free": 0}
+        bank_of = {}
+
+        def reserve(key, kib):
+            place[key] = place["free"]
+            place["free"] += kib * 1024
 
         def staged(key, shape, dtype, after=None):
             if after is None:
@@ -64,16 +72,12 @@ def tile_moe_pre_mlp_relu_kernel(tc, xT, w1, w2, gate, offs, pos1, pos2, out):
                 place[key] = place[after]
             else:
                 place[key] = place[after[0]] + after[1] * 1024
-            tiles[key] = ring.tile(shape, dtype, name=key, offset=place[key], align_bytes=MX_ALIGN)
+            tiles[key] = stage.tile(shape, dtype, name=key, offset=place[key], align_bytes=MX_ALIGN)
             return tiles[key]
 
-        def reserve(key, kib):
-            place[key] = place["free"]
-            place["free"] += kib * 1024
-
         def in_bank(key, shape, after=None):
-            place[key] = place.pop(after) if after else "bank_" + key
-            return psum.tile(shape, F32, name="bank", tag=place[key])
+            bank_of[key] = bank_of.pop(after) if after else key
+            return psum.tile(shape, F32, name="bank", tag=bank_of[key])
 
         for g in reversed(range(PASSES)):
             for t in reversed(range(PACK)):
@@ -85,14 +89,14 @@ def tile_moe_pre_mlp_relu_kernel(tc, xT, w1, w2, gate, offs, pos1, pos2, out):
         def load_w1(e, g, after=None):
             nc.sync.dma_start(staged("w%d%d" % (e, g), [P, PACK, H], F32, after)[:], w1_rows[e, g])
 
-        def load_w2(group, after=None):
-            raw = staged("v%d" % group, [P, PACK, W2_GROUP, N], F32, after)
+        def load_w2_low(after):
+            nc.sync.dma_start(staged("v0", [P, GROUP, PACK, N], F32, after)[:], w2_runs[:, :GROUP])
+
+        def load_w2_high(after):
+            raw = staged("v1", [P, PACK, GROUP, N], F32, after)
             for r in range(2):
                 for t in range(PACK):
-                    nc.sync.dma_start(raw[r:P:2, t], w2_rows[r, t][:, group * W2_GROUP:(group + 1) * W2_GROUP])
-
-        def load_w2_runs(after):
-            nc.sync.dma_start(staged("v0", [P, W2_GROUP, PACK, N], F32, after)[:], w2_runs[:, :W2_GROUP])
+                    nc.sync.dma_start(raw[r:P:2, t], w2_rows[r, t][:, GROUP:])
 
         def spread_gate():
             identity = keep.tile([P, P], F32, name="identity")
@@ -112,50 +116,71 @@ def tile_moe_pre_mlp_relu_kernel(tc, xT, w1, w2, gate, offs, pos1, pos2, out):
                     nc.tensor.transpose(gates[pair][:, c * P:(c + 1) * P],
                                         by_slot[:, column:column + 1].to_broadcast([P, P]), identity[:])
 
-        def open_batch(g, pair0, pair1, after=None):
-            tile = staged("g%d%d" % (g, pair0), [P, PACK, (pair1 - pair0) * PAIR], F32, after)
-            for pair in range(pair0, pair1):
-                batches[g, pair] = (tile, pair0)
+        def copy_vector(dst, src):
+            nc.vector.tensor_copy(dst, src)
 
-        def gather(copy, g, t, pair0, pair1):
-            tile, first = batches[g, pair0]
-            copy(tile[:, t, (pair0 - first) * PAIR:(pair1 - first) * PAIR],
-                 tiles["p%d%d" % (g, t)][:].indirect(offs_sb[:, pair0 * PAIR // ENTRIES:pair1 * PAIR // ENTRIES]))
+        def copy_scalar(dst, src):
+            nc.scalar.copy(dst, src)
 
-        def pick_on_scalar(dst, src):
+        def pick_scalar(dst, src):
             nc.scalar.activation(dst, src, COPY)
 
-        def times_gate(g, pair, after=None):
-            dst = staged("x%d%d" % (g, pair), [P, PAIR * PACK], BF16, after)
-            tile, first = batches[g, pair]
-            src = tile[:, :, (pair - first) * PAIR:(pair - first + 1) * PAIR]
+        def relu_scalar(dst, src):
+            nc.scalar.activation(dst, src, RELU)
+
+        def relu_vector(dst, src):
+            nc.vector.tensor_scalar_max(dst, src, 0.0)
+
+        def gather(g, pair0, pair1, vector_planes, after=None):
+            tile = staged("g%d%d" % (g, pair0), [P, PACK, (pair1 - pair0) * PAIR], F32, after)
+            entries = offs_sb[:, pair0 * PAIR // ENTRIES:pair1 * PAIR // ENTRIES]
+            for t in range(PACK):
+                pick = copy_vector if t < vector_planes else pick_scalar
+                pick(tile[:, t, :], tiles["p%d%d" % (g, t)][:].indirect(entries))
+            for pair in range(pair0, pair1):
+                batch_of[g, pair] = tile[:, :, (pair - pair0) * PAIR:(pair - pair0 + 1) * PAIR]
+
+        def open_x(g, half, after=None):
+            staged("x%d%d" % (g, half), [P, 2 * PAIR * PACK], BF16, after)
+
+        def times_gate(g, pair):
+            dst = tiles["x%d%d" % (g, pair // 2)][:, pair % 2 * PAIR * PACK:(pair % 2 + 1) * PAIR * PACK]
             weights = gates[pair][:].rearrange("p (c i) -> p c i", i=RUN)
-            nc.vector.tensor_tensor(dst[:].rearrange("p (c i t) -> p c t i", i=RUN, t=PACK),
-                                    src.rearrange("p t (c i) -> p c t i", i=RUN),
+            nc.vector.tensor_tensor(dst.rearrange("p (c i t) -> p c t i", i=RUN, t=PACK),
+                                    batch_of[g, pair].rearrange("p t (c i) -> p c t i", i=RUN),
                                     weights.unsqueeze(2).to_broadcast([P, PAIR // RUN, PACK, RUN]), MULT)
 
-        def round_w1(copy, e, g, after=None):
-            dst = staged("r%d%d" % (e, g), [P, H * PACK], BF16, after)
-            copy(dst[:].rearrange("p (t u r j) -> p u t j r", t=PACK, r=2, j=PACK),
+        def open_pieces(pieces, after=None):
+            key = "r%d%d" % pieces[0]
+            staged(key, [P, len(pieces) * H * PACK], BF16, after)
+            for n, piece in enumerate(pieces):
+                piece_at[piece] = (key, n * H)
+
+        def rounded(e, g):
+            key, c0 = piece_at[e, g]
+            return tiles[key][:, c0 * PACK:(c0 + H) * PACK]
+
+        def round_w1_gpsimd(pieces, after=None):
+            open_pieces(pieces, after)
+            for e, g in pieces:
+                nc.gpsimd.tensor_scalar(rounded(e, g).rearrange("p (t q j) -> p q t j", t=PACK, j=PACK),
+                                        tiles["w%d%d" % (e, g)][:].rearrange("p j (q t) -> p q t j", t=PACK),
+                                        1.0, 0.0, MULT, ADD)
+
+        def round_w1(copy, e, g):
+            copy(rounded(e, g).rearrange("p (t u r j) -> p u t j r", t=PACK, r=2, j=PACK),
                  tiles["w%d%d" % (e, g)][:].rearrange("p j (u t r) -> p u t j r", t=PACK, r=2))
 
-        def round_w1_gpsimd(e, g, after=None):
-            dst = staged("r%d%d" % (e, g), [P, H * PACK], BF16, after)
-            nc.gpsimd.tensor_scalar(dst[:].rearrange("p (t q j) -> p q t j", t=PACK, j=PACK),
-                                    tiles["w%d%d" % (e, g)][:].rearrange("p j (q t) -> p q t j", t=PACK),
-                                    1.0, 0.0, MULT, ADD)
+        def round_w2(copy, group, raw_order, after):
+            dst = staged("s%d" % group, [P, GROUP * N * PACK], BF16, after)
+            copy(dst[:].rearrange("p (e c i t) -> p e c t i", e=GROUP, i=RUN, t=PACK),
+                 tiles["v%d" % group][:].rearrange(raw_order + " (c i) -> p e c t i", i=RUN))
 
-        def round_w2(copy, group, pattern, after):
-            dst = staged("s%d" % group, [P, W2_GROUP * N * PACK], BF16, after)
-            copy(dst[:].rearrange("p (e c i t) -> p e c t i", e=W2_GROUP, i=RUN, t=PACK),
-                 tiles["v%d" % group][:].rearrange(pattern + " (c i) -> p e c t i", i=RUN))
-
-        def quantize(key, after=None, scales_after=None):
-            source = tiles[key]
-            width = source.shape[1] // PACK
+        def quantize(key, after=None):
+            width = tiles[key].shape[1] // PACK
             codes = staged("codes_" + key, [P, width], U32, after)
-            scales = staged("scales_" + key, [P, width], U8, scales_after)
-            nc.vector.quantize_mx(out=codes[:].bitcast(FP8X4), scales=scales[:], in_=source[:])
+            scales = staged("scales_" + key, [P, width], U8)
+            nc.vector.quantize_mx(out=codes[:].bitcast(FP8X4), scales=scales[:], in_=tiles[key][:])
             codes_of[key] = (codes, scales)
 
         def matmul(dst, left, l0, right, r0, width, start, stop):
@@ -164,37 +189,30 @@ def tile_moe_pre_mlp_relu_kernel(tc, xT, w1, w2, gate, offs, pos1, pos2, out):
                                 rhs=r_codes[:, r0:r0 + width].bitcast(FP8X4), rhs_scale=r_scales[:, r0:r0 + width],
                                 start=start, stop=stop)
 
-        def relu_scalar(dst, src):
-            nc.scalar.activation(dst, src, RELU)
-
-        def relu_vector(dst, src):
-            nc.vector.tensor_scalar_max(dst, src, 0.0)
-
-        def open_h(e0, e1, after=None):
+        def open_h(e0, e1, after):
             staged("h%d" % e0, [P, (e1 - e0) * C * PACK], BF16, after)
             for e in range(e0, e1):
                 h_first[e] = e0
 
-        def hidden(e, banks_after, *relus):
-            h_bf = tiles["h%d" % h_first[e]]
+        def hidden(e, banks_after, relus=(relu_scalar, relu_scalar)):
             for b in range(C // BANK):
                 bank = in_bank("a%d%d" % (e, b), [P, PACK, BANK], banks_after[b])
                 for g in range(PASSES):
+                    key, c0 = piece_at[e, g]
                     for t in range(PACK):
-                        matmul(bank[:, t, :], "r%d%d" % (e, g), t * P, "x%d%d" % (g, e // 2),
-                               e % 2 * C + b * BANK, BANK, g == 0 and t == 0, g == PASSES - 1 and t == PACK - 1)
-                c0 = ((e - h_first[e]) * C + b * BANK) * PACK
-                relus[b % len(relus)](h_bf[:, c0:c0 + BANK * PACK].rearrange("p (s t) -> p s t", t=PACK),
-                                      bank[:].rearrange("p t s -> p s t"))
+                        matmul(bank[:, t, :], key, c0 + t * P, "x%d%d" % (g, e // GROUP), e % GROUP * C + b * BANK, BANK,
+                               g == 0 and t == 0, g == PASSES - 1 and t == PACK - 1)
+                s0 = (e - h_first[e]) * C + b * BANK
+                relus[b](tiles["h%d" % h_first[e]][:, s0 * PACK:(s0 + BANK) * PACK].rearrange("p (s t) -> p s t", t=PACK),
+                         bank[:].rearrange("p t s -> p s t"))
 
-        def second_layer(e0, e1, bank_after, copy):
-            bank = in_bank("y%d" % e0, [P, (e1 - e0) * C], bank_after)
-            for e in range(e0, e1):
-                matmul(bank[:, (e - e0) * C:(e - e0 + 1) * C], "s%d" % (e // W2_GROUP), e % W2_GROUP * N,
-                       "h%d" % h_first[e], (e - h_first[e]) * C, C, True, True)
-            copy(tiles["y"][:, e0 * C:e1 * C], bank[:])
-
-        on_vector, on_scalar = nc.vector.tensor_copy, nc.scalar.copy
+        def second_layer(s0, s1, bank_after, copy):
+            bank = in_bank("y%d" % s0, [P, s1 - s0], bank_after)
+            for a in range(s0, s1, C):
+                e, width = a // C, min(C, s1 - a)
+                matmul(bank[:, a - s0:a - s0 + width], "s%d" % (e // GROUP), e % GROUP * N,
+                       "h%d" % h_first[e], a - h_first[e] * C, width, True, True)
+            copy(tiles["y"][:, s0:s1], bank[:])
 
         nc.sync.dma_start(offs_sb[:], offs)
         load_plane(0, 0)
@@ -205,125 +223,124 @@ def tile_moe_pre_mlp_relu_kernel(tc, xT, w1, w2, gate, offs, pos1, pos2, out):
         load_plane(0, 3)
         load_w1(0, 1)
         load_plane(1, 0)
-        reserve("before_w10", 2)
         load_w1(1, 0)
-        reserve("behind_w10", 6)
+        reserve("behind_w10", 2)
         for t in range(1, PACK):
             load_plane(1, t)
         load_w1(1, 1)
+        reserve("w20", 8 + 6)
         load_w1(4, 0)
-        reserve("before_w20", 4)
-        load_w1(2, 0)
-        open_batch(0, 2, 4)
-        for e, g in ((2, 1), (3, 0), (4, 1), (5, 0), (5, 1), (3, 1)):
+        load_w1(2, 0, after="w20")
+        load_w1(2, 1)
+        reserve("w30", 8)
+        load_w1(4, 1)
+        load_w1(3, 0, after="w30")
+        for e, g in ((5, 0), (5, 1), (3, 1)):
             load_w1(e, g)
 
-        open_batch(0, 0, 2)
-        open_batch(1, 0, 2)
-        for t in range(PACK):
-            gather(on_vector, 0, t, 2, 4)
-            gather(pick_on_scalar, 0, t, 0, 2)
-        round_w1_gpsimd(0, 0)
-        round_w1_gpsimd(0, 1)
-        round_w1_gpsimd(1, 0, after="w00")
-        times_gate(0, 2, after="before_w20")
+        gather(0, 2, 4, PACK)
+        gather(0, 0, 2, 0)
+        gather(1, 0, 2, 0)
+        round_w1_gpsimd([(0, 0), (0, 1)])
+        round_w1_gpsimd([(1, 0)])
+        open_x(0, 1, after="w00")
+        times_gate(0, 2)
         times_gate(0, 3)
-        for t in range(PACK):
-            gather(pick_on_scalar, 1, t, 0, 2)
-        quantize("x02", after=("w00", 4))
-        quantize("x03", after=("w00", 6))
-        quantize("r00", after="w01")
-        quantize("r01", after=("w01", 2))
+        quantize("r00")
+        quantize("x01")
         quantize("r10")
 
-        round_w1_gpsimd(1, 1, after="r10")
-        round_w1_gpsimd(2, 0, after="w11")
-        times_gate(0, 0, after=("w10", -2))
-        times_gate(0, 1, after=("w10", 2))
-        open_batch(1, 2, 3, after=("w10", 6))
-        for t in range(PACK):
-            gather(on_vector if t < 2 else pick_on_scalar, 1, t, 2, 3)
-        round_w1(on_scalar, 4, 0, after=("g00", 8))
-        quantize("x00", after=("w11", 4))
-        quantize("x01", after=("w11", 6))
-        quantize("r11", after=("w01", 4))
-        quantize("r20")
+        round_w1_gpsimd([(1, 1), (2, 0)], after=("r10", -4))
+        open_x(0, 0, after=("w10", 2))
+        times_gate(0, 0)
+        times_gate(0, 1)
+        gather(1, 2, 3, VECTOR_PLANES, after=("w10", -6))
+        open_pieces([(4, 0), (4, 1)], after="g00")
+        round_w1(copy_scalar, 4, 0)
+        quantize("x00", after=("w20", 2))
+        quantize("r11", after="r00")
 
-        round_w1_gpsimd(2, 1, after="r20")
-        round_w1_gpsimd(3, 0, after="w21")
-        open_batch(1, 3, 4, after=("w20", 6))
-        times_gate(1, 0, after=("w20", 2))
-        for t in range(PACK):
-            gather(on_vector if t < 2 else pick_on_scalar, 1, t, 3, 4)
-        times_gate(1, 1, after=("w20", -2))
-        round_w1(on_scalar, 4, 1, after=("g00", 12))
-        round_w1(on_scalar, 5, 0, after="w40")
-        round_w1(on_scalar, 5, 1, after=("w40", 4))
-        quantize("x10", after=("w21", 4))
-        quantize("x11", after=("w21", 6))
-        quantize("r21", after=("w01", 6))
-        quantize("r30")
-        load_w1(6, 0, after=("g02", 8))
-        load_w1(6, 1, after="r00")
-        load_w1(7, 0, after="g00")
-        load_w1(7, 1, after="g10")
-        load_w2_runs(after=("g10", 8))
-        load_w2(1, after="w50")
+        round_w1_gpsimd([(2, 1), (3, 0)], after="r11")
+        open_x(1, 0, after=("w20", -6))
+        times_gate(1, 0)
+        times_gate(1, 1)
+        gather(1, 3, 4, VECTOR_PLANES, after=("w20", 6))
+        round_w1(copy_scalar, 4, 1)
+        open_pieces([(5, 0), (5, 1)], after="w40")
+        round_w1(copy_scalar, 5, 0)
+        round_w1(copy_scalar, 5, 1)
+        quantize("x10")
+        quantize("r21")
+        load_w1(6, 0, after="g02")
+        load_w1(6, 1, after=("g02", 8))
+        load_w1(7, 0, after=("g00", 8))
+        load_w1(7, 1, after=("g10", 8))
+        load_w2_low(after="x01")
+        load_w2_high(after="w50")
         nc.sync.dma_start(pos1_sb[:], pos1)
         nc.sync.dma_start(pos2_sb[:], pos2)
 
-        round_w1_gpsimd(3, 1, after="r30")
-        times_gate(1, 2, after="w30")
-        times_gate(1, 3, after=("w30", 4))
+        round_w1_gpsimd([(3, 1)], after="r21")
+        open_x(1, 1, after=("w30", -6))
+        times_gate(1, 2)
+        times_gate(1, 3)
         open_h(0, 2, after="w51")
-        hidden(0, ["turned", None], relu_scalar)
-        hidden(1, [None, None], relu_scalar)
         open_h(2, 3, after=("w51", 4))
-        hidden(2, ["gate0", "gate1"], relu_scalar)
-        round_w1(on_scalar, 6, 0, after="w41")
-        round_w1(on_scalar, 6, 1, after=("w41", 4))
-        for n, key in enumerate(("r31", "x12", "r40", "r41")):
-            quantize(key, after=("g12", 2 * n))
-        for n, key in enumerate(("r50", "r51", "x13", "h0")):
-            quantize(key, after=("g13", 2 * n))
-        round_w1(on_scalar, 7, 0, after="w61")
+        hidden(0, ("turned", None))
+        hidden(1, (None, None))
+        hidden(2, ("gate0", "gate1"))
+        open_pieces([(6, 0), (6, 1)], after="w41")
+        round_w1(copy_scalar, 6, 0)
+        round_w1(copy_scalar, 6, 1)
+        open_pieces([(7, 0)], after="w61")
+        round_w1(copy_scalar, 7, 0)
+
+        quantize("r40", after="g12")
+        quantize("x11", after="g10")
+        quantize("r31", after=("g12", 4))
+        quantize("r50", after="g13")
+        quantize("h0", after=("g13", 4))
+        quantize("h2", after=("g13", 6))
         open_h(3, 5, after="w70")
         open_h(5, 6, after=("w70", 4))
-        hidden(3, ["a00", "a01"], relu_scalar)
-        hidden(4, ["a10", "a11"], relu_scalar)
-        hidden(5, ["a20", "a21"], relu_scalar)
-        quantize("r60", after="x12")
-        quantize("h2", after=("x12", 2))
-        quantize("r61", after="x13")
-        quantize("r70", after=("x13", 2))
-        round_w1(on_vector, 7, 1, after="r40")
-        round_w2(on_scalar, 1, "p t e", after="r70")
-        quantize("r71", after="r50")
-        open_h(6, 8, after="v1")
-        hidden(6, ["gate2", "gate3"], relu_scalar)
+        hidden(3, ("a00", "a01"))
+        hidden(4, ("a10", "a11"))
+        hidden(5, ("a20", "a21"))
+        quantize("r60", after="x11")
+        quantize("r70", after=("x11", 4))
+        open_pieces([(7, 1)], after="r50")
+        round_w1(copy_vector, 7, 1)
+        round_w2(copy_scalar, 1, "p t e", after="r70")
+        quantize("r71", after=("r50", 4))
+        open_h(6, 7, after="v1")
+        open_h(7, 8, after=("v1", 2))
+        hidden(6, ("gate2", "gate3"))
         quantize("h3", after="w71")
         quantize("h5", after=("w71", 2))
-        round_w2(on_vector, 0, "p e t", after="r71")
+        round_w2(copy_vector, 0, "p e t", after="r71")
         quantize("s0", after="h3")
         quantize("s1", after="v0")
         staged("y", [P, SLOTS], F32, after=("v1", 4))
-        second_layer(2, 4, "a51", on_vector)
-        hidden(7, ["a30", "a31"], relu_scalar, relu_vector)
+        second_layer(2 * C, 4 * C, "a51", copy_vector)
+        hidden(7, ("a30", "a31"), (relu_scalar, relu_vector))
         quantize("h6", after=("v0", 2))
-        second_layer(0, 2, "a50", on_scalar)
-        second_layer(4, 6, "a40", on_scalar)
-        second_layer(6, 7, "a41", on_scalar)
-        second_layer(7, 8, "a60", on_vector)
+        quantize("h7", after=("v0", 3))
+        second_layer(0, 2 * C, "a50", copy_scalar)
+        second_layer(4 * C, 6 * C, "a40", copy_scalar)
+        second_layer(6 * C, 7 * C, "a41", copy_scalar)
+        second_layer(7 * C, 7 * C + BANK, "a60", copy_vector)
+        second_layer(7 * C + BANK, SLOTS, "a61", copy_scalar)
 
         y_sb = tiles["y"]
         both = staged("both", [P, T], F32, after="p10")
-        for n, (t0, t1) in enumerate(TOKEN_PIECES):
-            first = staged("first%d" % t0, [P, t1 - t0], F32, after="p0%d" % n if n < PACK else "p11")
-            (on_vector if n == 1 else pick_on_scalar)(first[:], y_sb[:].indirect(pos1_sb[:, t0 // ENTRIES:t1 // ENTRIES]))
+        first = staged("first", [P, T], F32, after="p00")
+        for n, (t0, t1) in enumerate(TOKEN_RANGES):
+            pick = copy_vector if n == VECTOR_RANGE else pick_scalar
+            pick(first[:, t0:t1], y_sb[:].indirect(pos1_sb[:, t0 // ENTRIES:t1 // ENTRIES]))
         stored = 0
-        for n, (t0, t1) in enumerate(TOKEN_PIECES):
+        for n, (t0, t1) in enumerate(TOKEN_RANGES):
             nc.vector.tensor_tensor(both[:, t0:t1], y_sb[:].indirect(pos2_sb[:, t0 // ENTRIES:t1 // ENTRIES]),
-                                    tiles["first%d" % t0][:], ADD)
-            if n >= 2:
+                                    first[:, t0:t1], ADD)
+            if n >= FIRST_STORE:
                 nc.sync.dma_start(out[:, stored:t1], both[:, stored:t1])
                 stored = t1

@@ -56,7 +56,7 @@ def tile_moe_pre_mlp_relu_kernel(tc, xT, w1, w2, gate, offs, pos1, pos2, out):
         w2_rows = w2.rearrange("e (u t r) n -> r t u e n", t=PACK, r=2)
 
         tiles, gates, codes_of = {}, {}, {}
-        batch_of, piece_at, h_first = {}, {}, {}
+        batch_of, x_at, piece_at, h_first = {}, {}, {}, {}
         place = {"free": 0}
         bank_of = {}
 
@@ -79,9 +79,10 @@ def tile_moe_pre_mlp_relu_kernel(tc, xT, w1, w2, gate, offs, pos1, pos2, out):
             bank_of[key] = bank_of.pop(after) if after else key
             return psum.tile(shape, F32, name="bank", tag=bank_of[key])
 
-        for g in reversed(range(PASSES)):
-            for t in reversed(range(PACK)):
-                nc.gpsimd.memset(staged("p%d%d" % (g, t), [P, T + SPARE], F32)[:, T:], 0.0)
+        planes = [staged("p%d%d" % (g, t), [P, T + SPARE], F32) for g in range(PASSES) for t in range(PACK)]
+        for plane in reversed(planes[1:]):
+            nc.gpsimd.memset(plane[:, T:], 0.0)
+        nc.scalar.activation(planes[0][:, T:], planes[-1][:, T:], COPY)
 
         def load_plane(g, t):
             nc.sync.dma_start(tiles["p%d%d" % (g, t)][:, :T], x_rows[g, t])
@@ -140,11 +141,15 @@ def tile_moe_pre_mlp_relu_kernel(tc, xT, w1, w2, gate, offs, pos1, pos2, out):
             for pair in range(pair0, pair1):
                 batch_of[g, pair] = tile[:, :, (pair - pair0) * PAIR:(pair - pair0 + 1) * PAIR]
 
-        def open_x(g, half, after=None):
-            staged("x%d%d" % (g, half), [P, 2 * PAIR * PACK], BF16, after)
+        def open_x(parts, after):
+            key = "x%d%d" % parts[0]
+            staged(key, [P, len(parts) * PAIR * PACK], BF16, after)
+            for n, part in enumerate(parts):
+                x_at[part] = (key, n * PAIR)
 
         def times_gate(g, pair):
-            dst = tiles["x%d%d" % (g, pair // 2)][:, pair % 2 * PAIR * PACK:(pair % 2 + 1) * PAIR * PACK]
+            key, s0 = x_at[g, pair]
+            dst = tiles[key][:, s0 * PACK:(s0 + PAIR) * PACK]
             weights = gates[pair][:].rearrange("p (c i) -> p c i", i=RUN)
             nc.vector.tensor_tensor(dst.rearrange("p (c i t) -> p c t i", i=RUN, t=PACK),
                                     batch_of[g, pair].rearrange("p t (c i) -> p c t i", i=RUN),
@@ -198,9 +203,9 @@ def tile_moe_pre_mlp_relu_kernel(tc, xT, w1, w2, gate, offs, pos1, pos2, out):
             for b in range(C // BANK):
                 bank = in_bank("a%d%d" % (e, b), [P, PACK, BANK], banks_after[b])
                 for g in range(PASSES):
-                    key, c0 = piece_at[e, g]
+                    (w_key, c0), (x_key, x0) = piece_at[e, g], x_at[g, e // 2]
                     for t in range(PACK):
-                        matmul(bank[:, t, :], key, c0 + t * P, "x%d%d" % (g, e // GROUP), e % GROUP * C + b * BANK, BANK,
+                        matmul(bank[:, t, :], w_key, c0 + t * P, x_key, x0 + e % 2 * C + b * BANK, BANK,
                                g == 0 and t == 0, g == PASSES - 1 and t == PACK - 1)
                 s0 = (e - h_first[e]) * C + b * BANK
                 relus[b](tiles["h%d" % h_first[e]][:, s0 * PACK:(s0 + BANK) * PACK].rearrange("p (s t) -> p s t", t=PACK),
@@ -243,60 +248,60 @@ def tile_moe_pre_mlp_relu_kernel(tc, xT, w1, w2, gate, offs, pos1, pos2, out):
         gather(1, 0, 2, 0)
         round_w1_gpsimd([(0, 0), (0, 1)])
         round_w1_gpsimd([(1, 0)])
-        open_x(0, 1, after="w00")
+        open_x([(0, 2), (0, 3)], after="w00")
         times_gate(0, 2)
         times_gate(0, 3)
         quantize("r00")
-        quantize("x01")
+        quantize("x02")
         quantize("r10")
 
         round_w1_gpsimd([(1, 1), (2, 0)], after=("r10", -4))
-        open_x(0, 0, after=("w10", 2))
+        open_x([(0, 0), (1, 0)], after=("w10", 2))
         times_gate(0, 0)
-        times_gate(0, 1)
         gather(1, 2, 3, VECTOR_PLANES, after=("w10", -6))
-        open_pieces([(4, 0), (4, 1)], after="g00")
+        times_gate(1, 0)
+        open_pieces([(4, 0), (4, 1)], after="g02")
         round_w1(copy_scalar, 4, 0)
         quantize("x00", after=("w20", 2))
         quantize("r11", after="r00")
 
         round_w1_gpsimd([(2, 1), (3, 0)], after="r11")
-        open_x(1, 0, after=("w20", -6))
-        times_gate(1, 0)
+        open_x([(0, 1), (1, 1)], after=("w20", -6))
+        times_gate(0, 1)
         times_gate(1, 1)
-        gather(1, 3, 4, VECTOR_PLANES, after=("w20", 6))
+        gather(1, 3, 4, 1, after=("w20", 6))
         round_w1(copy_scalar, 4, 1)
+        open_h(0, 2, after="w41")
+        hidden(0, ("turned", None))
+        hidden(1, (None, None))
         open_pieces([(5, 0), (5, 1)], after="w40")
         round_w1(copy_scalar, 5, 0)
         round_w1(copy_scalar, 5, 1)
-        quantize("x10")
+        quantize("x01")
         quantize("r21")
-        load_w1(6, 0, after="g02")
-        load_w1(6, 1, after=("g02", 8))
-        load_w1(7, 0, after=("g00", 8))
-        load_w1(7, 1, after=("g10", 8))
-        load_w2_low(after="x01")
+        load_w1(6, 0, after=("g02", 8))
+        load_w1(6, 1, after="x02")
+        load_w1(7, 0, after="g00")
+        load_w1(7, 1, after=("g00", 8))
+        load_w2_low(after=("g10", 8))
         load_w2_high(after="w50")
         nc.sync.dma_start(pos1_sb[:], pos1)
         nc.sync.dma_start(pos2_sb[:], pos2)
 
         round_w1_gpsimd([(3, 1)], after="r21")
-        open_x(1, 1, after=("w30", -6))
+        open_x([(1, 2), (1, 3)], after=("w30", -6))
         times_gate(1, 2)
         times_gate(1, 3)
-        open_h(0, 2, after="w51")
-        open_h(2, 3, after=("w51", 4))
-        hidden(0, ("turned", None))
-        hidden(1, (None, None))
-        hidden(2, ("gate0", "gate1"))
-        open_pieces([(6, 0), (6, 1)], after="w41")
+        open_pieces([(6, 0), (6, 1)], after="x00")
         round_w1(copy_scalar, 6, 0)
+        open_h(2, 3, after="w60")
+        hidden(2, ("gate0", "gate1"))
         round_w1(copy_scalar, 6, 1)
         open_pieces([(7, 0)], after="w61")
         round_w1(copy_scalar, 7, 0)
 
         quantize("r40", after="g12")
-        quantize("x11", after="g10")
+        quantize("x12", after="g10")
         quantize("r31", after=("g12", 4))
         quantize("r50", after="g13")
         quantize("h0", after=("g13", 4))
@@ -306,8 +311,8 @@ def tile_moe_pre_mlp_relu_kernel(tc, xT, w1, w2, gate, offs, pos1, pos2, out):
         hidden(3, ("a00", "a01"))
         hidden(4, ("a10", "a11"))
         hidden(5, ("a20", "a21"))
-        quantize("r60", after="x11")
-        quantize("r70", after=("x11", 4))
+        quantize("r60", after="x12")
+        quantize("r70", after=("x12", 4))
         open_pieces([(7, 1)], after="r50")
         round_w1(copy_vector, 7, 1)
         round_w2(copy_scalar, 1, "p t e", after="r70")

@@ -269,7 +269,7 @@ def tile_moe_pre_mlp_relu_kernel(tc, xT, w1, w2, gate, offs, pos1, pos2, out):
         open_x([(0, 1), (1, 1)], after=("w20", -6))
         times_gate(0, 1)
         times_gate(1, 1)
-        gather(1, 3, 4, 1, after=("w20", 6))
+        gather(1, 3, 4, VECTOR_PLANES, after=("w20", 6))
         round_w1(copy_scalar, 4, 1)
         open_h(0, 2, after="w41")
         hidden(0, ("turned", None))

@@ -52,8 +52,7 @@ def tile_moe_pre_mlp_relu_kernel(tc, xT, w1, w2, gate, offs, pos1, pos2, out):
 
         x_rows = xT.rearrange("(g p t) n -> g t p n", g=PASSES, t=PACK)
         w1_rows = w1.rearrange("e (g p j) c -> e g p j c", g=PASSES, j=PACK)
-        w2_runs = w2.rearrange("e (p t) n -> p e t n", t=PACK)
-        w2_rows = w2.rearrange("e (u t r) n -> r t u e n", t=PACK, r=2)
+        w2_rows = w2.rearrange("e (p t) n -> p e t n", t=PACK)
 
         tiles, gates, codes_of = {}, {}, {}
         batch_of, x_at, piece_at, h_first = {}, {}, {}, {}
@@ -90,14 +89,9 @@ def tile_moe_pre_mlp_relu_kernel(tc, xT, w1, w2, gate, offs, pos1, pos2, out):
         def load_w1(e, g, after=None):
             nc.sync.dma_start(staged("w%d%d" % (e, g), [P, PACK, H], F32, after)[:], w1_rows[e, g])
 
-        def load_w2_low(after):
-            nc.sync.dma_start(staged("v0", [P, GROUP, PACK, N], F32, after)[:], w2_runs[:, :GROUP])
-
-        def load_w2_high(after):
-            raw = staged("v1", [P, PACK, GROUP, N], F32, after)
-            for r in range(2):
-                for t in range(PACK):
-                    nc.sync.dma_start(raw[r:P:2, t], w2_rows[r, t][:, GROUP:])
+        def load_w2(group, after):
+            nc.sync.dma_start(staged("v%d" % group, [P, GROUP, PACK, N], F32, after)[:],
+                              w2_rows[:, group * GROUP:(group + 1) * GROUP])
 
         def spread_gate():
             identity = keep.tile([P, P], F32, name="identity")
@@ -173,13 +167,13 @@ def tile_moe_pre_mlp_relu_kernel(tc, xT, w1, w2, gate, offs, pos1, pos2, out):
                                         1.0, 0.0, MULT, ADD)
 
         def round_w1(copy, e, g):
-            copy(rounded(e, g).rearrange("p (t u r j) -> p u t j r", t=PACK, r=2, j=PACK),
-                 tiles["w%d%d" % (e, g)][:].rearrange("p j (u t r) -> p u t j r", t=PACK, r=2))
+            copy(rounded(e, g).rearrange("p (t q j) -> p q j t", t=PACK, j=PACK),
+                 tiles["w%d%d" % (e, g)][:].rearrange("p j (q t) -> p q j t", t=PACK))
 
-        def round_w2(copy, group, raw_order, after):
+        def round_w2(copy, group, after):
             dst = staged("s%d" % group, [P, GROUP * N * PACK], BF16, after)
             copy(dst[:].rearrange("p (e c i t) -> p e c t i", e=GROUP, i=RUN, t=PACK),
-                 tiles["v%d" % group][:].rearrange(raw_order + " (c i) -> p e c t i", i=RUN))
+                 tiles["v%d" % group][:].rearrange("p e t (c i) -> p e c t i", i=RUN))
 
         def quantize(key, after=None):
             width = tiles[key].shape[1] // PACK
@@ -283,8 +277,8 @@ def tile_moe_pre_mlp_relu_kernel(tc, xT, w1, w2, gate, offs, pos1, pos2, out):
         load_w1(6, 1, after="x02")
         load_w1(7, 0, after="g00")
         load_w1(7, 1, after=("g00", 8))
-        load_w2_low(after=("g10", 8))
-        load_w2_high(after="w50")
+        load_w2(0, after=("g10", 8))
+        load_w2(1, after="w50")
         nc.sync.dma_start(pos1_sb[:], pos1)
         nc.sync.dma_start(pos2_sb[:], pos2)
 
@@ -315,14 +309,14 @@ def tile_moe_pre_mlp_relu_kernel(tc, xT, w1, w2, gate, offs, pos1, pos2, out):
         quantize("r70", after=("x12", 4))
         open_pieces([(7, 1)], after="r50")
         round_w1(copy_vector, 7, 1)
-        round_w2(copy_scalar, 1, "p t e", after="r70")
+        round_w2(copy_scalar, 1, after="r70")
         quantize("r71", after=("r50", 4))
         open_h(6, 7, after="v1")
         open_h(7, 8, after=("v1", 2))
         hidden(6, ("gate2", "gate3"))
         quantize("h3", after="w71")
         quantize("h5", after=("w71", 2))
-        round_w2(copy_vector, 0, "p e t", after="r71")
+        round_w2(copy_vector, 0, after="r71")
         quantize("s0", after="h3")
         quantize("s1", after="v0")
         staged("y", [P, SLOTS], F32, after=("v1", 4))

@@ -21,16 +21,14 @@ COPY = mybir.ActivationFunctionType.Copy
 P = 128
 PACK = 4
 PASSES = K // (P * PACK)
-PAIR = 2 * C
-PAIRS = SLOTS // PAIR
 BANK = C // 2
+GATE_BANK = 2 * C
 RUN = 2
 ENTRIES = 16
 SPARE = 16
 GROUP = 4
 MX_ALIGN = 64
 WIDTH = {F32: 4, U32: 4, BF16: 2, U8: 1}
-VECTOR_PLANES = 2
 TOKEN_RANGES = ((0, 128), (128, 256), (256, 576), (576, 896), (896, T))
 VECTOR_RANGE = 1
 FIRST_STORE = 2
@@ -49,67 +47,34 @@ def tile_moe_pre_mlp_relu_kernel(tc, xT, w1, w2, gate, offs, pos1, pos2, out):
         offs_sb = keep.tile([P, SLOTS // ENTRIES], U16, name="offs_sb")
         pos1_sb = keep.tile([P, T // ENTRIES], U16, name="pos1_sb")
         pos2_sb = keep.tile([P, T // ENTRIES], U16, name="pos2_sb")
+        identity = keep.tile([P, P], F32, name="identity")
+        gate_rows = keep.tile([P, P], F32, name="gate_rows")
+        gate_by_slot = keep.tile([P, SLOTS // P], F32, name="gate_by_slot")
 
         x_rows = xT.rearrange("(g p t) n -> g t p n", g=PASSES, t=PACK)
         w1_rows = w1.rearrange("e (g p j) c -> e g p j c", g=PASSES, j=PACK)
         w2_rows = w2.rearrange("e (p t) n -> p e t n", t=PACK)
 
         tiles, gates, codes_of = {}, {}, {}
-        batch_of, x_at, piece_at, h_first = {}, {}, {}, {}
+        fetched_at, x_at, piece_at, h_at = {}, {}, {}, {}
         place = {"free": 0}
         bank_of = {}
 
-        def reserve(key, kib):
-            place[key] = place["free"]
-            place["free"] += kib * 1024
-
-        def staged(key, shape, dtype, after=None):
-            if after is None:
+        def staged(key, shape, dtype, over=None):
+            if over is None:
                 place[key] = place["free"]
                 place["free"] += prod(shape[1:]) * WIDTH[dtype]
-            elif isinstance(after, str):
-                place[key] = place[after]
+            elif isinstance(over, str):
+                place[key] = place[over]
             else:
-                place[key] = place[after[0]] + after[1] * 1024
+                place[key] = place[over[0]] + int(over[1] * 1024)
             tiles[key] = stage.tile(shape, dtype, name=key, offset=place[key], align_bytes=MX_ALIGN)
             return tiles[key]
 
-        def in_bank(key, shape, after=None):
-            bank_of[key] = bank_of.pop(after) if after else key
-            return psum.tile(shape, F32, name="bank", tag=bank_of[key])
-
-        planes = [staged("p%d%d" % (g, t), [P, T + SPARE], F32) for g in range(PASSES) for t in range(PACK)]
-        for plane in reversed(planes[1:]):
-            nc.gpsimd.memset(plane[:, T:], 0.0)
-        nc.scalar.activation(planes[0][:, T:], planes[-1][:, T:], COPY)
-
-        def load_plane(g, t):
-            nc.sync.dma_start(tiles["p%d%d" % (g, t)][:, :T], x_rows[g, t])
-
-        def load_w1(e, g, after=None):
-            nc.sync.dma_start(staged("w%d%d" % (e, g), [P, PACK, H], F32, after)[:], w1_rows[e, g])
-
-        def load_w2(group, after):
-            nc.sync.dma_start(staged("v%d" % group, [P, GROUP, PACK, N], F32, after)[:],
-                              w2_rows[:, group * GROUP:(group + 1) * GROUP])
-
-        def spread_gate():
-            identity = keep.tile([P, P], F32, name="identity")
-            chunks = SLOTS // P
-            rows = keep.tile([P, P], F32, name="gate_rows")
-            nc.vector.memset(rows[:], 0.0)
-            make_identity(nc, identity[:])
-            nc.sync.dma_start(rows[:chunks, :], gate[0].rearrange("(c p) -> c p", p=P))
-            turned = in_bank("turned", [P, P])
-            nc.tensor.transpose(turned[:], rows[:], identity[:])
-            by_slot = keep.tile([P, chunks], F32, name="gate_by_slot")
-            nc.vector.tensor_copy(by_slot[:], turned[:, :chunks])
-            for pair in range(PAIRS):
-                gates[pair] = in_bank("gate%d" % pair, [P, PAIR])
-                for c in range(PAIR // P):
-                    column = pair * PAIR // P + c
-                    nc.tensor.transpose(gates[pair][:, c * P:(c + 1) * P],
-                                        by_slot[:, column:column + 1].to_broadcast([P, P]), identity[:])
+        def in_bank(key, shape, over=None):
+            bank_of[key] = bank_of.pop(over) if over else key
+            tiles[key] = psum.tile(shape, F32, name="bank", tag=bank_of[key])
+            return tiles[key]
 
         def copy_vector(dst, src):
             nc.vector.tensor_copy(dst, src)
@@ -126,59 +91,89 @@ def tile_moe_pre_mlp_relu_kernel(tc, xT, w1, w2, gate, offs, pos1, pos2, out):
         def relu_vector(dst, src):
             nc.vector.tensor_scalar_max(dst, src, 0.0)
 
-        def gather(g, pair0, pair1, vector_planes, after=None):
-            tile = staged("g%d%d" % (g, pair0), [P, PACK, (pair1 - pair0) * PAIR], F32, after)
-            entries = offs_sb[:, pair0 * PAIR // ENTRIES:pair1 * PAIR // ENTRIES]
-            for t in range(PACK):
-                pick = copy_vector if t < vector_planes else pick_scalar
-                pick(tile[:, t, :], tiles["p%d%d" % (g, t)][:].indirect(entries))
-            for pair in range(pair0, pair1):
-                batch_of[g, pair] = tile[:, :, (pair - pair0) * PAIR:(pair - pair0 + 1) * PAIR]
+        def load_plane(g, t):
+            nc.sync.dma_start(tiles["p%d%d" % (g, t)][:, :T], x_rows[g, t])
 
-        def open_x(parts, after):
-            key = "x%d%d" % parts[0]
-            staged(key, [P, len(parts) * PAIR * PACK], BF16, after)
-            for n, part in enumerate(parts):
-                x_at[part] = (key, n * PAIR)
+        def load_w1(e, g, over=None):
+            nc.sync.dma_start(staged("w%d%d" % (e, g), [P, PACK, H], F32, over)[:], w1_rows[e, g])
 
-        def times_gate(g, pair):
-            key, s0 = x_at[g, pair]
-            dst = tiles[key][:, s0 * PACK:(s0 + PAIR) * PACK]
-            weights = gates[pair][:].rearrange("p (c i) -> p c i", i=RUN)
-            nc.vector.tensor_tensor(dst.rearrange("p (c i t) -> p c t i", i=RUN, t=PACK),
-                                    batch_of[g, pair].rearrange("p t (c i) -> p c t i", i=RUN),
-                                    weights.unsqueeze(2).to_broadcast([P, PAIR // RUN, PACK, RUN]), MULT)
+        def load_w2(group, over):
+            nc.sync.dma_start(staged("v%d" % group, [P, GROUP, PACK, N], F32, over)[:],
+                              w2_rows[:, group * GROUP:(group + 1) * GROUP])
 
-        def open_pieces(pieces, after=None):
+        def load_gate():
+            nc.vector.memset(gate_rows[:], 0.0)
+            make_identity(nc, identity[:])
+            nc.sync.dma_start(gate_rows[:SLOTS // P, :], gate[0].rearrange("(c p) -> c p", p=P))
+
+        def spread_gate(order):
+            turned = in_bank("turned", [P, P])
+            nc.tensor.transpose(turned[:], gate_rows[:], identity[:])
+            nc.vector.tensor_copy(gate_by_slot[:], turned[:, :SLOTS // P])
+            for n in order:
+                gates[n] = in_bank("gate%d" % n, [P, GATE_BANK])
+                for c in range(GATE_BANK // P):
+                    column = n * GATE_BANK // P + c
+                    nc.tensor.transpose(gates[n][:, c * P:(c + 1) * P],
+                                        gate_by_slot[:, column:column + 1].to_broadcast([P, P]), identity[:])
+
+        def open_fetched(g, e0, e1, over=None):
+            staged("f%d%d" % (g, e0), [P, PACK, (e1 - e0) * C], F32, over)
+            for e in range(e0, e1):
+                fetched_at[g, e] = ("f%d%d" % (g, e0), (e - e0) * C)
+
+        def fetch(pick, g, planes, e0, e1):
+            key, s0 = fetched_at[g, e0]
+            entries = offs_sb[:, e0 * C // ENTRIES:e1 * C // ENTRIES]
+            for t in planes:
+                pick(tiles[key][:, t, s0:s0 + (e1 - e0) * C], tiles["p%d%d" % (g, t)][:].indirect(entries))
+
+        def open_x(parts, over=None):
+            key = "x%d%d" % parts[0][:2]
+            s0 = 0
+            for g, e0, e1 in parts:
+                for e in range(e0, e1):
+                    x_at[g, e] = (key, s0)
+                    s0 += C
+            staged(key, [P, s0 * PACK], BF16, over)
+
+        def times_gate(g, e0, e1):
+            (f_key, f0), (x_key, x0), width = fetched_at[g, e0], x_at[g, e0], (e1 - e0) * C
+            g0 = e0 * C % GATE_BANK
+            weights = gates[e0 * C // GATE_BANK][:, g0:g0 + width].rearrange("p (c i) -> p c i", i=RUN)
+            nc.vector.tensor_tensor(
+                tiles[x_key][:, x0 * PACK:(x0 + width) * PACK].rearrange("p (c i t) -> p c t i", i=RUN, t=PACK),
+                tiles[f_key][:, :, f0:f0 + width].rearrange("p t (c i) -> p c t i", i=RUN),
+                weights.unsqueeze(2).to_broadcast([P, width // RUN, PACK, RUN]), MULT)
+
+        def round_gpsimd(dst, src):
+            nc.gpsimd.tensor_scalar(dst, src, 1.0, 0.0, MULT, ADD)
+
+        def open_pieces(pieces, over=None):
             key = "r%d%d" % pieces[0]
-            staged(key, [P, len(pieces) * H * PACK], BF16, after)
+            staged(key, [P, len(pieces) * H * PACK], BF16, over)
             for n, piece in enumerate(pieces):
                 piece_at[piece] = (key, n * H)
 
-        def rounded(e, g):
+        def round_piece(copy, e, g):
             key, c0 = piece_at[e, g]
-            return tiles[key][:, c0 * PACK:(c0 + H) * PACK]
-
-        def round_w1_gpsimd(pieces, after=None):
-            open_pieces(pieces, after)
-            for e, g in pieces:
-                nc.gpsimd.tensor_scalar(rounded(e, g).rearrange("p (t q j) -> p q t j", t=PACK, j=PACK),
-                                        tiles["w%d%d" % (e, g)][:].rearrange("p j (q t) -> p q t j", t=PACK),
-                                        1.0, 0.0, MULT, ADD)
-
-        def round_w1(copy, e, g):
-            copy(rounded(e, g).rearrange("p (t q j) -> p q j t", t=PACK, j=PACK),
+            copy(tiles[key][:, c0 * PACK:(c0 + H) * PACK].rearrange("p (t q j) -> p q j t", t=PACK, j=PACK),
                  tiles["w%d%d" % (e, g)][:].rearrange("p j (q t) -> p q j t", t=PACK))
 
-        def round_w2(copy, group, after):
-            dst = staged("s%d" % group, [P, GROUP * N * PACK], BF16, after)
+        def round_w1(copy, pieces, over=None):
+            open_pieces(pieces, over)
+            for e, g in pieces:
+                round_piece(copy, e, g)
+
+        def round_w2(copy, group, over=None):
+            dst = staged("s%d" % group, [P, GROUP * N * PACK], BF16, over)
             copy(dst[:].rearrange("p (e c i t) -> p e c t i", e=GROUP, i=RUN, t=PACK),
                  tiles["v%d" % group][:].rearrange("p e t (c i) -> p e c t i", i=RUN))
 
-        def quantize(key, after=None):
+        def quantize(key, codes_over=None, scales_over=None):
             width = tiles[key].shape[1] // PACK
-            codes = staged("codes_" + key, [P, width], U32, after)
-            scales = staged("scales_" + key, [P, width], U8)
+            codes = staged("codes_" + key, [P, width], U32, codes_over)
+            scales = staged("scales_" + key, [P, width], U8, scales_over)
             nc.vector.quantize_mx(out=codes[:].bitcast(FP8X4), scales=scales[:], in_=tiles[key][:])
             codes_of[key] = (codes, scales)
 
@@ -188,151 +183,177 @@ def tile_moe_pre_mlp_relu_kernel(tc, xT, w1, w2, gate, offs, pos1, pos2, out):
                                 rhs=r_codes[:, r0:r0 + width].bitcast(FP8X4), rhs_scale=r_scales[:, r0:r0 + width],
                                 start=start, stop=stop)
 
-        def open_h(e0, e1, after):
-            staged("h%d" % e0, [P, (e1 - e0) * C * PACK], BF16, after)
+        def open_h(e0, e1, over=None):
+            staged("h%d" % e0, [P, (e1 - e0) * C * PACK], BF16, over)
             for e in range(e0, e1):
-                h_first[e] = e0
+                h_at[e] = ("h%d" % e0, (e - e0) * C)
 
-        def hidden(e, banks_after, relus=(relu_scalar, relu_scalar)):
-            for b in range(C // BANK):
-                bank = in_bank("a%d%d" % (e, b), [P, PACK, BANK], banks_after[b])
-                for g in range(PASSES):
-                    (w_key, c0), (x_key, x0) = piece_at[e, g], x_at[g, e // 2]
+        def first_layer(e, banks_over):
+            banks = [in_bank("a%d%d" % (e, b), [P, PACK, BANK], banks_over[b]) for b in range(C // BANK)]
+            for g in range(PASSES):
+                (w_key, c0), (x_key, x0) = piece_at[e, g], x_at[g, e]
+                for b, bank in enumerate(banks):
                     for t in range(PACK):
-                        matmul(bank[:, t, :], w_key, c0 + t * P, x_key, x0 + e % 2 * C + b * BANK, BANK,
+                        matmul(bank[:, t, :], w_key, c0 + t * P, x_key, x0 + b * BANK, BANK,
                                g == 0 and t == 0, g == PASSES - 1 and t == PACK - 1)
-                s0 = (e - h_first[e]) * C + b * BANK
-                relus[b](tiles["h%d" % h_first[e]][:, s0 * PACK:(s0 + BANK) * PACK].rearrange("p (s t) -> p s t", t=PACK),
-                         bank[:].rearrange("p t s -> p s t"))
 
-        def second_layer(s0, s1, bank_after, copy):
-            bank = in_bank("y%d" % s0, [P, s1 - s0], bank_after)
+        def hidden(relu, e, halves=(0, 1)):
+            key, s0 = h_at[e]
+            for b in halves:
+                dst = tiles[key][:, (s0 + b * BANK) * PACK:(s0 + (b + 1) * BANK) * PACK]
+                relu(dst.rearrange("p (s t) -> p s t", t=PACK), tiles["a%d%d" % (e, b)][:].rearrange("p t s -> p s t"))
+
+        def second_layer(s0, s1, bank_over, copy):
+            bank = in_bank("y%d" % s0, [P, s1 - s0], bank_over)
             for a in range(s0, s1, C):
                 e, width = a // C, min(C, s1 - a)
-                matmul(bank[:, a - s0:a - s0 + width], "s%d" % (e // GROUP), e % GROUP * N,
-                       "h%d" % h_first[e], a - h_first[e] * C, width, True, True)
+                key, h0 = h_at[e]
+                matmul(bank[:, a - s0:a - s0 + width], "s%d" % (e // GROUP), e % GROUP * N, key, h0 + a % C, width, True, True)
             copy(tiles["y"][:, s0:s1], bank[:])
+
+
+        wide = ((0, 0), (0, 1), (1, 0), (1, 1), (1, 2))
+        for g in range(PASSES):
+            for t in range(PACK):
+                staged("p%d%d" % (g, t), [P, T + SPARE * ((g, t) in wide)], F32)
+        for g, t in reversed(wide[1:]):
+            nc.gpsimd.memset(tiles["p%d%d" % (g, t)][:, T:], 0.0)
+        nc.scalar.activation(tiles["p00"][:, T:], tiles["p12"][:, T:], COPY)
 
         nc.sync.dma_start(offs_sb[:], offs)
         load_plane(0, 0)
         load_plane(0, 1)
-        spread_gate()
+        load_gate()
         load_w1(0, 0)
         load_plane(0, 2)
         load_plane(0, 3)
         load_w1(0, 1)
-        load_plane(1, 0)
         load_w1(1, 0)
-        reserve("behind_w10", 2)
-        for t in range(1, PACK):
-            load_plane(1, t)
+        load_plane(1, 0)
         load_w1(1, 1)
-        reserve("w20", 8 + 6)
-        load_w1(4, 0)
-        load_w1(2, 0, after="w20")
-        load_w1(2, 1)
-        reserve("w30", 8)
-        load_w1(4, 1)
-        load_w1(3, 0, after="w30")
-        for e, g in ((5, 0), (5, 1), (3, 1)):
+        load_plane(1, 1)
+        load_plane(1, 2)
+        load_plane(1, 3)
+        for e, g in ((2, 0), (2, 1), (3, 0), (3, 1), (4, 0), (4, 1), (5, 0), (5, 1)):
             load_w1(e, g)
 
-        gather(0, 2, 4, PACK)
-        gather(0, 0, 2, 0)
-        gather(1, 0, 2, 0)
-        round_w1_gpsimd([(0, 0), (0, 1)])
-        round_w1_gpsimd([(1, 0)])
-        open_x([(0, 2), (0, 3)], after="w00")
-        times_gate(0, 2)
-        times_gate(0, 3)
-        quantize("r00")
-        quantize("x02")
-        quantize("r10")
-
-        round_w1_gpsimd([(1, 1), (2, 0)], after=("r10", -4))
-        open_x([(0, 0), (1, 0)], after=("w10", 2))
-        times_gate(0, 0)
-        gather(1, 2, 3, VECTOR_PLANES, after=("w10", -6))
-        times_gate(1, 0)
-        open_pieces([(4, 0), (4, 1)], after="g02")
-        round_w1(copy_scalar, 4, 0)
-        quantize("x00", after=("w20", 2))
-        quantize("r11", after="r00")
-
-        round_w1_gpsimd([(2, 1), (3, 0)], after="r11")
-        open_x([(0, 1), (1, 1)], after=("w20", -6))
-        times_gate(0, 1)
-        times_gate(1, 1)
-        gather(1, 3, 4, VECTOR_PLANES, after=("w20", 6))
-        round_w1(copy_scalar, 4, 1)
-        open_h(0, 2, after="w41")
-        hidden(0, ("turned", None))
-        hidden(1, (None, None))
-        open_pieces([(5, 0), (5, 1)], after="w40")
-        round_w1(copy_scalar, 5, 0)
-        round_w1(copy_scalar, 5, 1)
-        quantize("x01")
-        quantize("r21")
-        load_w1(6, 0, after=("g02", 8))
-        load_w1(6, 1, after="x02")
-        load_w1(7, 0, after="g00")
-        load_w1(7, 1, after=("g00", 8))
-        load_w2(0, after=("g10", 8))
-        load_w2(1, after="w50")
+        open_fetched(0, 0, 4)
+        open_fetched(0, 4, 6)
+        open_fetched(0, 6, 8)
+        fetch(copy_vector, 0, (0,), 6, 8)
+        fetch(copy_vector, 0, (0,), 4, 6)
+        fetch(pick_scalar, 0, (0, 1), 0, 4)
+        spread_gate((3, 2, 0, 1))
+        fetch(copy_vector, 0, (1,), 6, 8)
+        fetch(copy_vector, 0, (1,), 4, 6)
+        round_w1(round_gpsimd, [(0, 0), (0, 1)])
+        round_w1(round_gpsimd, [(1, 0), (1, 1)])
+        fetch(copy_vector, 0, (2, 3), 6, 8)
+        fetch(pick_scalar, 0, (2, 3), 4, 6)
+        fetch(pick_scalar, 0, (2, 3), 0, 2)
+        fetch(pick_scalar, 0, (2, 3), 2, 4)
+        open_x([(0, 6, 8), (0, 4, 6)])
+        times_gate(0, 6, 8)
+        times_gate(0, 4, 6)
+        open_x([(0, 0, 4)], over="f06")
+        times_gate(0, 0, 2)
+        times_gate(0, 2, 4)
+        load_w1(6, 0, over="f04")
+        load_w1(6, 1, over="f00")
+        load_w1(7, 0, over=("f00", 8))
+        load_w1(7, 1, over="p00")
+        load_w2(0, over="p02")
+        load_w2(1, over=None)
         nc.sync.dma_start(pos1_sb[:], pos1)
         nc.sync.dma_start(pos2_sb[:], pos2)
+        quantize("r00", "w11", ("w11", 4))
+        quantize("x06", "w00", ("w11", 5))
+        quantize("r10", ("w00", 4), "w10")
+        quantize("x00", "w01", ("w11", 6))
 
-        round_w1_gpsimd([(3, 1)], after="r21")
-        open_x([(1, 2), (1, 3)], after=("w30", -6))
-        times_gate(1, 2)
-        times_gate(1, 3)
-        open_pieces([(6, 0), (6, 1)], after="x00")
-        round_w1(copy_scalar, 6, 0)
-        open_h(2, 3, after="w60")
-        hidden(2, ("gate0", "gate1"))
-        round_w1(copy_scalar, 6, 1)
-        open_pieces([(7, 0)], after="w61")
-        round_w1(copy_scalar, 7, 0)
+        open_fetched(1, 0, 4)
+        fetch(pick_scalar, 1, (0, 1, 2), 0, 4)
+        fetch(pick_scalar, 1, (3,), 0, 2)
+        fetch(pick_scalar, 1, (3,), 2, 4)
+        round_w1(round_gpsimd, [(2, 0), (2, 1)], over="x00")
+        open_fetched(1, 4, 6, over="r00")
+        open_x([(1, 0, 4)], over="x06")
+        fetch(copy_vector, 1, (0,), 4, 6)
+        times_gate(1, 0, 2)
+        times_gate(1, 2, 4)
+        fetch(pick_scalar, 1, (1, 2, 3), 4, 6)
+        round_w1(copy_scalar, [(3, 0), (3, 1)], over="r10")
+        quantize("x10", "w21", ("w21", 4))
+        quantize("r20", "w20", ("w20", 4))
 
-        quantize("r40", after="g12")
-        quantize("x12", after="g10")
-        quantize("r31", after=("g12", 4))
-        quantize("r50", after="g13")
-        quantize("h0", after=("g13", 4))
-        quantize("h2", after=("g13", 6))
-        open_h(3, 5, after="w70")
-        open_h(5, 6, after=("w70", 4))
-        hidden(3, ("a00", "a01"))
-        hidden(4, ("a10", "a11"))
-        hidden(5, ("a20", "a21"))
-        quantize("r60", after="x12")
-        quantize("r70", after=("x12", 4))
-        open_pieces([(7, 1)], after="r50")
-        round_w1(copy_vector, 7, 1)
-        round_w2(copy_scalar, 1, after="r70")
-        quantize("r71", after=("r50", 4))
-        open_h(6, 7, after="v1")
-        open_h(7, 8, after=("v1", 2))
-        hidden(6, ("gate2", "gate3"))
-        quantize("h3", after="w71")
-        quantize("h5", after=("w71", 2))
-        round_w2(copy_vector, 0, after="r71")
-        quantize("s0", after="h3")
-        quantize("s1", after="v0")
-        staged("y", [P, SLOTS], F32, after=("v1", 4))
-        second_layer(2 * C, 4 * C, "a51", copy_vector)
-        hidden(7, ("a30", "a31"), (relu_scalar, relu_vector))
-        quantize("h6", after=("v0", 2))
-        quantize("h7", after=("v0", 3))
-        second_layer(0, 2 * C, "a50", copy_scalar)
-        second_layer(4 * C, 6 * C, "a40", copy_scalar)
-        second_layer(6 * C, 7 * C, "a41", copy_scalar)
+        round_w1(round_gpsimd, [(4, 0), (4, 1)], over="r20")
+        open_x([(1, 4, 6)], over="x10")
+        open_fetched(1, 6, 7, over=("x10", 4))
+        first_layer(0, ("turned", None))
+        first_layer(1, (None, None))
+        first_layer(2, ("gate0", "gate1"))
+        open_h(0, 2, over="w31")
+        open_h(2, 3, over=("w31", 4))
+        times_gate(1, 4, 6)
+        fetch(copy_vector, 1, range(PACK), 6, 7)
+        hidden(relu_scalar, 0)
+        hidden(relu_scalar, 1)
+        hidden(relu_scalar, 2, (0,))
+        hidden(relu_vector, 2, (1,))
+        round_w1(copy_scalar, [(5, 0), (5, 1)], over="f14")
+        quantize("r30", "w41", ("w41", 4))
+        quantize("x14", ("w41", 5), ("w41", 7))
+        quantize("r40", "w40", ("w40", 4))
+
+        round_w1(round_gpsimd, [(6, 0), (6, 1)], over="r40")
+        open_fetched(1, 7, 8, over="r30")
+        open_x([(1, 6, 8)], over=("r30", 4))
+        first_layer(3, ("a00", "a01"))
+        first_layer(4, ("a10", "a11"))
+        open_h(3, 5, over="w51")
+        fetch(copy_vector, 1, (0, 1), 7, 8)
+        times_gate(1, 6, 7)
+        fetch(copy_vector, 1, (2, 3), 7, 8)
+        times_gate(1, 7, 8)
+        hidden(relu_scalar, 3)
+        hidden(relu_scalar, 4, (0,))
+        hidden(relu_vector, 4, (1,))
+        round_w1(copy_scalar, [(7, 0), (7, 1)], over="x14")
+        quantize("r50", "w61", ("w61", 4))
+        quantize("x16", ("w61", 5), ("w61", 7))
+        quantize("r60", "w60", ("w60", 4))
+        quantize("h0", "r50", ("r50", 2))
+        quantize("r70", "w50", ("r50", 6.5))
+
+        first_layer(5, ("a20", "a21"))
+        first_layer(6, ("gate2", "gate3"))
+        first_layer(7, ("a30", "a31"))
+        round_w2(copy_scalar, 0, over="f17")
+        open_h(5, 6, over=("v0", 4))
+        hidden(relu_scalar, 5)
+        open_h(6, 7, over="v0")
+        open_h(7, 8, over=("v0", 2))
+        hidden(relu_scalar, 6)
+        hidden(relu_scalar, 7)
+        quantize("h2", ("r50", 3), ("r50", 4))
+        quantize("h3", ("r50", 4.5), ("r50", 7.5))
+        round_w2(copy_vector, 1, over="r60")
+        quantize("s0", ("r60", 4), ("r60", 6))
+        quantize("s1")
+        quantize("h5", "v1", ("v1", 1))
+        quantize("h6", ("v1", 2), ("v1", 3))
+        staged("y", [P, SLOTS], F32, over="w30")
+        quantize("h7", ("v1", 4), ("v1", 5))
+        second_layer(0, 2 * C, "a40", copy_scalar)
+        second_layer(2 * C, 4 * C, "a41", copy_scalar)
+        second_layer(4 * C, 6 * C, "a50", copy_vector)
+        second_layer(6 * C, 7 * C, "a51", copy_scalar)
         second_layer(7 * C, 7 * C + BANK, "a60", copy_vector)
         second_layer(7 * C + BANK, SLOTS, "a61", copy_scalar)
 
         y_sb = tiles["y"]
-        both = staged("both", [P, T], F32, after="p10")
-        first = staged("first", [P, T], F32, after="p00")
+        both = staged("both", [P, T], F32, over="p10")
+        first = staged("first", [P, T], F32, over="p11")
         for n, (t0, t1) in enumerate(TOKEN_RANGES):
             pick = copy_vector if n == VECTOR_RANGE else pick_scalar
             pick(first[:, t0:t1], y_sb[:].indirect(pos1_sb[:, t0 // ENTRIES:t1 // ENTRIES]))

@@ -147,7 +147,7 @@ def tile_moe_pre_mlp_relu_kernel(tc, xT, w1, w2, gate, offs, pos1, pos2, out):
                 weights.unsqueeze(2).to_broadcast([P, width // RUN, PACK, RUN]), MULT)
 
         def round_gpsimd(dst, src):
-            nc.gpsimd.tensor_scalar(dst, src, 1.0, 0.0, MULT, ADD)
+            nc.gpsimd.tensor_copy(dst, src)
 
         def open_pieces(pieces, over=None):
             key = "r%d%d" % pieces[0]
@@ -160,10 +160,21 @@ def tile_moe_pre_mlp_relu_kernel(tc, xT, w1, w2, gate, offs, pos1, pos2, out):
             copy(tiles[key][:, c0 * PACK:(c0 + H) * PACK].rearrange("p (t q j) -> p q j t", t=PACK, j=PACK),
                  tiles["w%d%d" % (e, g)][:].rearrange("p j (q t) -> p q j t", t=PACK))
 
+        def round_pairs(copy, e, g):
+            key, c0 = piece_at[e, g]
+            copy(tiles[key][:, c0 * PACK:(c0 + H) * PACK].rearrange("p (t q u v) -> p q u t v", t=PACK, u=RUN, v=RUN),
+                 tiles["w%d%d" % (e, g)][:].rearrange("p (u v) (q t) -> p q u t v", t=PACK, v=RUN))
+
+        def round_half(copy, e, g, half):
+            key, c0 = piece_at[e, g]
+            c0 += half * H // 2
+            copy(tiles[key][:, c0 * PACK:(c0 + H // 2) * PACK].rearrange("p (t q j) -> p q j t", t=RUN, j=PACK),
+                 tiles["w%d%d" % (e, g)][:].rearrange("p j (q t) -> p q j t", t=PACK)[:, :, :, half * RUN:(half + 1) * RUN])
+
         def round_w1(copy, pieces, over=None):
             open_pieces(pieces, over)
             for e, g in pieces:
-                round_piece(copy, e, g)
+                (round_pairs if copy is round_gpsimd else round_piece)(copy, e, g)
 
         def round_w2(copy, group, over=None):
             dst = staged("s%d" % group, [P, GROUP * N * PACK], BF16, over)

@@ -26,7 +26,6 @@ GATE_BANK = 2 * C
 RUN = 2
 ENTRIES = 16
 SPARE = 16
-GROUP = 4
 MX_ALIGN = 64
 WIDTH = {F32: 4, U32: 4, BF16: 2, U8: 1}
 TOKEN_RANGES = ((0, 128), (128, 256), (256, 576), (576, 896), (896, T))
@@ -56,7 +55,7 @@ def tile_moe_pre_mlp_relu_kernel(tc, xT, w1, w2, gate, offs, pos1, pos2, out):
         w2_rows = w2.rearrange("e (p t) n -> p e t n", t=PACK)
 
         tiles, gates, codes_of = {}, {}, {}
-        fetched_at, x_at, piece_at, h_at = {}, {}, {}, {}
+        fetched_at, x_at, piece_at, h_at, w2_at = {}, {}, {}, {}, {}
         place = {"free": 0}
         bank_of = {}
 
@@ -97,9 +96,8 @@ def tile_moe_pre_mlp_relu_kernel(tc, xT, w1, w2, gate, offs, pos1, pos2, out):
         def load_w1(e, g, over=None):
             nc.sync.dma_start(staged("w%d%d" % (e, g), [P, PACK, H], F32, over)[:], w1_rows[e, g])
 
-        def load_w2(group, over):
-            nc.sync.dma_start(staged("v%d" % group, [P, GROUP, PACK, N], F32, over)[:],
-                              w2_rows[:, group * GROUP:(group + 1) * GROUP])
+        def load_w2(e0, e1, over=None):
+            nc.sync.dma_start(staged("v%d" % e0, [P, e1 - e0, PACK, N], F32, over)[:], w2_rows[:, e0:e1])
 
         def load_gate():
             nc.vector.memset(gate_rows[:], 0.0)
@@ -160,26 +158,23 @@ def tile_moe_pre_mlp_relu_kernel(tc, xT, w1, w2, gate, offs, pos1, pos2, out):
             copy(tiles[key][:, c0 * PACK:(c0 + H) * PACK].rearrange("p (t q j) -> p q j t", t=PACK, j=PACK),
                  tiles["w%d%d" % (e, g)][:].rearrange("p j (q t) -> p q j t", t=PACK))
 
-        def round_pairs(copy, e, g):
+        def round_pairs(copy, e, g, t0=0, t1=PACK):
             key, c0 = piece_at[e, g]
-            copy(tiles[key][:, c0 * PACK:(c0 + H) * PACK].rearrange("p (t q u v) -> p q u t v", t=PACK, u=RUN, v=RUN),
-                 tiles["w%d%d" % (e, g)][:].rearrange("p (u v) (q t) -> p q u t v", t=PACK, v=RUN))
-
-        def round_half(copy, e, g, half):
-            key, c0 = piece_at[e, g]
-            c0 += half * H // 2
-            copy(tiles[key][:, c0 * PACK:(c0 + H // 2) * PACK].rearrange("p (t q j) -> p q j t", t=RUN, j=PACK),
-                 tiles["w%d%d" % (e, g)][:].rearrange("p j (q t) -> p q j t", t=PACK)[:, :, :, half * RUN:(half + 1) * RUN])
+            dst = tiles[key][:, (c0 + t0 * P) * PACK:(c0 + t1 * P) * PACK]
+            src = tiles["w%d%d" % (e, g)][:].rearrange("p (u v) (q t) -> p q u t v", t=PACK, v=RUN)
+            copy(dst.rearrange("p (t q u v) -> p q u t v", q=P, u=RUN, v=RUN), src[:, :, :, t0:t1])
 
         def round_w1(copy, pieces, over=None):
             open_pieces(pieces, over)
             for e, g in pieces:
                 (round_pairs if copy is round_gpsimd else round_piece)(copy, e, g)
 
-        def round_w2(copy, group, over=None):
-            dst = staged("s%d" % group, [P, GROUP * N * PACK], BF16, over)
-            copy(dst[:].rearrange("p (e c i t) -> p e c t i", e=GROUP, i=RUN, t=PACK),
-                 tiles["v%d" % group][:].rearrange("p e t (c i) -> p e c t i", i=RUN))
+        def round_w2(copy, e0, e1, over=None):
+            dst = staged("s%d" % e0, [P, (e1 - e0) * N * PACK], BF16, over)
+            copy(dst[:].rearrange("p (e c i t) -> p e c t i", e=e1 - e0, i=RUN, t=PACK),
+                 tiles["v%d" % e0][:].rearrange("p e t (c i) -> p e c t i", i=RUN))
+            for e in range(e0, e1):
+                w2_at[e] = ("s%d" % e0, (e - e0) * N)
 
         def quantize(key, codes_over=None, scales_over=None):
             width = tiles[key].shape[1] // PACK
@@ -219,7 +214,7 @@ def tile_moe_pre_mlp_relu_kernel(tc, xT, w1, w2, gate, offs, pos1, pos2, out):
             for a in range(s0, s1, C):
                 e, width = a // C, min(C, s1 - a)
                 key, h0 = h_at[e]
-                matmul(bank[:, a - s0:a - s0 + width], "s%d" % (e // GROUP), e % GROUP * N, key, h0 + a % C, width, True, True)
+                matmul(bank[:, a - s0:a - s0 + width], *w2_at[e], key, h0 + a % C, width, True, True)
             copy(tiles["y"][:, s0:s1], bank[:])
 
 
@@ -247,6 +242,7 @@ def tile_moe_pre_mlp_relu_kernel(tc, xT, w1, w2, gate, offs, pos1, pos2, out):
         load_plane(1, 3)
         for e, g in ((2, 0), (2, 1), (3, 0), (3, 1), (4, 0), (4, 1), (5, 0), (5, 1)):
             load_w1(e, g)
+        place["free"] += 2 * 1024
 
         open_fetched(0, 0, 4)
         open_fetched(0, 4, 6)
@@ -273,8 +269,10 @@ def tile_moe_pre_mlp_relu_kernel(tc, xT, w1, w2, gate, offs, pos1, pos2, out):
         load_w1(6, 1, over="f00")
         load_w1(7, 0, over=("f00", 8))
         load_w1(7, 1, over="p00")
-        load_w2(0, over="p02")
-        load_w2(1, over=None)
+        load_w2(0, 2, over="p02")
+        load_w2(2, 4, over="p03")
+        load_w2(4, 6)
+        load_w2(6, 8)
         nc.sync.dma_start(pos1_sb[:], pos1)
         nc.sync.dma_start(pos2_sb[:], pos2)
         quantize("r00", "w11", ("w11", 4))
@@ -287,13 +285,13 @@ def tile_moe_pre_mlp_relu_kernel(tc, xT, w1, w2, gate, offs, pos1, pos2, out):
         fetch(pick_scalar, 1, (3,), 0, 2)
         fetch(pick_scalar, 1, (3,), 2, 4)
         round_w1(round_gpsimd, [(2, 0), (2, 1)], over="x00")
-        open_fetched(1, 4, 6, over="r00")
+        open_fetched(1, 4, 6, over="r10")
         open_x([(1, 0, 4)], over="x06")
         fetch(copy_vector, 1, (0,), 4, 6)
         times_gate(1, 0, 2)
         times_gate(1, 2, 4)
         fetch(pick_scalar, 1, (1, 2, 3), 4, 6)
-        round_w1(copy_scalar, [(3, 0), (3, 1)], over="r10")
+        round_w1(copy_scalar, [(3, 0), (3, 1)], over="r00")
         quantize("x10", "w21", ("w21", 4))
         quantize("r20", "w20", ("w20", 4))
 
@@ -311,56 +309,65 @@ def tile_moe_pre_mlp_relu_kernel(tc, xT, w1, w2, gate, offs, pos1, pos2, out):
         hidden(relu_scalar, 1)
         hidden(relu_scalar, 2, (0,))
         hidden(relu_vector, 2, (1,))
-        round_w1(copy_scalar, [(5, 0), (5, 1)], over="f14")
+        round_w1(copy_scalar, [(5, 0)], over="f14")
+        round_w1(copy_scalar, [(5, 1)], over=("f14", 4))
         quantize("r30", "w41", ("w41", 4))
         quantize("x14", ("w41", 5), ("w41", 7))
         quantize("r40", "w40", ("w40", 4))
 
-        round_w1(round_gpsimd, [(6, 0), (6, 1)], over="r40")
-        open_fetched(1, 7, 8, over="r30")
-        open_x([(1, 6, 8)], over=("r30", 4))
+        quantize("r50", "w50", ("r30", 7))
+        quantize("h0", ("w50", 2), ("r30", 6))
+        quantize("h2", ("w50", 4), ("r30", 5))
+        quantize("r51", None, ("r30", 4))
+
+        open_pieces([(6, 0), (6, 1)], over="r51")
+        round_pairs(round_gpsimd, 6, 0)
+        round_pairs(round_gpsimd, 6, 1, 0, 2)
+        open_fetched(1, 7, 8, over=("w51", 2))
+        open_x([(1, 6, 8)], over=("w51", 6))
         first_layer(3, ("a00", "a01"))
         first_layer(4, ("a10", "a11"))
-        open_h(3, 5, over="w51")
+        first_layer(5, ("a20", "a21"))
+        open_h(3, 5, over=("w51", -2))
+        open_h(5, 6, over="r50")
         fetch(copy_vector, 1, (0, 1), 7, 8)
         times_gate(1, 6, 7)
         fetch(copy_vector, 1, (2, 3), 7, 8)
         times_gate(1, 7, 8)
-        hidden(relu_scalar, 3)
-        hidden(relu_scalar, 4, (0,))
-        hidden(relu_vector, 4, (1,))
-        round_w1(copy_scalar, [(7, 0), (7, 1)], over="x14")
-        quantize("r50", "w61", ("w61", 4))
-        quantize("x16", ("w61", 5), ("w61", 7))
+        for e in range(3, 6):
+            hidden(relu_scalar, e)
+        round_pairs(copy_scalar, 6, 1, 2, 4)
+        round_w1(copy_scalar, [(7, 0)], over="f16")
+        round_w1(copy_scalar, [(7, 1)], over="f17")
+        quantize("x16", "w61", ("w61", 2))
         quantize("r60", "w60", ("w60", 4))
-        quantize("h0", "r50", ("r50", 2))
-        quantize("r70", "w50", ("r50", 6.5))
+        quantize("r70", ("w61", 3), ("w61", 5))
+        quantize("h3", ("w60", 5), ("w61", 6))
+        quantize("h5", None, ("w61", 7))
 
-        first_layer(5, ("a20", "a21"))
         first_layer(6, ("gate2", "gate3"))
+        quantize("r71", "r60", ("r60", 2))
         first_layer(7, ("a30", "a31"))
-        round_w2(copy_scalar, 0, over="f17")
-        open_h(5, 6, over=("v0", 4))
-        hidden(relu_scalar, 5)
+        round_w2(copy_scalar, 0, 2, over="w71")
         open_h(6, 7, over="v0")
         open_h(7, 8, over=("v0", 2))
         hidden(relu_scalar, 6)
         hidden(relu_scalar, 7)
-        quantize("h2", ("r50", 3), ("r50", 4))
-        quantize("h3", ("r50", 4.5), ("r50", 7.5))
-        round_w2(copy_vector, 1, over="r60")
-        quantize("s0", ("r60", 4), ("r60", 6))
-        quantize("s1")
-        quantize("h5", "v1", ("v1", 1))
-        quantize("h6", ("v1", 2), ("v1", 3))
+        round_w2(copy_vector, 2, 4, over="r70")
+        quantize("s0")
+        round_w2(copy_vector, 4, 6, over="r71")
+        quantize("s2", None, "s0")
+        round_w2(copy_vector, 6, 8)
+        quantize("h6", "v4", ("v4", 1))
+        quantize("s4", ("v4", 2), ("v4", 3))
         staged("y", [P, SLOTS], F32, over="w30")
-        quantize("h7", ("v1", 4), ("v1", 5))
         second_layer(0, 2 * C, "a40", copy_scalar)
         second_layer(2 * C, 4 * C, "a41", copy_scalar)
-        second_layer(4 * C, 6 * C, "a50", copy_vector)
-        second_layer(6 * C, 7 * C, "a51", copy_scalar)
-        second_layer(7 * C, 7 * C + BANK, "a60", copy_vector)
-        second_layer(7 * C + BANK, SLOTS, "a61", copy_scalar)
+        quantize("h7", "v6", ("v6", 1))
+        quantize("s6")
+        second_layer(4 * C, 6 * C, "a50", copy_scalar)
+        second_layer(6 * C, 7 * C, "a51", copy_vector)
+        second_layer(7 * C, 8 * C, "a60", copy_scalar)
 
         y_sb = tiles["y"]
         both = staged("both", [P, T], F32, over="p10")

from contextlib import ExitStack
from math import prod

import concourse.mybir as mybir
from concourse.masks import make_identity

K, T, E, C, H, N = 1024, 1024, 8, 256, 512, 128
SLOTS = E * C

F32 = mybir.dt.float32
BF16 = mybir.dt.bfloat16
U32 = mybir.dt.uint32
U16 = mybir.dt.uint16
U8 = mybir.dt.uint8
FP8X4 = mybir.dt.float8_e4m3fn_x4
MULT = mybir.AluOpType.mult
ADD = mybir.AluOpType.add
RELU = mybir.ActivationFunctionType.Relu
COPY = mybir.ActivationFunctionType.Copy

P = 128
PACK = 4
PASSES = K // (P * PACK)
BANK = C // 2
GATE_BANK = 2 * C
RUN = 2
ENTRIES = 16
SPARE = 16
MX_ALIGN = 64
WIDTH = {F32: 4, U32: 4, BF16: 2, U8: 1}
TOKEN_RANGES = ((0, 128), (128, 256), (256, 576), (576, 896), (896, T))
VECTOR_RANGE = 1
FIRST_STORE = 2

FLOPS = 2 * SLOTS * (K * H + H * N)
BYTES = 4 * (K * T + E * K * H + E * H * N + SLOTS + N * T) + 2 * P * (SLOTS + 2 * T) // ENTRIES


def tile_moe_pre_mlp_relu_kernel(tc, xT, w1, w2, gate, offs, pos1, pos2, out):
    nc = tc.nc
    with ExitStack() as ctx:
        keep = ctx.enter_context(tc.tile_pool(name="keep", bufs=1))
        stage = ctx.enter_context(tc.tile_pool(name="stage", bufs=1))
        psum = ctx.enter_context(tc.psum_pool(name="psum", bufs=1))

        offs_sb = keep.tile([P, SLOTS // ENTRIES], U16, name="offs_sb")
        pos1_sb = keep.tile([P, T // ENTRIES], U16, name="pos1_sb")
        pos2_sb = keep.tile([P, T // ENTRIES], U16, name="pos2_sb")
        identity = keep.tile([P, P], F32, name="identity")
        gate_rows = keep.tile([P, P], F32, name="gate_rows")
        gate_by_slot = keep.tile([P, SLOTS // P], F32, name="gate_by_slot")

        x_rows = xT.rearrange("(g p t) n -> g t p n", g=PASSES, t=PACK)
        w1_rows = w1.rearrange("e (g p j) c -> e g p j c", g=PASSES, j=PACK)
        w2_rows = w2.rearrange("e (p t) n -> p e t n", t=PACK)

        tiles, gates, codes_of = {}, {}, {}
        fetched_at, x_at, piece_at, h_at, w2_at = {}, {}, {}, {}, {}
        place = {"free": 0}
        bank_of = {}

        def staged(key, shape, dtype, over=None):
            if over is None:
                place[key] = place["free"]
                place["free"] += prod(shape[1:]) * WIDTH[dtype]
            elif isinstance(over, str):
                place[key] = place[over]
            else:
                place[key] = place[over[0]] + int(over[1] * 1024)
            tiles[key] = stage.tile(shape, dtype, name=key, offset=place[key], align_bytes=MX_ALIGN)
            return tiles[key]

        def in_bank(key, shape, over=None):
            bank_of[key] = bank_of.pop(over) if over else key
            tiles[key] = psum.tile(shape, F32, name="bank", tag=bank_of[key])
            return tiles[key]

        def copy_vector(dst, src):
            nc.vector.tensor_copy(dst, src)

        def copy_scalar(dst, src):
            nc.scalar.copy(dst, src)

        def pick_scalar(dst, src):
            nc.scalar.activation(dst, src, COPY)

        def relu_scalar(dst, src):
            nc.scalar.activation(dst, src, RELU)

        def relu_vector(dst, src):
            nc.vector.tensor_scalar_max(dst, src, 0.0)

        def load_plane(g, t):
            nc.sync.dma_start(tiles["p%d%d" % (g, t)][:, :T], x_rows[g, t])

        def load_w1(e, g, over=None):
            nc.sync.dma_start(staged("w%d%d" % (e, g), [P, PACK, H], F32, over)[:], w1_rows[e, g])

        def load_w2(e0, e1, over=None):
            nc.sync.dma_start(staged("v%d" % e0, [P, e1 - e0, PACK, N], F32, over)[:], w2_rows[:, e0:e1])

        def load_gate():
            nc.vector.memset(gate_rows[:], 0.0)
            make_identity(nc, identity[:])
            nc.sync.dma_start(gate_rows[:SLOTS // P, :], gate[0].rearrange("(c p) -> c p", p=P))

        def spread_gate(order):
            turned = in_bank("turned", [P, P])
            nc.tensor.transpose(turned[:], gate_rows[:], identity[:])
            nc.vector.tensor_copy(gate_by_slot[:], turned[:, :SLOTS // P])
            for n in order:
                gates[n] = in_bank("gate%d" % n, [P, GATE_BANK])
                for c in range(GATE_BANK // P):
                    column = n * GATE_BANK // P + c
                    nc.tensor.transpose(gates[n][:, c * P:(c + 1) * P],
                                        gate_by_slot[:, column:column + 1].to_broadcast([P, P]), identity[:])

        def open_fetched(g, e0, e1, over=None):
            staged("f%d%d" % (g, e0), [P, PACK, (e1 - e0) * C], F32, over)
            for e in range(e0, e1):
                fetched_at[g, e] = ("f%d%d" % (g, e0), (e - e0) * C)

        def fetch(pick, g, planes, e0, e1):
            key, s0 = fetched_at[g, e0]
            entries = offs_sb[:, e0 * C // ENTRIES:e1 * C // ENTRIES]
            for t in planes:
                pick(tiles[key][:, t, s0:s0 + (e1 - e0) * C], tiles["p%d%d" % (g, t)][:].indirect(entries))

        def open_x(parts, over=None):
            key = "x%d%d" % parts[0][:2]
            s0 = 0
            for g, e0, e1 in parts:
                for e in range(e0, e1):
                    x_at[g, e] = (key, s0)
                    s0 += C
            staged(key, [P, s0 * PACK], BF16, over)

        def times_gate(g, e0, e1):
            (f_key, f0), (x_key, x0), width = fetched_at[g, e0], x_at[g, e0], (e1 - e0) * C
            g0 = e0 * C % GATE_BANK
            weights = gates[e0 * C // GATE_BANK][:, g0:g0 + width].rearrange("p (c i) -> p c i", i=RUN)
            nc.vector.tensor_tensor(
                tiles[x_key][:, x0 * PACK:(x0 + width) * PACK].rearrange("p (c i t) -> p c t i", i=RUN, t=PACK),
                tiles[f_key][:, :, f0:f0 + width].rearrange("p t (c i) -> p c t i", i=RUN),
                weights.unsqueeze(2).to_broadcast([P, width // RUN, PACK, RUN]), MULT)

        def round_gpsimd(dst, src):
            nc.gpsimd.tensor_copy(dst, src)

        def open_pieces(pieces, over=None):
            key = "r%d%d" % pieces[0]
            staged(key, [P, len(pieces) * H * PACK], BF16, over)
            for n, piece in enumerate(pieces):
                piece_at[piece] = (key, n * H)

        def round_piece(copy, e, g):
            key, c0 = piece_at[e, g]
            copy(tiles[key][:, c0 * PACK:(c0 + H) * PACK].rearrange("p (t q j) -> p q j t", t=PACK, j=PACK),
                 tiles["w%d%d" % (e, g)][:].rearrange("p j (q t) -> p q j t", t=PACK))

        def round_pairs(copy, e, g, t0=0, t1=PACK):
            key, c0 = piece_at[e, g]
            dst = tiles[key][:, (c0 + t0 * P) * PACK:(c0 + t1 * P) * PACK]
            src = tiles["w%d%d" % (e, g)][:].rearrange("p (u v) (q t) -> p q u t v", t=PACK, v=RUN)
            copy(dst.rearrange("p (t q u v) -> p q u t v", q=P, u=RUN, v=RUN), src[:, :, :, t0:t1])

        def round_w1(copy, pieces, over=None):
            open_pieces(pieces, over)
            for e, g in pieces:
                (round_pairs if copy is round_gpsimd else round_piece)(copy, e, g)

        def round_w2(copy, e0, e1, over=None):
            dst = staged("s%d" % e0, [P, (e1 - e0) * N * PACK], BF16, over)
            copy(dst[:].rearrange("p (e c i t) -> p e c t i", e=e1 - e0, i=RUN, t=PACK),
                 tiles["v%d" % e0][:].rearrange("p e t (c i) -> p e c t i", i=RUN))
            for e in range(e0, e1):
                w2_at[e] = ("s%d" % e0, (e - e0) * N)

        def quantize(key, codes_over=None, scales_over=None):
            width = tiles[key].shape[1] // PACK
            codes = staged("codes_" + key, [P, width], U32, codes_over)
            scales = staged("scales_" + key, [P, width], U8, scales_over)
            nc.vector.quantize_mx(out=codes[:].bitcast(FP8X4), scales=scales[:], in_=tiles[key][:])
            codes_of[key] = (codes, scales)

        def matmul(dst, left, l0, right, r0, width, start, stop):
            (l_codes, l_scales), (r_codes, r_scales) = codes_of[left], codes_of[right]
            nc.tensor.matmul_mx(out=dst, lhsT=l_codes[:, l0:l0 + P].bitcast(FP8X4), lhsT_scale=l_scales[:, l0:l0 + P],
                                rhs=r_codes[:, r0:r0 + width].bitcast(FP8X4), rhs_scale=r_scales[:, r0:r0 + width],
                                start=start, stop=stop)

        def open_h(e0, e1, over=None):
            staged("h%d" % e0, [P, (e1 - e0) * C * PACK], BF16, over)
            for e in range(e0, e1):
                h_at[e] = ("h%d" % e0, (e - e0) * C)

        def first_layer(e, banks_over):
            banks = [in_bank("a%d%d" % (e, b), [P, PACK, BANK], banks_over[b]) for b in range(C // BANK)]
            for g in range(PASSES):
                (w_key, c0), (x_key, x0) = piece_at[e, g], x_at[g, e]
                for b, bank in enumerate(banks):
                    for t in range(PACK):
                        matmul(bank[:, t, :], w_key, c0 + t * P, x_key, x0 + b * BANK, BANK,
                               g == 0 and t == 0, g == PASSES - 1 and t == PACK - 1)

        def hidden(relu, e, halves=(0, 1)):
            key, s0 = h_at[e]
            for b in halves:
                dst = tiles[key][:, (s0 + b * BANK) * PACK:(s0 + (b + 1) * BANK) * PACK]
                relu(dst.rearrange("p (s t) -> p s t", t=PACK), tiles["a%d%d" % (e, b)][:].rearrange("p t s -> p s t"))

        def second_layer(s0, s1, bank_over, copy):
            bank = in_bank("y%d" % s0, [P, s1 - s0], bank_over)
            for a in range(s0, s1, C):
                e, width = a // C, min(C, s1 - a)
                key, h0 = h_at[e]
                matmul(bank[:, a - s0:a - s0 + width], *w2_at[e], key, h0 + a % C, width, True, True)
            copy(tiles["y"][:, s0:s1], bank[:])


        wide = ((0, 0), (0, 1), (1, 0), (1, 1), (1, 2))
        for g in range(PASSES):
            for t in range(PACK):
                staged("p%d%d" % (g, t), [P, T + SPARE * ((g, t) in wide)], F32)
        for g, t in reversed(wide[1:]):
            nc.gpsimd.memset(tiles["p%d%d" % (g, t)][:, T:], 0.0)
        nc.scalar.activation(tiles["p00"][:, T:], tiles["p12"][:, T:], COPY)

        nc.sync.dma_start(offs_sb[:], offs)
        load_plane(0, 0)
        load_plane(0, 1)
        load_gate()
        load_w1(0, 0)
        load_plane(0, 2)
        load_plane(0, 3)
        load_w1(0, 1)
        load_w1(1, 0)
        load_plane(1, 0)
        load_w1(1, 1)
        load_plane(1, 1)
        load_plane(1, 2)
        load_plane(1, 3)
        for e, g in ((2, 0), (2, 1), (3, 0), (3, 1), (4, 0), (4, 1), (5, 0), (5, 1)):
            load_w1(e, g)
        place["free"] += 2 * 1024

        open_fetched(0, 0, 4)
        open_fetched(0, 4, 6)
        open_fetched(0, 6, 8)
        fetch(copy_vector, 0, (0,), 6, 8)
        fetch(copy_vector, 0, (0,), 4, 6)
        fetch(pick_scalar, 0, (0, 1), 0, 4)
        spread_gate((3, 2, 0, 1))
        fetch(copy_vector, 0, (1,), 6, 8)
        fetch(copy_vector, 0, (1,), 4, 6)
        round_w1(round_gpsimd, [(0, 0), (0, 1)])
        round_w1(round_gpsimd, [(1, 0), (1, 1)])
        fetch(copy_vector, 0, (2, 3), 6, 8)
        fetch(pick_scalar, 0, (2, 3), 4, 6)
        fetch(pick_scalar, 0, (2, 3), 0, 2)
        fetch(pick_scalar, 0, (2, 3), 2, 4)
        open_x([(0, 6, 8), (0, 4, 6)])
        times_gate(0, 6, 8)
        times_gate(0, 4, 6)
        open_x([(0, 0, 4)], over="f06")
        times_gate(0, 0, 2)
        times_gate(0, 2, 4)
        load_w1(6, 0, over="f04")
        load_w1(6, 1, over="f00")
        load_w1(7, 0, over=("f00", 8))
        load_w1(7, 1, over="p00")
        load_w2(0, 2, over="p02")
        load_w2(2, 4, over="p03")
        load_w2(4, 6)
        load_w2(6, 8)
        nc.sync.dma_start(pos1_sb[:], pos1)
        nc.sync.dma_start(pos2_sb[:], pos2)
        quantize("r00", "w11", ("w11", 4))
        quantize("x06", "w00", ("w11", 5))
        quantize("r10", ("w00", 4), "w10")
        quantize("x00", "w01", ("w11", 6))

        open_fetched(1, 0, 4)
        fetch(pick_scalar, 1, (0, 1, 2), 0, 4)
        fetch(pick_scalar, 1, (3,), 0, 2)
        fetch(pick_scalar, 1, (3,), 2, 4)
        round_w1(round_gpsimd, [(2, 0), (2, 1)], over="x00")
        open_fetched(1, 4, 6, over="r10")
        open_x([(1, 0, 4)], over="x06")
        fetch(copy_vector, 1, (0,), 4, 6)
        times_gate(1, 0, 2)
        times_gate(1, 2, 4)
        fetch(pick_scalar, 1, (1, 2, 3), 4, 6)
        round_w1(copy_scalar, [(3, 0), (3, 1)], over="r00")
        quantize("x10", "w21", ("w21", 4))
        quantize("r20", "w20", ("w20", 4))

        round_w1(round_gpsimd, [(4, 0), (4, 1)], over="r20")
        open_x([(1, 4, 6)], over="x10")
        open_fetched(1, 6, 7, over=("x10", 4))
        first_layer(0, ("turned", None))
        first_layer(1, (None, None))
        first_layer(2, ("gate0", "gate1"))
        open_h(0, 2, over="w31")
        open_h(2, 3, over=("w31", 4))
        times_gate(1, 4, 6)
        fetch(copy_vector, 1, range(PACK), 6, 7)
        hidden(relu_scalar, 0)
        hidden(relu_scalar, 1)
        hidden(relu_scalar, 2, (0,))
        hidden(relu_vector, 2, (1,))
        round_w1(copy_scalar, [(5, 0)], over="f14")
        round_w1(copy_scalar, [(5, 1)], over=("f14", 4))
        quantize("r30", "w41", ("w41", 4))
        quantize("x14", ("w41", 5), ("w41", 7))
        quantize("r40", "w40", ("w40", 4))

        quantize("r50", "w50", ("r30", 7))
        quantize("h0", ("w50", 2), ("r30", 6))
        quantize("h2", ("w50", 4), ("r30", 5))
        quantize("r51", None, ("r30", 4))

        open_pieces([(6, 0), (6, 1)], over="r51")
        round_pairs(round_gpsimd, 6, 0)
        round_pairs(round_gpsimd, 6, 1, 0, 2)
        open_fetched(1, 7, 8, over=("w51", 2))
        open_x([(1, 6, 8)], over=("w51", 6))
        first_layer(3, ("a00", "a01"))
        first_layer(4, ("a10", "a11"))
        first_layer(5, ("a20", "a21"))
        open_h(3, 5, over=("w51", -2))
        open_h(5, 6, over="r50")
        fetch(copy_vector, 1, (0, 1), 7, 8)
        times_gate(1, 6, 7)
        fetch(copy_vector, 1, (2, 3), 7, 8)
        times_gate(1, 7, 8)
        for e in range(3, 6):
            hidden(relu_scalar, e)
        round_pairs(copy_scalar, 6, 1, 2, 4)
        round_w1(copy_scalar, [(7, 0)], over="f16")
        round_w1(copy_scalar, [(7, 1)], over="f17")
        quantize("x16", "w61", ("w61", 2))
        quantize("r60", "w60", ("w60", 4))
        quantize("r70", ("w61", 3), ("w61", 5))
        quantize("h3", ("w60", 5), ("w61", 6))
        quantize("h5", None, ("w61", 7))

        first_layer(6, ("gate2", "gate3"))
        quantize("r71", "r60", ("r60", 2))
        first_layer(7, ("a30", "a31"))
        round_w2(copy_scalar, 0, 2, over="w71")
        open_h(6, 7, over="v0")
        open_h(7, 8, over=("v0", 2))
        hidden(relu_scalar, 6)
        hidden(relu_scalar, 7)
        round_w2(copy_vector, 2, 4, over="r70")
        quantize("s0")
        round_w2(copy_vector, 4, 6, over="r71")
        quantize("s2", None, "s0")
        round_w2(copy_vector, 6, 8)
        quantize("h6", "v4", ("v4", 1))
        quantize("s4", ("v4", 2), ("v4", 3))
        staged("y", [P, SLOTS], F32, over="w30")
        second_layer(0, 2 * C, "a40", copy_scalar)
        second_layer(2 * C, 4 * C, "a41", copy_scalar)
        quantize("h7", "v6", ("v6", 1))
        quantize("s6")
        second_layer(4 * C, 6 * C, "a50", copy_scalar)
        second_layer(6 * C, 7 * C, "a51", copy_vector)
        second_layer(7 * C, 8 * C, "a60", copy_scalar)

        y_sb = tiles["y"]
        both = staged("both", [P, T], F32, over="p10")
        first = staged("first", [P, T], F32, over="p11")
        for n, (t0, t1) in enumerate(TOKEN_RANGES):
            pick = copy_vector if n == VECTOR_RANGE else pick_scalar
            pick(first[:, t0:t1], y_sb[:].indirect(pos1_sb[:, t0 // ENTRIES:t1 // ENTRIES]))
        stored = 0
        for n, (t0, t1) in enumerate(TOKEN_RANGES):
            nc.vector.tensor_tensor(both[:, t0:t1], y_sb[:].indirect(pos2_sb[:, t0 // ENTRIES:t1 // ENTRIES]),
                                    first[:, t0:t1], ADD)
            if n >= FIRST_STORE:
                nc.sync.dma_start(out[:, stored:t1], both[:, stored:t1])
                stored = t1
